import numpy as np
import ml_dtypes


def mxq(x, axis, fmt="e4m3"):
    dtype, down = {"e4m3": (ml_dtypes.float8_e4m3fn, 7), "e5m2": (ml_dtypes.float8_e5m2, 14)}[fmt]
    v = np.moveaxis(np.asarray(x, np.float32).astype(ml_dtypes.bfloat16).astype(np.float64), axis, -1)
    blocks = v.reshape(v.shape[:-1] + (-1, 32))
    amax = np.abs(blocks).max(-1, keepdims=True)
    byte = np.maximum(np.where(amax > 0, np.frexp(amax)[1] - 1 + 127, 0) - down, 1)
    scale = np.exp2(byte - 127.0)
    codes = (blocks / scale).astype(np.float32).astype(dtype).astype(np.float64)
    return np.moveaxis((codes * scale).reshape(v.shape), -1, axis)


WIDE = False


def mx_kscale(k):
    if not WIDE:
        return np.ones(k)
    levels = np.array([10, -10, 5, -5, 0])
    if k % 512:
        return np.exp2(np.random.permutation(np.resize(levels, k // 32))).repeat(32)
    a = np.empty((k // 512, 16))
    for p in range(k // 512):
        a[p, :8] = np.random.permutation(np.resize(levels, 8))
        for g in range(8):
            far = levels[np.abs(levels - a[p, g]) >= 10]
            a[p, g + 8] = far[np.random.randint(len(far))]
    return np.exp2(a.ravel()).repeat(32)


def f64(x):
    return np.asarray(x).astype(np.float64)


def striped(idx):
    return np.tile(idx.reshape(-1, 16).T, (8, 1)).astype(np.uint16)


def unstriped(offs):
    return offs[:16].T.reshape(-1).astype(np.int64)


E2M1 = np.array([0.0, 0.5, 1.0, 1.5, 2.0, 3.0, 4.0, 6.0, -0.0, -0.5, -1.0, -1.5, -2.0, -3.0, -4.0, -6.0])


def pack_weight(w, fmt):
    k, n = w.shape
    w = f64(np.asarray(w, np.float32).astype(ml_dtypes.bfloat16)).reshape(k // 32, 32, n)
    amax = np.abs(w).max(1)
    if fmt == "e4m3":
        byte = np.frexp(amax)[1] - 1 + 127 - 7
    else:
        mant, ex = np.frexp(amax / 6.0)
        byte = np.where(mant > 0.5, ex, ex - 1) + 127
    byte = np.clip(np.where(amax > 0, byte, 1), 1, 254)
    scaled = (w * np.exp2(127.0 - byte)[:, None, :]).reshape(k, n).astype(np.float32)
    by_word = np.ascontiguousarray(scaled.reshape(k // 512, 128, 4, n).transpose(0, 1, 3, 2))
    if fmt == "e4m3":
        words = by_word.astype(ml_dtypes.float8_e4m3fn).view(np.uint8)
    else:
        c = by_word.astype(ml_dtypes.float4_e2m1fn).view(np.uint8) & 0xF
        words = (c[..., 0::2] | (c[..., 1::2] << 4)).reshape(k // 512, 128, 2 * n)
    return np.ascontiguousarray(words), np.ascontiguousarray(byte.astype(np.uint8).reshape(k // 512, 16, n))


def unpack_weight(words, scales, fmt):
    g, _, n = scales.shape
    words = np.ascontiguousarray(words).reshape(g, 128, n, -1)
    if fmt == "e4m3":
        vals = words.view(ml_dtypes.float8_e4m3fn).astype(np.float64)
    else:
        nib = np.empty((g, 128, n, 4), np.uint8)
        nib[..., 0::2] = words & 0xF
        nib[..., 1::2] = words >> 4
        vals = E2M1[nib]
    vals = vals * np.repeat(np.exp2(scales.astype(np.float64) - 127.0), 8, axis=1)[..., None]
    return vals.transpose(0, 1, 3, 2).reshape(g * 512, n)


def gelu(v):
    return 0.5 * v * (1.0 + np.tanh(np.sqrt(2.0 / np.pi) * (v + 0.044715 * v**3)))


K, H, N, T, TC, S, T2 = 1024, 1024, 512, 2048, 1024, 512, 1024

def setup_inputs():
    n = np.random.standard_normal
    s = mx_kscale(K)[:, None]
    u = mx_kscale(H)
    u2 = u * u
    tab_words, tab_scales = pack_weight(n((K, T)) * s, "e4m3")
    tab2_words, tab2_scales = pack_weight(n((K, TC)) * s, "e4m3")
    w2_words, w2_scales = pack_weight(n((K, H)) / np.sqrt(K) / s, "e2m1")
    w3_words, w3_scales = pack_weight(n((H, N)) / np.sqrt(H) / u2[:, None], "e4m3")
    perm = np.random.permutation(T2)
    return {
        "tab_words": tab_words, "tab_scales": tab_scales,
        "tab2_words": tab2_words, "tab2_scales": tab2_scales,
        "offs": striped(np.random.permutation(T)[:S]),
        "offs2": striped(np.random.permutation(TC)[:S]),
        "offs3": striped(perm[:S]), "offs4": striped(perm[S:]),
        "w1": (n((K, H)) / np.sqrt(K) / s * u[None, :]).astype(np.float32),
        "w2_words": w2_words, "w2_scales": w2_scales,
        "w3_words": w3_words, "w3_scales": w3_scales,
        "c1": (n(H) * u).astype(np.float32),
        "amp": (1.5 * np.exp(0.3 * n(H)) * u2).astype(np.float32),
        "c0": (0.7 * n(H) * u2).astype(np.float32),
        "wg1": np.exp(0.3 * n((128, S))).astype(np.float32),
        "wg2": np.exp(0.3 * n((128, S))).astype(np.float32),
    }

def reference(tab_words, tab_scales, tab2_words, tab2_scales, offs, offs2, offs3, offs4, w1, w2_words, w2_scales, w3_words, w3_scales, c1, amp, c0, wg1, wg2):
    v = unpack_weight(tab_words, tab_scales, "e4m3")[:, unstriped(offs)]
    v2 = unpack_weight(tab2_words, tab2_scales, "e4m3")[:, unstriped(offs2)]
    a = mxq(f64(w1), 0, "e4m3").T @ v
    b = unpack_weight(w2_words, w2_scales, "e2m1").T @ v2
    h1 = a * (a + f64(c1)[:, None])
    h2 = f64(amp)[:, None] / (1.0 + np.square(b))
    page = np.zeros((H, T2))
    page[:, unstriped(offs3)] = np.tile(f64(wg1), (H // 128, 1)) * h1
    page[:, unstriped(offs4)] = np.tile(f64(wg2), (H // 128, 1)) * h2
    z = page + f64(c0)[:, None]
    return unpack_weight(w3_words, w3_scales, "e4m3").T @ mxq(z, 0, "e4m3")

@@ -1,0 +1,354 @@
+from contextlib import ExitStack
+
+import concourse.mybir as mybir
+
+K, H, N, T, TC, S, T2 = 1024, 1024, 512, 2048, 1024, 512, 1024
+FLOPS = 2 * K * H * S * 2 + 2 * H * N * T2
+
+F32 = mybir.dt.float32
+BF16 = mybir.dt.bfloat16
+I32 = mybir.dt.int32
+U32 = mybir.dt.uint32
+U16 = mybir.dt.uint16
+U8 = mybir.dt.uint8
+E4M3 = mybir.dt.float8_e4m3fn_x4
+E2M1 = mybir.dt.float4_e2m1fn_x4
+ACT = mybir.ActivationFunctionType
+MULT = mybir.AluOpType.mult
+ADD = mybir.AluOpType.add
+
+P = 128
+PACK = 4
+KP = P * PACK
+PASSES = 2
+QUADS = 4
+PLANES = PASSES * PACK
+QW = 256
+NQ = T2 // QW
+
+
+def tile_list_creep_life_weave_kernel(
+    tc, tab_words, tab_scales, tab2_words, tab2_scales, offs, offs2, offs3, offs4,
+    w1, w2_words, w2_scales, w3_words, w3_scales, c1, amp, c0, wg1, wg2, out,
+):
+    nc = tc.nc
+    with ExitStack() as ctx:
+        lists = ctx.enter_context(tc.tile_pool(name="lists", bufs=1))
+        keep = ctx.enter_context(tc.tile_pool(name="keep", bufs=1))
+        psum = ctx.enter_context(tc.psum_pool(name="psum", bufs=1))
+
+        def held(name, shape, dtype, tag=None):
+            return keep.tile(shape, dtype, name=name, tag=tag or name, align_bytes=64)
+
+        def load_list(name, src):
+            tile = lists.tile([P, S // 16], U16, name=name)
+            nc.sync.dma_start(tile[:], src)
+            return tile
+
+        def load_words(name, src, tag):
+            tile = held(name, [P, src.shape[1]], U32, tag=tag)
+            nc.sync.dma_start(tile[:].bitcast(I32), src.rearrange("p t i -> p (t i)").bitcast(I32))
+            return tile
+
+        def load_scales_side_by_side(queue, tile, src):
+            rows = tile[:].bitcast(I32).rearrange("p (g n) -> p g n", g=PASSES)
+            for q in range(QUADS):
+                queue.dma_start(
+                    rows[32 * q : 32 * q + 4],
+                    src[:, 4 * q : 4 * q + 4, :].bitcast(I32).rearrange("g r n -> r g n"),
+                )
+
+        def load_scales_stacked(queue, tile, src):
+            for q in range(QUADS):
+                queue.dma_start(
+                    tile[32 * q : 32 * q + 4 * PASSES, :].bitcast(I32),
+                    src[:, 4 * q : 4 * q + 4, :].bitcast(I32),
+                )
+
+        def load_vector(name, src):
+            tile = held(name, [P, PASSES, PACK], F32)
+            nc.gpsimd.dma_start(tile[:], src.rearrange("(a p t) -> p a t", a=PASSES, t=PACK))
+            return tile
+
+        def load_confidence(name, src, tag, queues):
+            tile = held(name, [P, PACK * S], F32, tag=tag)
+            rows = src.rearrange("(u t) j -> u (t j)", t=PACK)
+            for q in range(QUADS):
+                queues[q // 2].dma_start(tile[32 * q : 32 * (q + 1), :], rows)
+            return tile
+
+        def load_w1(g, a, tag):
+            tile = held("w1raw%d%d" % (g, a), [P, PACK, KP], F32, tag=tag)
+            nc.sync.dma_start(
+                tile[:],
+                w1[g * KP : (g + 1) * KP, a * KP : (a + 1) * KP].rearrange("(p j) c -> p j c", j=PACK),
+            )
+            return tile
+
+        tab2_sc = held("tab2_sc", [P, PASSES * TC], U8)
+        w2_sc_raw = held("w2_sc_raw", [P, PASSES * H], U8)
+        nc.gpsimd.memset(tab2_sc[:].bitcast(I32), 0)
+        nc.vector.memset(w2_sc_raw[:].bitcast(I32), 0)
+        warm_in = held("warm_in", [P, 1], F32)
+        warm_out = held("warm_out", [P, 1], F32)
+        nc.gpsimd.memset(warm_in[:], 1.0)
+        nc.scalar.activation(warm_out[:], warm_in[:], ACT.Abs_reciprocal_sqrt, bias=1.0)
+
+        def load_w2(a):
+            tile = held("w2_raw%d" % a, [P, PASSES, 2 * KP], U8, tag="T%d" % a)
+            nc.sync.dma_start(
+                tile[:].bitcast(I32),
+                w2_words[:, :, 2 * a * KP : 2 * (a + 1) * KP].bitcast(I32).rearrange("g p n -> p g n"),
+            )
+            return tile
+
+        w2_raw = [load_w2(0)]
+        idx2 = load_list("idx2", offs2)
+        idx1 = load_list("idx1", offs)
+        idx4 = load_list("idx4", offs4)
+        idx3 = load_list("idx3", offs3)
+        tab2_w = [load_words("tab2_w%d" % g, tab2_words[g], "T%d" % (2 + g)) for g in range(PASSES)]
+        w2_raw.append(load_w2(1))
+        load_scales_side_by_side(nc.sync, tab2_sc, tab2_scales)
+        amp_t = load_vector("amp_t", amp)
+        load_scales_side_by_side(nc.sync, w2_sc_raw, w2_scales)
+        c1_t = load_vector("c1_t", c1)
+        tab_sc = held("tab_sc", [P, T], U8)
+        nc.gpsimd.memset(tab_sc[:].bitcast(I32), 0)
+        c0_t = load_vector("c0_t", c0)
+
+        w2_w = [held("w2_w%d" % a, [P, PASSES * 2 * KP], U8) for a in range(PASSES)]
+        w2_sc = [held("w2_sc%d" % a, [P, PASSES * KP], U8) for a in range(PASSES)]
+
+        def reorder_w2_words(a):
+            nc.vector.tensor_copy(
+                w2_w[a][:].bitcast(U16).rearrange("p (g t m) -> p g m t", g=PASSES, t=PACK),
+                w2_raw[a][:].bitcast(U16).rearrange("p g (m t) -> p g m t", t=PACK),
+            )
+
+        def reorder_w2_scales(a):
+            src = w2_sc_raw[:].rearrange("p (g n) -> p g n", g=PASSES)[:, :, a * KP : (a + 1) * KP]
+            nc.vector.tensor_copy(
+                w2_sc[a][:].rearrange("p (g t m) -> p g m t", g=PASSES, t=PACK),
+                src.rearrange("p g (m t) -> p g m t", t=PACK),
+            )
+
+        def gather(name, window, idx, dtype):
+            tile = held(name, [P, S], dtype)
+            nc.vector.tensor_copy(tile[:], window.indirect(idx[:]))
+            return tile
+
+        reorder_w2_words(0)
+        tab_w = [load_words("tab_w0", tab_words[0], "T0")]
+        reorder_w2_words(1)
+        wg2_t = load_confidence("wg2_t", wg2, "T1", (nc.sync, nc.scalar))
+        v2_w = [gather("v2_w0", tab2_w[0][:], idx2, U32)]
+        tab_w.append(load_words("tab_w1", tab_words[1], "T2"))
+        load_scales_stacked(nc.sync, tab_sc, tab_scales)
+        v2_w.append(gather("v2_w1", tab2_w[1][:], idx2, U32))
+        v2_sc = [gather("v2_sc%d" % g, tab2_sc[:, g * TC : (g + 1) * TC], idx2, U8) for g in range(PASSES)]
+        for a in range(PASSES):
+            reorder_w2_scales(a)
+        v_w = [gather("v_w%d" % g, tab_w[g][:], idx1, U32) for g in range(PASSES)]
+        v_sc = gather("v_sc", tab_sc[:], idx1, U8)
+        w1_raw = {}
+        w1_raw[0, 0] = load_w1(0, 0, "T0")
+
+        def bank(i, name):
+            return psum.tile([P, S], F32, name=name, tag="bank%d" % i)
+
+        def column(vec, i):
+            return vec[:, i // PACK, i % PACK : i % PACK + 1]
+
+        def slot(tile, i):
+            return tile[:, (i % PACK) * S : (i % PACK + 1) * S]
+
+        SQUARE_TAGS = ["sq", "sq", "sq", "T0", "T4", "recip", "recip", "recip"]
+        RECIP_TAGS = ["recip", "recip", "grouped00", "grouped10", "recip", "grouped01", "sq", "sq"]
+        COOL_TAGS = ["T4", "T6", "T8", "T7", "w3_w", "w3_sc", "cool6", "cool7"]
+        PAGE_TAGS = ["T3", "T2", "tab_sc", "grouped00", "grouped10", "page5", "grouped11", "T0"]
+        HOT_TAGS = ["hot0", "hot1", "T8", "T7", "hot4", "hot5", "hot6", "hot7"]
+        cool, hot, hot_w, pages = {}, {}, {}, {}
+
+        def cool_stream(i):
+            a, t = divmod(i, PACK)
+            acc = bank(i, "b%d" % i)
+            for g in range(PASSES):
+                c = g * KP + t * P
+                nc.tensor.matmul_mx(
+                    out=acc[:],
+                    lhsT=w2_w[a][:, 2 * c : 2 * (c + P)].bitcast(E2M1),
+                    lhsT_scale=w2_sc[a][:, c : c + P],
+                    rhs=v2_w[g][:].bitcast(E4M3),
+                    rhs_scale=v2_sc[g][:],
+                    start=(g == 0),
+                    stop=(g == PASSES - 1),
+                )
+            square = held("square%d" % i, [P, S], F32, tag=SQUARE_TAGS[i])
+            nc.scalar.activation(square[:], acc[:], ACT.Square)
+            root = held("root%d" % i, [P, S], F32, tag="root")
+            nc.scalar.activation(root[:], square[:], ACT.Abs_reciprocal_sqrt, bias=1.0)
+            recip = held("recip%d" % i, [P, S], F32, tag=RECIP_TAGS[i])
+            nc.scalar.activation(recip[:], root[:], ACT.Square)
+            cool[i] = held("cool%d" % i, [P, S], F32, tag=COOL_TAGS[i])
+            nc.scalar.activation(cool[i][:], recip[:], ACT.Copy, scale=column(amp_t, i))
+
+        w1_w, w1_sc = {}, {}
+
+        def quantise_w1(g, a):
+            if True:
+                grouped = held("grouped%d%d" % (g, a), [P, PACK * KP], BF16)
+                nc.scalar.copy(
+                    grouped[:].rearrange("p (t m j) -> p m t j", t=PACK, j=PACK),
+                    w1_raw[g, a][:].rearrange("p j (m t) -> p m t j", t=PACK),
+                )
+                w1_w[g, a] = held("w1_w%d%d" % (g, a), [P, KP], U32)
+                w1_sc[g, a] = held("w1_sc%d%d" % (g, a), [P, KP], U8)
+                nc.vector.quantize_mx(out=w1_w[g, a][:].bitcast(E4M3), scales=w1_sc[g, a][:], in_=grouped[:])
+
+        hot_acc = {}
+        feature = [held("feature%d" % a, [P, PACK * S], F32) for a in range(PASSES)]
+
+        def hot_features(a):
+            for t in range(PACK):
+                i = PACK * a + t
+                hot_acc[i] = bank(i, "a%d" % i)
+                for g in range(PASSES):
+                    nc.tensor.matmul_mx(
+                        out=hot_acc[i][:],
+                        lhsT=w1_w[g, a][:, t * P : (t + 1) * P].bitcast(E4M3),
+                        lhsT_scale=w1_sc[g, a][:, t * P : (t + 1) * P],
+                        rhs=v_w[g][:].bitcast(E4M3),
+                        rhs_scale=v_sc[4 * g : P, :],
+                        start=(g == 0),
+                        stop=(g == PASSES - 1),
+                    )
+                nc.scalar.copy(slot(feature[a], i), hot_acc[i][:])
+            hot_w[a] = feature[a]
+            nc.vector.tensor_tensor(hot_w[a][:], feature[a][:], wg1_t[:], MULT)
+
+        def hot_shifted(i):
+            hot[i] = held("hot%d" % i, [P, S], F32, tag=HOT_TAGS[i])
+            nc.scalar.activation(hot[i][:], hot_acc[i][:], ACT.Identity, bias=column(c1_t, i))
+
+        def scatter_cool(i):
+            pages[i] = held("page%d" % i, [P, T2], F32, tag=PAGE_TAGS[i])
+            nc.vector.tensor_tensor(pages[i][:].indirect(idx4[:]), cool[i][:], slot(wg2_t, i), MULT)
+
+        def scatter_hot(i):
+            nc.vector.tensor_tensor(pages[i][:].indirect(idx3[:]), hot[i][:], slot(hot_w[i // PACK], i), MULT)
+
+        def round_plane(pairs, i, c, width):
+            u, e = divmod(i % PACK, 2)
+            chunk = pairs[:, PACK * c : PACK * (c + width)].rearrange("p (u c e) -> p u c e", u=2, e=2)
+            nc.scalar.activation(chunk[:, u, :, e], pages[i][:, c : c + width], ACT.Identity, bias=column(c0_t, i))
+
+        z_w = {}
+        z_sc = [held("z_sc%d" % a, [P, T2], U8) for a in range(PASSES)]
+
+        def weave_views(z, pairs, c, width, dtype):
+            cols = slice(PACK * c, PACK * (c + width))
+            return (
+                z[:, cols].bitcast(dtype).rearrange("p (c u) -> p c u", u=2),
+                pairs[:, cols].bitcast(dtype).rearrange("p (u c) -> p c u", u=2),
+            )
+
+        def quantise_z(a, z, c, width):
+            nc.vector.quantize_mx(
+                out=z_w[a][:, c : c + width].bitcast(E4M3),
+                scales=z_sc[a][:, c : c + width],
+                in_=z[:, PACK * c : PACK * (c + width)],
+            )
+
+        def score_pass(a, acc, q, half):
+            for m in range(2):
+                n0 = (2 * half + m) * P
+                nc.tensor.matmul_mx(
+                    out=acc[:, m * QW : (m + 1) * QW],
+                    lhsT=w3_w[:, a, n0 : n0 + P].bitcast(E4M3),
+                    lhsT_scale=w3_sc[4 * a : P, n0 : n0 + P],
+                    rhs=z_w[a][:, q * QW : (q + 1) * QW].bitcast(E4M3),
+                    rhs_scale=z_sc[a][:, q * QW : (q + 1) * QW],
+                    start=(a == 0 and m == 0),
+                    stop=(a == PASSES - 1 and m == 1),
+                )
+
+        last = PLANES - 1
+
+        def cool_plane(i):
+            cool_stream(i)
+            scatter_cool(i)
+
+        def hot_plane(i):
+            hot_shifted(i)
+            scatter_hot(i)
+
+        cool_plane(0)
+        w1_raw[1, 0] = load_w1(1, 0, "T4")
+        cool_plane(1)
+        wg1_t = load_confidence("wg1_t", wg1, "T6", (nc.sync, nc.sync))
+        cool_plane(2)
+        w1_raw[0, 1] = load_w1(0, 1, "T8")
+        quantise_w1(0, 0)
+        cool_plane(3)
+        w1_raw[1, 1] = load_w1(1, 1, "T7")
+        quantise_w1(1, 0)
+        cool_plane(4)
+        w3_w = held("w3_w", [P, PASSES, N], U32)
+        nc.sync.dma_start(w3_w[:].bitcast(I32), w3_words.rearrange("g p c i -> p g (c i)").bitcast(I32))
+        cool_plane(5)
+        w3_sc = held("w3_sc", [P, N], U8)
+        nc.gpsimd.memset(w3_sc[:].bitcast(I32), 0)
+        load_scales_stacked(nc.sync, w3_sc, w3_scales)
+        hot_features(0)
+        hot_plane(0)
+        hot_plane(1)
+        quantise_w1(0, 1)
+        hot_plane(2)
+        quantise_w1(1, 1)
+        hot_plane(3)
+        cool_plane(6)
+        cool_stream(7)
+        pairs = held("pairs0", [P, PACK * T2], BF16, tag="grouped01")
+        round_plane(pairs, 0, 0, T2)
+        round_plane(pairs, 1, 0, T2)
+        hot_features(1)
+        hot_plane(4)
+        round_plane(pairs, 2, 0, T2)
+        hot_plane(5)
+        round_plane(pairs, 3, 0, T2)
+        hot_plane(6)
+        hot_shifted(7)
+        z = held("z0", [P, PACK * T2], BF16, tag="T0")
+        nc.scalar.copy(*weave_views(z, pairs, 0, T2, U32))
+        z_w[0] = held("z_w0", [P, T2], U32, tag="hot6")
+        z_w[1] = held("z_w1", [P, T2], U32)
+        quantise_z(0, z, 0, T2)
+        scores = [bank(b, "score%d" % b) for b in range(2 * NQ)]
+        for b in range(2 * NQ):
+            score_pass(0, scores[b], b // 2, b % 2)
+
+        scatter_cool(last)
+        scatter_hot(last)
+        pairs = held("pairs1", [P, PACK * T2], BF16, tag="T4")
+        for i in range(PACK, PLANES):
+            for q in range(NQ):
+                round_plane(pairs, i, q * QW, QW)
+        z = held("z1", [P, PACK * T2], BF16, tag="feature0")
+        staged = [held("staged%d" % s, [P, NQ * S], F32, tag=("T8", "T7")[s]) for s in range(2)]
+        for q in range(NQ):
+            nc.vector.tensor_copy(*weave_views(z, pairs, q * QW, QW, I32))
+            quantise_z(1, z, q * QW, QW)
+            for half in range(2):
+                score_pass(1, scores[2 * q + half], q, half)
+        for b in range(2 * NQ):
+            q, half = divmod(b, 2)
+            result = staged[b // NQ][:, (b % NQ) * S : (b % NQ + 1) * S]
+            if b in (3, 5, 7):
+                nc.vector.tensor_copy(result, scores[b][:])
+            else:
+                nc.scalar.copy(result, scores[b][:])
+            nc.sync.dma_start(
+                out[2 * half * P : 2 * (half + 1) * P, q * QW : (q + 1) * QW].rearrange("(m p) c -> p m c", p=P),
+                result.rearrange("p (m c) -> p m c", m=2),
+            )

@@ -3,7 +3,7 @@ from contextlib import ExitStack
 import concourse.mybir as mybir
 
 K, H, N, T, TC, S, T2 = 1024, 1024, 512, 2048, 1024, 512, 1024
-FLOPS = 2 * K * H * S * 2 + 2 * H * N * T2
+FLOPS = 2 * (2 * K * H * S + H * N * T2)
 
 F32 = mybir.dt.float32
 BF16 = mybir.dt.bfloat16
@@ -15,16 +15,20 @@ E4M3 = mybir.dt.float8_e4m3fn_x4
 E2M1 = mybir.dt.float4_e2m1fn_x4
 ACT = mybir.ActivationFunctionType
 MULT = mybir.AluOpType.mult
-ADD = mybir.AluOpType.add
 
 P = 128
 PACK = 4
 KP = P * PACK
 PASSES = 2
-QUADS = 4
+QUAD = 32
+QUADS = P // QUAD
+SCALE_ROWS = 4
 PLANES = PASSES * PACK
-QW = 256
-NQ = T2 // QW
+LAST = PLANES - 1
+HALF = T2 // 2
+CHUNK = 256
+CHUNKS = T2 // CHUNK
+BANKS = 2 * CHUNKS
 
 
 def tile_list_creep_life_weave_kernel(
@@ -34,91 +38,91 @@ def tile_list_creep_life_weave_kernel(
     nc = tc.nc
     with ExitStack() as ctx:
         lists = ctx.enter_context(tc.tile_pool(name="lists", bufs=1))
-        keep = ctx.enter_context(tc.tile_pool(name="keep", bufs=1))
+        sbuf = ctx.enter_context(tc.tile_pool(name="sbuf", bufs=1))
         psum = ctx.enter_context(tc.psum_pool(name="psum", bufs=1))
 
-        def held(name, shape, dtype, tag=None):
-            return keep.tile(shape, dtype, name=name, tag=tag or name, align_bytes=64)
+        def tile(name, shape, dtype, after=None):
+            return sbuf.tile(shape, dtype, name=name, tag=after or name, align_bytes=64)
+
+        def bank(b, name):
+            return psum.tile([P, S], F32, name=name, tag="bank%d" % b)
 
         def load_list(name, src):
-            tile = lists.tile([P, S // 16], U16, name=name)
-            nc.sync.dma_start(tile[:], src)
-            return tile
+            dst = lists.tile([P, S // 16], U16, name=name)
+            nc.sync.dma_start(dst[:], src)
+            return dst
 
-        def load_words(name, src, tag):
-            tile = held(name, [P, src.shape[1]], U32, tag=tag)
-            nc.sync.dma_start(tile[:].bitcast(I32), src.rearrange("p t i -> p (t i)").bitcast(I32))
-            return tile
+        def load_table(name, src, after=None):
+            dst = tile(name, [P, src.shape[1]], U32, after)
+            nc.sync.dma_start(dst[:].bitcast(I32), src.rearrange("p c i -> p (c i)").bitcast(I32))
+            return dst
 
-        def load_scales_side_by_side(queue, tile, src):
-            rows = tile[:].bitcast(I32).rearrange("p (g n) -> p g n", g=PASSES)
+        def load_scales_side_by_side(dst, src):
+            rows = dst[:].bitcast(I32).rearrange("p (g c) -> p g c", g=PASSES)
             for q in range(QUADS):
-                queue.dma_start(
-                    rows[32 * q : 32 * q + 4],
-                    src[:, 4 * q : 4 * q + 4, :].bitcast(I32).rearrange("g r n -> r g n"),
+                nc.sync.dma_start(
+                    rows[QUAD * q : QUAD * q + SCALE_ROWS],
+                    src[:, SCALE_ROWS * q : SCALE_ROWS * (q + 1), :].bitcast(I32).rearrange("g r c -> r g c"),
                 )
 
-        def load_scales_stacked(queue, tile, src):
+        def load_scales_stacked(dst, src):
             for q in range(QUADS):
-                queue.dma_start(
-                    tile[32 * q : 32 * q + 4 * PASSES, :].bitcast(I32),
-                    src[:, 4 * q : 4 * q + 4, :].bitcast(I32),
+                nc.sync.dma_start(
+                    dst[QUAD * q : QUAD * q + PASSES * SCALE_ROWS, :].bitcast(I32),
+                    src[:, SCALE_ROWS * q : SCALE_ROWS * (q + 1), :].bitcast(I32),
                 )
 
-        def load_vector(name, src):
-            tile = held(name, [P, PASSES, PACK], F32)
-            nc.gpsimd.dma_start(tile[:], src.rearrange("(a p t) -> p a t", a=PASSES, t=PACK))
-            return tile
+        def load_coefficients(name, src):
+            dst = tile(name, [P, PASSES, PACK], F32)
+            nc.gpsimd.dma_start(dst[:], src.rearrange("(a p t) -> p a t", a=PASSES, t=PACK))
+            return dst
 
-        def load_confidence(name, src, tag, queues):
-            tile = held(name, [P, PACK * S], F32, tag=tag)
-            rows = src.rearrange("(u t) j -> u (t j)", t=PACK)
+        def load_confidence(name, src, first, count, after, upper_queue):
+            dst = tile(name, [P, count * S], F32, after)
+            rows = src.rearrange("(u t) j -> u (t j)", t=PACK)[:, first * S : (first + count) * S]
             for q in range(QUADS):
-                queues[q // 2].dma_start(tile[32 * q : 32 * (q + 1), :], rows)
-            return tile
+                queue = nc.sync if q < QUADS // 2 else upper_queue
+                queue.dma_start(dst[QUAD * q : QUAD * (q + 1), :], rows)
+            return dst
 
-        def load_w1(g, a, tag):
-            tile = held("w1raw%d%d" % (g, a), [P, PACK, KP], F32, tag=tag)
-            nc.sync.dma_start(
-                tile[:],
-                w1[g * KP : (g + 1) * KP, a * KP : (a + 1) * KP].rearrange("(p j) c -> p j c", j=PACK),
-            )
-            return tile
-
-        tab2_sc = held("tab2_sc", [P, PASSES * TC], U8)
-        w2_sc_raw = held("w2_sc_raw", [P, PASSES * H], U8)
-        nc.gpsimd.memset(tab2_sc[:].bitcast(I32), 0)
-        nc.vector.memset(w2_sc_raw[:].bitcast(I32), 0)
-        warm_in = held("warm_in", [P, 1], F32)
-        warm_out = held("warm_out", [P, 1], F32)
-        nc.gpsimd.memset(warm_in[:], 1.0)
-        nc.scalar.activation(warm_out[:], warm_in[:], ACT.Abs_reciprocal_sqrt, bias=1.0)
+        def load_w1(g, a, after):
+            dst = tile("w1_raw%d%d" % (g, a), [P, PACK, KP], F32, after)
+            src = w1[g * KP : (g + 1) * KP, a * KP : (a + 1) * KP]
+            nc.sync.dma_start(dst[:], src.rearrange("(p j) c -> p j c", j=PACK))
+            return dst
 
         def load_w2(a):
-            tile = held("w2_raw%d" % a, [P, PASSES, 2 * KP], U8, tag="T%d" % a)
-            nc.sync.dma_start(
-                tile[:].bitcast(I32),
-                w2_words[:, :, 2 * a * KP : 2 * (a + 1) * KP].bitcast(I32).rearrange("g p n -> p g n"),
-            )
-            return tile
+            dst = tile("w2_raw%d" % a, [P, PASSES, 2 * KP], U8)
+            src = w2_words[:, :, 2 * a * KP : 2 * (a + 1) * KP]
+            nc.sync.dma_start(dst[:].bitcast(I32), src.bitcast(I32).rearrange("g p c -> p g c"))
+            return dst
+
+        tab2_sc = tile("tab2_sc", [P, PASSES * TC], U8)
+        w2_sc_raw = tile("w2_sc_raw", [P, PASSES * H], U8)
+        nc.gpsimd.memset(tab2_sc[:].bitcast(I32), 0)
+        nc.vector.memset(w2_sc_raw[:].bitcast(I32), 0)
+        warm_in = tile("warm_in", [P, 1], F32)
+        warm_out = tile("warm_out", [P, 1], F32)
+        nc.gpsimd.memset(warm_in[:], 1.0)
+        nc.scalar.activation(warm_out[:], warm_in[:], ACT.Abs_reciprocal_sqrt, bias=1.0)
 
         w2_raw = [load_w2(0)]
         idx2 = load_list("idx2", offs2)
         idx1 = load_list("idx1", offs)
         idx4 = load_list("idx4", offs4)
         idx3 = load_list("idx3", offs3)
-        tab2_w = [load_words("tab2_w%d" % g, tab2_words[g], "T%d" % (2 + g)) for g in range(PASSES)]
+        tab2_w = [load_table("tab2_w%d" % g, tab2_words[g]) for g in range(PASSES)]
         w2_raw.append(load_w2(1))
-        load_scales_side_by_side(nc.sync, tab2_sc, tab2_scales)
-        amp_t = load_vector("amp_t", amp)
-        load_scales_side_by_side(nc.sync, w2_sc_raw, w2_scales)
-        c1_t = load_vector("c1_t", c1)
-        tab_sc = held("tab_sc", [P, T], U8)
+        load_scales_side_by_side(tab2_sc, tab2_scales)
+        amp_t = load_coefficients("amp_t", amp)
+        load_scales_side_by_side(w2_sc_raw, w2_scales)
+        c1_t = load_coefficients("c1_t", c1)
+        tab_sc = tile("tab_sc", [P, T], U8)
         nc.gpsimd.memset(tab_sc[:].bitcast(I32), 0)
-        c0_t = load_vector("c0_t", c0)
+        c0_t = load_coefficients("c0_t", c0)
 
-        w2_w = [held("w2_w%d" % a, [P, PASSES * 2 * KP], U8) for a in range(PASSES)]
-        w2_sc = [held("w2_sc%d" % a, [P, PASSES * KP], U8) for a in range(PASSES)]
+        w2_w = [tile("w2_w%d" % a, [P, PASSES * 2 * KP], U8) for a in range(PASSES)]
+        w2_sc = [tile("w2_sc%d" % a, [P, PASSES * KP], U8) for a in range(PASSES)]
 
         def reorder_w2_words(a):
             nc.vector.tensor_copy(
@@ -127,50 +131,44 @@ def tile_list_creep_life_weave_kernel(
             )
 
         def reorder_w2_scales(a):
-            src = w2_sc_raw[:].rearrange("p (g n) -> p g n", g=PASSES)[:, :, a * KP : (a + 1) * KP]
+            src = w2_sc_raw[:].rearrange("p (g c) -> p g c", g=PASSES)[:, :, a * KP : (a + 1) * KP]
             nc.vector.tensor_copy(
                 w2_sc[a][:].rearrange("p (g t m) -> p g m t", g=PASSES, t=PACK),
                 src.rearrange("p g (m t) -> p g m t", t=PACK),
             )
 
         def gather(name, window, idx, dtype):
-            tile = held(name, [P, S], dtype)
-            nc.vector.tensor_copy(tile[:], window.indirect(idx[:]))
-            return tile
+            dst = tile(name, [P, S], dtype)
+            nc.vector.tensor_copy(dst[:], window.indirect(idx[:]))
+            return dst
 
         reorder_w2_words(0)
-        tab_w = [load_words("tab_w0", tab_words[0], "T0")]
+        tab_w = [load_table("tab_w0", tab_words[0], after="w2_raw0")]
         reorder_w2_words(1)
-        wg2_t = load_confidence("wg2_t", wg2, "T1", (nc.sync, nc.scalar))
+        wg2_first = load_confidence("wg2_first", wg2, 0, 1, "w2_raw1", nc.scalar)
         v2_w = [gather("v2_w0", tab2_w[0][:], idx2, U32)]
-        tab_w.append(load_words("tab_w1", tab_words[1], "T2"))
-        load_scales_stacked(nc.sync, tab_sc, tab_scales)
+        tab_w.append(load_table("tab_w1", tab_words[1], after="tab2_w0"))
+        load_scales_stacked(tab_sc, tab_scales)
         v2_w.append(gather("v2_w1", tab2_w[1][:], idx2, U32))
+        wg2_rest = load_confidence("wg2_rest", wg2, 1, PACK - 1, "tab2_w1", nc.sync)
         v2_sc = [gather("v2_sc%d" % g, tab2_sc[:, g * TC : (g + 1) * TC], idx2, U8) for g in range(PASSES)]
         for a in range(PASSES):
             reorder_w2_scales(a)
         v_w = [gather("v_w%d" % g, tab_w[g][:], idx1, U32) for g in range(PASSES)]
         v_sc = gather("v_sc", tab_sc[:], idx1, U8)
-        w1_raw = {}
-        w1_raw[0, 0] = load_w1(0, 0, "T0")
+        w1_raw = {(0, 0): load_w1(0, 0, after="w2_raw0"), (1, 0): load_w1(1, 0, after="tab2_w0")}
 
-        def bank(i, name):
-            return psum.tile([P, S], F32, name=name, tag="bank%d" % i)
+        def column(coefficients, i):
+            a, t = divmod(i, PACK)
+            return coefficients[:, a, t : t + 1]
 
-        def column(vec, i):
-            return vec[:, i // PACK, i % PACK : i % PACK + 1]
+        def slot(wide, t):
+            return wide[:, t * S : (t + 1) * S]
 
-        def slot(tile, i):
-            return tile[:, (i % PACK) * S : (i % PACK + 1) * S]
+        cool, shifted, weighted, hot_acc, pages = {}, {}, {}, {}, {}
+        w1_w, w1_sc, z_w, z_sc = {}, {}, {}, {}
 
-        SQUARE_TAGS = ["sq", "sq", "sq", "T0", "T4", "recip", "recip", "recip"]
-        RECIP_TAGS = ["recip", "recip", "grouped00", "grouped10", "recip", "grouped01", "sq", "sq"]
-        COOL_TAGS = ["T4", "T6", "T8", "T7", "w3_w", "w3_sc", "cool6", "cool7"]
-        PAGE_TAGS = ["T3", "T2", "tab_sc", "grouped00", "grouped10", "page5", "grouped11", "T0"]
-        HOT_TAGS = ["hot0", "hot1", "T8", "T7", "hot4", "hot5", "hot6", "hot7"]
-        cool, hot, hot_w, pages = {}, {}, {}, {}
-
-        def cool_stream(i):
+        def cool_values(i, square_after="square", recip_tag="recip"):
             a, t = divmod(i, PACK)
             acc = bank(i, "b%d" % i)
             for g in range(PASSES):
@@ -184,32 +182,33 @@ def tile_list_creep_life_weave_kernel(
                     start=(g == 0),
                     stop=(g == PASSES - 1),
                 )
-            square = held("square%d" % i, [P, S], F32, tag=SQUARE_TAGS[i])
+            square = tile("square%d" % i, [P, S], F32, square_after)
             nc.scalar.activation(square[:], acc[:], ACT.Square)
-            root = held("root%d" % i, [P, S], F32, tag="root")
+            root = tile("root%d" % i, [P, S], F32, "root")
             nc.scalar.activation(root[:], square[:], ACT.Abs_reciprocal_sqrt, bias=1.0)
-            recip = held("recip%d" % i, [P, S], F32, tag=RECIP_TAGS[i])
+            recip = tile("recip%d" % i, [P, S], F32, recip_tag)
             nc.scalar.activation(recip[:], root[:], ACT.Square)
-            cool[i] = held("cool%d" % i, [P, S], F32, tag=COOL_TAGS[i])
+            cool[i] = tile("cool%d" % i, [P, S], F32)
             nc.scalar.activation(cool[i][:], recip[:], ACT.Copy, scale=column(amp_t, i))
 
-        w1_w, w1_sc = {}, {}
+        def scatter_cool(i, page_after=None):
+            t = i % PACK
+            pages[i] = tile("page%d" % i, [P, T2], F32, page_after)
+            confidence = wg2_first[:] if t == 0 else slot(wg2_rest, t - 1)
+            nc.vector.tensor_tensor(pages[i][:].indirect(idx4[:]), cool[i][:], confidence, MULT)
 
         def quantise_w1(g, a):
-            if True:
-                grouped = held("grouped%d%d" % (g, a), [P, PACK * KP], BF16)
-                nc.scalar.copy(
-                    grouped[:].rearrange("p (t m j) -> p m t j", t=PACK, j=PACK),
-                    w1_raw[g, a][:].rearrange("p j (m t) -> p m t j", t=PACK),
-                )
-                w1_w[g, a] = held("w1_w%d%d" % (g, a), [P, KP], U32)
-                w1_sc[g, a] = held("w1_sc%d%d" % (g, a), [P, KP], U8)
-                nc.vector.quantize_mx(out=w1_w[g, a][:].bitcast(E4M3), scales=w1_sc[g, a][:], in_=grouped[:])
-
-        hot_acc = {}
-        feature = [held("feature%d" % a, [P, PACK * S], F32) for a in range(PASSES)]
+            grouped = tile("grouped%d%d" % (g, a), [P, PACK * KP], BF16)
+            nc.scalar.copy(
+                grouped[:].rearrange("p (t m j) -> p m t j", t=PACK, j=PACK),
+                w1_raw[g, a][:].rearrange("p j (m t) -> p m t j", t=PACK),
+            )
+            w1_w[g, a] = tile("w1_w%d%d" % (g, a), [P, KP], U32)
+            w1_sc[g, a] = tile("w1_sc%d%d" % (g, a), [P, KP], U8)
+            nc.vector.quantize_mx(out=w1_w[g, a][:].bitcast(E4M3), scales=w1_sc[g, a][:], in_=grouped[:])
 
         def hot_features(a):
+            weighted[a] = tile("weighted%d" % a, [P, PACK * S], F32)
             for t in range(PACK):
                 i = PACK * a + t
                 hot_acc[i] = bank(i, "a%d" % i)
@@ -219,136 +218,138 @@ def tile_list_creep_life_weave_kernel(
                         lhsT=w1_w[g, a][:, t * P : (t + 1) * P].bitcast(E4M3),
                         lhsT_scale=w1_sc[g, a][:, t * P : (t + 1) * P],
                         rhs=v_w[g][:].bitcast(E4M3),
-                        rhs_scale=v_sc[4 * g : P, :],
+                        rhs_scale=v_sc[SCALE_ROWS * g : P, :],
                         start=(g == 0),
                         stop=(g == PASSES - 1),
                     )
-                nc.scalar.copy(slot(feature[a], i), hot_acc[i][:])
-            hot_w[a] = feature[a]
-            nc.vector.tensor_tensor(hot_w[a][:], feature[a][:], wg1_t[:], MULT)
+                nc.scalar.copy(slot(weighted[a], t), hot_acc[i][:])
+            nc.vector.tensor_tensor(weighted[a][:], weighted[a][:], wg1_t[:], MULT)
 
-        def hot_shifted(i):
-            hot[i] = held("hot%d" % i, [P, S], F32, tag=HOT_TAGS[i])
-            nc.scalar.activation(hot[i][:], hot_acc[i][:], ACT.Identity, bias=column(c1_t, i))
-
-        def scatter_cool(i):
-            pages[i] = held("page%d" % i, [P, T2], F32, tag=PAGE_TAGS[i])
-            nc.vector.tensor_tensor(pages[i][:].indirect(idx4[:]), cool[i][:], slot(wg2_t, i), MULT)
+        def hot_shifted(i, after=None):
+            shifted[i] = tile("shifted%d" % i, [P, S], F32, after)
+            nc.scalar.activation(shifted[i][:], hot_acc[i][:], ACT.Identity, bias=column(c1_t, i))
 
         def scatter_hot(i):
-            nc.vector.tensor_tensor(pages[i][:].indirect(idx3[:]), hot[i][:], slot(hot_w[i // PACK], i), MULT)
+            a, t = divmod(i, PACK)
+            nc.vector.tensor_tensor(pages[i][:].indirect(idx3[:]), shifted[i][:], slot(weighted[a], t), MULT)
 
         def round_plane(pairs, i, c, width):
             u, e = divmod(i % PACK, 2)
-            chunk = pairs[:, PACK * c : PACK * (c + width)].rearrange("p (u c e) -> p u c e", u=2, e=2)
-            nc.scalar.activation(chunk[:, u, :, e], pages[i][:, c : c + width], ACT.Identity, bias=column(c0_t, i))
+            part = pairs[:, PACK * c : PACK * (c + width)].rearrange("p (u c e) -> p u c e", u=2, e=2)
+            nc.scalar.activation(part[:, u, :, e], pages[i][:, c : c + width], ACT.Identity, bias=column(c0_t, i))
 
-        z_w = {}
-        z_sc = [held("z_sc%d" % a, [P, T2], U8) for a in range(PASSES)]
-
-        def weave_views(z, pairs, c, width, dtype):
-            cols = slice(PACK * c, PACK * (c + width))
+        def weave_views(z, pairs, dtype):
             return (
-                z[:, cols].bitcast(dtype).rearrange("p (c u) -> p c u", u=2),
-                pairs[:, cols].bitcast(dtype).rearrange("p (u c) -> p c u", u=2),
+                z.bitcast(dtype).rearrange("p (c u) -> p c u", u=2),
+                pairs.bitcast(dtype).rearrange("p (u c) -> p c u", u=2),
             )
 
-        def quantise_z(a, z, c, width):
-            nc.vector.quantize_mx(
-                out=z_w[a][:, c : c + width].bitcast(E4M3),
-                scales=z_sc[a][:, c : c + width],
-                in_=z[:, PACK * c : PACK * (c + width)],
-            )
+        def quantise_z(key, z, after=None):
+            width = z.shape[1] // PACK
+            z_w[key] = tile("z_w%d%d" % key, [P, width], U32, after)
+            z_sc[key] = tile("z_sc%d%d" % key, [P, width], U8)
+            nc.vector.quantize_mx(out=z_w[key][:].bitcast(E4M3), scales=z_sc[key][:], in_=z)
 
-        def score_pass(a, acc, q, half):
+        def score_pass(a, b, key, c):
             for m in range(2):
-                n0 = (2 * half + m) * P
+                n0 = (2 * (b % 2) + m) * P
                 nc.tensor.matmul_mx(
-                    out=acc[:, m * QW : (m + 1) * QW],
+                    out=scores[b][:, m * CHUNK : (m + 1) * CHUNK],
                     lhsT=w3_w[:, a, n0 : n0 + P].bitcast(E4M3),
-                    lhsT_scale=w3_sc[4 * a : P, n0 : n0 + P],
-                    rhs=z_w[a][:, q * QW : (q + 1) * QW].bitcast(E4M3),
-                    rhs_scale=z_sc[a][:, q * QW : (q + 1) * QW],
+                    lhsT_scale=w3_sc[SCALE_ROWS * a : P, n0 : n0 + P],
+                    rhs=z_w[key][:, c : c + CHUNK].bitcast(E4M3),
+                    rhs_scale=z_sc[key][:, c : c + CHUNK],
                     start=(a == 0 and m == 0),
                     stop=(a == PASSES - 1 and m == 1),
                 )
 
-        last = PLANES - 1
-
-        def cool_plane(i):
-            cool_stream(i)
-            scatter_cool(i)
-
-        def hot_plane(i):
-            hot_shifted(i)
-            scatter_hot(i)
-
-        cool_plane(0)
-        w1_raw[1, 0] = load_w1(1, 0, "T4")
-        cool_plane(1)
-        wg1_t = load_confidence("wg1_t", wg1, "T6", (nc.sync, nc.sync))
-        cool_plane(2)
-        w1_raw[0, 1] = load_w1(0, 1, "T8")
-        quantise_w1(0, 0)
-        cool_plane(3)
-        w1_raw[1, 1] = load_w1(1, 1, "T7")
-        quantise_w1(1, 0)
-        cool_plane(4)
-        w3_w = held("w3_w", [P, PASSES, N], U32)
+        cool_values(0)
+        scatter_cool(0)
+        wg1_t = load_confidence("wg1_t", wg1, 0, PACK, "cool0", nc.sync)
+        cool_values(4)
+        scatter_cool(4, page_after="tab_sc")
+        w1_raw[0, 1] = load_w1(0, 1, after="cool4")
+        cool_values(1)
+        scatter_cool(1)
+        w1_raw[1, 1] = load_w1(1, 1, after="cool1")
+        cool_values(5, recip_tag="grouped00")
+        scatter_cool(5)
+        w3_w = tile("w3_w", [P, PASSES, N], U32, "cool5")
         nc.sync.dma_start(w3_w[:].bitcast(I32), w3_words.rearrange("g p c i -> p g (c i)").bitcast(I32))
-        cool_plane(5)
-        w3_sc = held("w3_sc", [P, N], U8)
+        quantise_w1(0, 0)
+        cool_values(2, square_after="w2_raw0", recip_tag="grouped10")
+        scatter_cool(2, page_after="grouped00")
+        w3_sc = tile("w3_sc", [P, N], U8, "cool2")
         nc.gpsimd.memset(w3_sc[:].bitcast(I32), 0)
-        load_scales_stacked(nc.sync, w3_sc, w3_scales)
-        hot_features(0)
-        hot_plane(0)
-        hot_plane(1)
-        quantise_w1(0, 1)
-        hot_plane(2)
-        quantise_w1(1, 1)
-        hot_plane(3)
-        cool_plane(6)
-        cool_stream(7)
-        pairs = held("pairs0", [P, PACK * T2], BF16, tag="grouped01")
-        round_plane(pairs, 0, 0, T2)
-        round_plane(pairs, 1, 0, T2)
-        hot_features(1)
-        hot_plane(4)
-        round_plane(pairs, 2, 0, T2)
-        hot_plane(5)
-        round_plane(pairs, 3, 0, T2)
-        hot_plane(6)
-        hot_shifted(7)
-        z = held("z0", [P, PACK * T2], BF16, tag="T0")
-        nc.scalar.copy(*weave_views(z, pairs, 0, T2, U32))
-        z_w[0] = held("z_w0", [P, T2], U32, tag="hot6")
-        z_w[1] = held("z_w1", [P, T2], U32)
-        quantise_z(0, z, 0, T2)
-        scores = [bank(b, "score%d" % b) for b in range(2 * NQ)]
-        for b in range(2 * NQ):
-            score_pass(0, scores[b], b // 2, b % 2)
+        load_scales_stacked(w3_sc, w3_scales)
+        quantise_w1(1, 0)
+        cool_values(3, square_after="tab2_w0")
+        scatter_cool(3, page_after="grouped10")
+        cool_values(6, square_after="recip", recip_tag="grouped01")
+        scatter_cool(6)
 
-        scatter_cool(last)
-        scatter_hot(last)
-        pairs = held("pairs1", [P, PACK * T2], BF16, tag="T4")
+        hot_features(0)
+        hot_shifted(0)
+        scatter_hot(0)
+        quantise_w1(0, 1)
+        hot_shifted(1, after="cool4")
+        scatter_hot(1)
+        quantise_w1(1, 1)
+        hot_shifted(2, after="cool1")
+        scatter_hot(2)
+        hot_shifted(3)
+        scatter_hot(3)
+        cool_values(LAST, square_after="recip", recip_tag="square")
+
+        pairs = tile("pairs0", [P, PACK * T2], BF16, "grouped01")
+
+        def round_first_pass(i):
+            for h in range(2):
+                round_plane(pairs, i, h * HALF, HALF)
+
+        round_first_pass(0)
+        round_first_pass(1)
+        hot_features(1)
+        hot_shifted(4)
+        scatter_hot(4)
+        round_first_pass(2)
+        hot_shifted(5)
+        scatter_hot(5)
+        round_first_pass(3)
+        hot_shifted(6)
+        scatter_hot(6)
+        hot_shifted(LAST)
+        halves = [tile("z0%d" % h, [P, PACK * HALF], BF16) for h in range(2)]
+        for h in range(2):
+            nc.scalar.copy(*weave_views(halves[h][:], pairs[:, PACK * h * HALF : PACK * (h + 1) * HALF], U32))
+        scores = [bank(b, "score%d" % b) for b in range(BANKS)]
+        quantise_z((0, 0), halves[0][:], after="shifted6")
+        for b in range(BANKS // 2):
+            score_pass(0, b, (0, 0), (b // 2) * CHUNK)
+        scatter_cool(LAST, page_after="z00")
+        quantise_z((0, 1), halves[1][:], after="cool%d" % LAST)
+        for b in range(BANKS // 2, BANKS):
+            score_pass(0, b, (0, 1), (b // 2) * CHUNK - HALF)
+        scatter_hot(LAST)
+
+        pairs = tile("pairs1", [P, PACK * T2], BF16, "tab2_w0")
         for i in range(PACK, PLANES):
-            for q in range(NQ):
-                round_plane(pairs, i, q * QW, QW)
-        z = held("z1", [P, PACK * T2], BF16, tag="feature0")
-        staged = [held("staged%d" % s, [P, NQ * S], F32, tag=("T8", "T7")[s]) for s in range(2)]
-        for q in range(NQ):
-            nc.vector.tensor_copy(*weave_views(z, pairs, q * QW, QW, I32))
-            quantise_z(1, z, q * QW, QW)
-            for half in range(2):
-                score_pass(1, scores[2 * q + half], q, half)
-        for b in range(2 * NQ):
-            q, half = divmod(b, 2)
-            result = staged[b // NQ][:, (b % NQ) * S : (b % NQ + 1) * S]
-            if b in (3, 5, 7):
+            for q in range(CHUNKS):
+                round_plane(pairs, i, q * CHUNK, CHUNK)
+        z = tile("z1", [P, PACK * T2], BF16, "weighted0")
+        for q in range(CHUNKS):
+            cols = slice(PACK * q * CHUNK, PACK * (q + 1) * CHUNK)
+            nc.vector.tensor_copy(*weave_views(z[:, cols], pairs[:, cols], I32))
+            quantise_z((1, q), z[:, cols])
+            for b in (2 * q, 2 * q + 1):
+                score_pass(1, b, (1, q), 0)
+        staged = [tile("staged%d" % s, [P, CHUNKS * S], F32, ("cool4", "cool1")[s]) for s in range(2)]
+        for b in range(BANKS):
+            q, lower = divmod(b, 2)
+            result = slot(staged[b // CHUNKS], b % CHUNKS)
+            if q > 0 and lower == 1:
                 nc.vector.tensor_copy(result, scores[b][:])
             else:
                 nc.scalar.copy(result, scores[b][:])
-            nc.sync.dma_start(
-                out[2 * half * P : 2 * (half + 1) * P, q * QW : (q + 1) * QW].rearrange("(m p) c -> p m c", p=P),
-                result.rearrange("p (m c) -> p m c", m=2),
-            )
+            rows = out[2 * lower * P : 2 * (lower + 1) * P, q * CHUNK : (q + 1) * CHUNK]
+            nc.sync.dma_start(rows.rearrange("(m p) c -> p m c", p=P), result.rearrange("p (m c) -> p m c", m=2))

@@ -15,6 +15,7 @@ E4M3 = mybir.dt.float8_e4m3fn_x4
 E2M1 = mybir.dt.float4_e2m1fn_x4
 ACT = mybir.ActivationFunctionType
 MULT = mybir.AluOpType.mult
+ADD = mybir.AluOpType.add
 
 P = 128
 PACK = 4
@@ -77,9 +78,9 @@ def tile_list_creep_life_weave_kernel(
             nc.gpsimd.dma_start(dst[:], src.rearrange("(a p t) -> p a t", a=PASSES, t=PACK))
             return dst
 
-        def load_confidence(name, src, first, count, after, upper_queue):
-            dst = tile(name, [P, count * S], F32, after)
-            rows = src.rearrange("(u t) j -> u (t j)", t=PACK)[:, first * S : (first + count) * S]
+        def load_confidence(name, src, after, upper_queue):
+            dst = tile(name, [P, PACK * S], F32, after)
+            rows = src.rearrange("(u t) j -> u (t j)", t=PACK)
             for q in range(QUADS):
                 queue = nc.sync if q < QUADS // 2 else upper_queue
                 queue.dma_start(dst[QUAD * q : QUAD * (q + 1), :], rows)
@@ -145,18 +146,17 @@ def tile_list_creep_life_weave_kernel(
         reorder_w2_words(0)
         tab_w = [load_table("tab_w0", tab_words[0], after="w2_raw0")]
         reorder_w2_words(1)
-        wg2_first = load_confidence("wg2_first", wg2, 0, 1, "w2_raw1", nc.scalar)
+        wg2_t = load_confidence("wg2_t", wg2, "w2_raw1", nc.scalar)
         v2_w = [gather("v2_w0", tab2_w[0][:], idx2, U32)]
         tab_w.append(load_table("tab_w1", tab_words[1], after="tab2_w0"))
         load_scales_stacked(tab_sc, tab_scales)
         v2_w.append(gather("v2_w1", tab2_w[1][:], idx2, U32))
-        wg2_rest = load_confidence("wg2_rest", wg2, 1, PACK - 1, "tab2_w1", nc.sync)
         v2_sc = [gather("v2_sc%d" % g, tab2_sc[:, g * TC : (g + 1) * TC], idx2, U8) for g in range(PASSES)]
         for a in range(PASSES):
             reorder_w2_scales(a)
         v_w = [gather("v_w%d" % g, tab_w[g][:], idx1, U32) for g in range(PASSES)]
         v_sc = gather("v_sc", tab_sc[:], idx1, U8)
-        w1_raw = {(0, 0): load_w1(0, 0, after="w2_raw0"), (1, 0): load_w1(1, 0, after="tab2_w0")}
+        w1_raw = {(0, 0): load_w1(0, 0, after="w2_raw0")}
 
         def column(coefficients, i):
             a, t = divmod(i, PACK)
@@ -165,7 +165,7 @@ def tile_list_creep_life_weave_kernel(
         def slot(wide, t):
             return wide[:, t * S : (t + 1) * S]
 
-        cool, shifted, weighted, hot_acc, pages = {}, {}, {}, {}, {}
+        cool, feature, weighted, hot_acc, pages = {}, {}, {}, {}, {}
         w1_w, w1_sc, z_w, z_sc = {}, {}, {}, {}
 
         def cool_values(i, square_after="square", recip_tag="recip"):
@@ -192,10 +192,8 @@ def tile_list_creep_life_weave_kernel(
             nc.scalar.activation(cool[i][:], recip[:], ACT.Copy, scale=column(amp_t, i))
 
         def scatter_cool(i, page_after=None):
-            t = i % PACK
             pages[i] = tile("page%d" % i, [P, T2], F32, page_after)
-            confidence = wg2_first[:] if t == 0 else slot(wg2_rest, t - 1)
-            nc.vector.tensor_tensor(pages[i][:].indirect(idx4[:]), cool[i][:], confidence, MULT)
+            nc.vector.tensor_tensor(pages[i][:].indirect(idx4[:]), cool[i][:], slot(wg2_t, i % PACK), MULT)
 
         def quantise_w1(g, a):
             grouped = tile("grouped%d%d" % (g, a), [P, PACK * KP], BF16)
@@ -207,8 +205,7 @@ def tile_list_creep_life_weave_kernel(
             w1_sc[g, a] = tile("w1_sc%d%d" % (g, a), [P, KP], U8)
             nc.vector.quantize_mx(out=w1_w[g, a][:].bitcast(E4M3), scales=w1_sc[g, a][:], in_=grouped[:])
 
-        def hot_features(a):
-            weighted[a] = tile("weighted%d" % a, [P, PACK * S], F32)
+        def hot_matmuls(a):
             for t in range(PACK):
                 i = PACK * a + t
                 hot_acc[i] = bank(i, "a%d" % i)
@@ -222,26 +219,32 @@ def tile_list_creep_life_weave_kernel(
                         start=(g == 0),
                         stop=(g == PASSES - 1),
                     )
-                nc.scalar.copy(slot(weighted[a], t), hot_acc[i][:])
-            nc.vector.tensor_tensor(weighted[a][:], weighted[a][:], wg1_t[:], MULT)
 
-        def hot_shifted(i, after=None):
-            shifted[i] = tile("shifted%d" % i, [P, S], F32, after)
-            nc.scalar.activation(shifted[i][:], hot_acc[i][:], ACT.Identity, bias=column(c1_t, i))
+        def hot_weights(a, after):
+            weighted[a] = tile("weighted%d" % a, [P, PACK * S], F32, after)
+            for t in range(PACK):
+                i = PACK * a + t
+                nc.vector.scalar_tensor_tensor(
+                    slot(weighted[a], t), hot_acc[i][:], column(c1_t, i), slot(wg1_t, t), ADD, MULT
+                )
+
+        def hot_feature(i, after=None):
+            feature[i] = tile("feature%d" % i, [P, S], F32, after)
+            nc.scalar.copy(feature[i][:], hot_acc[i][:])
 
         def scatter_hot(i):
             a, t = divmod(i, PACK)
-            nc.vector.tensor_tensor(pages[i][:].indirect(idx3[:]), shifted[i][:], slot(weighted[a], t), MULT)
+            nc.vector.tensor_tensor(pages[i][:].indirect(idx3[:]), feature[i][:], slot(weighted[a], t), MULT)
 
-        def round_plane(pairs, i, c, width):
-            u, e = divmod(i % PACK, 2)
-            part = pairs[:, PACK * c : PACK * (c + width)].rearrange("p (u c e) -> p u c e", u=2, e=2)
-            nc.scalar.activation(part[:, u, :, e], pages[i][:, c : c + width], ACT.Identity, bias=column(c0_t, i))
+        def round_plane(planes, i, c, width):
+            nc.scalar.activation(
+                planes[:, i % PACK, c : c + width], pages[i][:, c : c + width], ACT.Identity, bias=column(c0_t, i)
+            )
 
-        def weave_views(z, pairs, dtype):
+        def weave_views(z, planes):
             return (
-                z.bitcast(dtype).rearrange("p (c u) -> p c u", u=2),
-                pairs.bitcast(dtype).rearrange("p (u c) -> p c u", u=2),
+                z.rearrange("p (c n t) -> p c t n", n=PACK, t=PACK),
+                planes.rearrange("p t (c n) -> p c t n", n=PACK),
             )
 
         def quantise_z(key, z, after=None):
@@ -265,65 +268,60 @@ def tile_list_creep_life_weave_kernel(
 
         cool_values(0)
         scatter_cool(0)
-        wg1_t = load_confidence("wg1_t", wg1, 0, PACK, "cool0", nc.sync)
-        cool_values(4)
-        scatter_cool(4, page_after="tab_sc")
-        w1_raw[0, 1] = load_w1(0, 1, after="cool4")
+        w1_raw[1, 0] = load_w1(1, 0, after="cool0")
         cool_values(1)
-        scatter_cool(1)
-        w1_raw[1, 1] = load_w1(1, 1, after="cool1")
-        cool_values(5, recip_tag="grouped00")
-        scatter_cool(5)
-        w3_w = tile("w3_w", [P, PASSES, N], U32, "cool5")
-        nc.sync.dma_start(w3_w[:].bitcast(I32), w3_words.rearrange("g p c i -> p g (c i)").bitcast(I32))
+        scatter_cool(1, page_after="tab2_w0")
+        wg1_t = load_confidence("wg1_t", wg1, "cool1", nc.sync)
+        cool_values(2, recip_tag="grouped00")
+        scatter_cool(2, page_after="tab_sc")
+        w1_raw[0, 1] = load_w1(0, 1, after="cool2")
         quantise_w1(0, 0)
-        cool_values(2, square_after="w2_raw0", recip_tag="grouped10")
-        scatter_cool(2, page_after="grouped00")
-        w3_sc = tile("w3_sc", [P, N], U8, "cool2")
+        cool_values(3, square_after="w2_raw0", recip_tag="grouped10")
+        scatter_cool(3, page_after="grouped00")
+        w1_raw[1, 1] = load_w1(1, 1, after="cool3")
+        quantise_w1(1, 0)
+        cool_values(4, square_after="cool0")
+        scatter_cool(4, page_after="grouped10")
+        w3_w = tile("w3_w", [P, PASSES, N], U32, "cool4")
+        nc.sync.dma_start(w3_w[:].bitcast(I32), w3_words.rearrange("g p c i -> p g (c i)").bitcast(I32))
+        cool_values(5, square_after="recip", recip_tag="grouped01")
+        scatter_cool(5)
+
+        hot_matmuls(0)
+        hot_feature(0)
+        hot_weights(0, after="cool5")
+        scatter_hot(0)
+        w3_sc = tile("w3_sc", [P, N], U8, "feature0")
         nc.gpsimd.memset(w3_sc[:].bitcast(I32), 0)
         load_scales_stacked(w3_sc, w3_scales)
-        quantise_w1(1, 0)
-        cool_values(3, square_after="tab2_w0")
-        scatter_cool(3, page_after="grouped10")
-        cool_values(6, square_after="recip", recip_tag="grouped01")
-        scatter_cool(6)
-
-        hot_features(0)
-        hot_shifted(0)
-        scatter_hot(0)
         quantise_w1(0, 1)
-        hot_shifted(1, after="cool4")
+        hot_feature(1, after="cool2")
         scatter_hot(1)
         quantise_w1(1, 1)
-        hot_shifted(2, after="cool1")
+        hot_feature(2, after="cool3")
         scatter_hot(2)
-        hot_shifted(3)
+        hot_feature(3)
         scatter_hot(3)
+        cool_values(6, square_after="recip")
+        scatter_cool(6)
         cool_values(LAST, square_after="recip", recip_tag="square")
 
-        pairs = tile("pairs0", [P, PACK * T2], BF16, "grouped01")
-
-        def round_first_pass(i):
-            for h in range(2):
-                round_plane(pairs, i, h * HALF, HALF)
-
-        round_first_pass(0)
-        round_first_pass(1)
-        hot_features(1)
-        hot_shifted(4)
-        scatter_hot(4)
-        round_first_pass(2)
-        hot_shifted(5)
-        scatter_hot(5)
-        round_first_pass(3)
-        hot_shifted(6)
-        scatter_hot(6)
-        hot_shifted(LAST)
+        planes = tile("planes0", [P, PACK, T2], BF16, "grouped11")
+        round_plane(planes, 0, 0, T2)
+        round_plane(planes, 1, 0, T2)
+        hot_matmuls(1)
+        for i in range(PACK, PLANES):
+            hot_feature(i)
+        hot_weights(1, after="feature3")
+        for i in range(PACK, LAST):
+            scatter_hot(i)
+        round_plane(planes, 2, 0, T2)
+        round_plane(planes, 3, 0, T2)
         halves = [tile("z0%d" % h, [P, PACK * HALF], BF16) for h in range(2)]
         for h in range(2):
-            nc.scalar.copy(*weave_views(halves[h][:], pairs[:, PACK * h * HALF : PACK * (h + 1) * HALF], U32))
+            nc.scalar.copy(*weave_views(halves[h][:], planes[:, :, h * HALF : (h + 1) * HALF]))
         scores = [bank(b, "score%d" % b) for b in range(BANKS)]
-        quantise_z((0, 0), halves[0][:], after="shifted6")
+        quantise_z((0, 0), halves[0][:], after="feature6")
         for b in range(BANKS // 2):
             score_pass(0, b, (0, 0), (b // 2) * CHUNK)
         scatter_cool(LAST, page_after="z00")
@@ -332,22 +330,23 @@ def tile_list_creep_life_weave_kernel(
             score_pass(0, b, (0, 1), (b // 2) * CHUNK - HALF)
         scatter_hot(LAST)
 
-        pairs = tile("pairs1", [P, PACK * T2], BF16, "tab2_w0")
-        for i in range(PACK, PLANES):
-            for q in range(CHUNKS):
-                round_plane(pairs, i, q * CHUNK, CHUNK)
-        z = tile("z1", [P, PACK * T2], BF16, "weighted0")
+        planes = tile("planes1", [P, PACK, T2], BF16, "cool0")
+        for i in range(PACK, LAST):
+            round_plane(planes, i, 0, T2)
+        for q in range(CHUNKS):
+            round_plane(planes, LAST, q * CHUNK, CHUNK)
+        z = tile("z1", [P, PACK * T2], BF16, "cool5")
         for q in range(CHUNKS):
             cols = slice(PACK * q * CHUNK, PACK * (q + 1) * CHUNK)
-            nc.vector.tensor_copy(*weave_views(z[:, cols], pairs[:, cols], I32))
+            nc.vector.tensor_copy(*weave_views(z[:, cols], planes[:, :, q * CHUNK : (q + 1) * CHUNK]))
             quantise_z((1, q), z[:, cols])
             for b in (2 * q, 2 * q + 1):
                 score_pass(1, b, (1, q), 0)
-        staged = [tile("staged%d" % s, [P, CHUNKS * S], F32, ("cool4", "cool1")[s]) for s in range(2)]
+        staged = [tile("staged%d" % s, [P, CHUNKS * S], F32, ("cool2", "cool3")[s]) for s in range(2)]
         for b in range(BANKS):
             q, lower = divmod(b, 2)
             result = slot(staged[b // CHUNKS], b % CHUNKS)
-            if q > 0 and lower == 1:
+            if q >= CHUNKS // 2 and lower == 1:
                 nc.vector.tensor_copy(result, scores[b][:])
             else:
                 nc.scalar.copy(result, scores[b][:])

@@ -1,6 +1,7 @@
 from contextlib import ExitStack
 
 import concourse.mybir as mybir
+from concourse.masks import make_identity
 
 K, H, N, T, TC, S, T2 = 1024, 1024, 512, 2048, 1024, 512, 1024
 FLOPS = 2 * (2 * K * H * S + H * N * T2)
@@ -78,12 +79,11 @@ def tile_list_creep_life_weave_kernel(
             nc.gpsimd.dma_start(dst[:], src.rearrange("(a p t) -> p a t", a=PASSES, t=PACK))
             return dst
 
-        def load_confidence(name, src, after, upper_queue):
-            dst = tile(name, [P, PACK * S], F32, after)
-            rows = src.rearrange("(u t) j -> u (t j)", t=PACK)
+        def load_wg1(after):
+            dst = tile("wg1_t", [P, PACK * S], F32, after)
+            rows = wg1.rearrange("(u t) j -> u (t j)", t=PACK)
             for q in range(QUADS):
-                queue = nc.sync if q < QUADS // 2 else upper_queue
-                queue.dma_start(dst[QUAD * q : QUAD * (q + 1), :], rows)
+                nc.sync.dma_start(dst[QUAD * q : QUAD * (q + 1), :], rows)
             return dst
 
         def load_w1(g, a, after):
@@ -92,28 +92,22 @@ def tile_list_creep_life_weave_kernel(
             nc.sync.dma_start(dst[:], src.rearrange("(p j) c -> p j c", j=PACK))
             return dst
 
-        def load_w2(a):
-            dst = tile("w2_raw%d" % a, [P, PASSES, 2 * KP], U8)
-            src = w2_words[:, :, 2 * a * KP : 2 * (a + 1) * KP]
-            nc.sync.dma_start(dst[:].bitcast(I32), src.bitcast(I32).rearrange("g p c -> p g c"))
-            return dst
-
         tab2_sc = tile("tab2_sc", [P, PASSES * TC], U8)
         w2_sc_raw = tile("w2_sc_raw", [P, PASSES * H], U8)
         nc.gpsimd.memset(tab2_sc[:].bitcast(I32), 0)
         nc.vector.memset(w2_sc_raw[:].bitcast(I32), 0)
-        warm_in = tile("warm_in", [P, 1], F32)
-        warm_out = tile("warm_out", [P, 1], F32)
-        nc.gpsimd.memset(warm_in[:], 1.0)
-        nc.scalar.activation(warm_out[:], warm_in[:], ACT.Abs_reciprocal_sqrt, bias=1.0)
+        identity = tile("identity", [P, P], F32)
+        make_identity(nc, identity[:])
 
-        w2_raw = [load_w2(0)]
+        w2_raw = tile("w2_raw", [P, PASSES, 2 * H], U8)
+        nc.sync.dma_start(w2_raw[:].bitcast(I32), w2_words.bitcast(I32).rearrange("g p c -> p g c"))
         idx2 = load_list("idx2", offs2)
+        wg2_rows = tile("wg2_rows", [P, S], F32)
+        nc.sync.dma_start(wg2_rows[:], wg2)
         idx1 = load_list("idx1", offs)
         idx4 = load_list("idx4", offs4)
         idx3 = load_list("idx3", offs3)
         tab2_w = [load_table("tab2_w%d" % g, tab2_words[g]) for g in range(PASSES)]
-        w2_raw.append(load_w2(1))
         load_scales_side_by_side(tab2_sc, tab2_scales)
         amp_t = load_coefficients("amp_t", amp)
         load_scales_side_by_side(w2_sc_raw, w2_scales)
@@ -128,7 +122,7 @@ def tile_list_creep_life_weave_kernel(
         def reorder_w2_words(a):
             nc.vector.tensor_copy(
                 w2_w[a][:].bitcast(U16).rearrange("p (g t m) -> p g m t", g=PASSES, t=PACK),
-                w2_raw[a][:].bitcast(U16).rearrange("p g (m t) -> p g m t", t=PACK),
+                w2_raw[:].bitcast(U16)[:, :, a * KP : (a + 1) * KP].rearrange("p g (m t) -> p g m t", t=PACK),
             )
 
         def reorder_w2_scales(a):
@@ -143,10 +137,9 @@ def tile_list_creep_life_weave_kernel(
             nc.vector.tensor_copy(dst[:], window.indirect(idx[:]))
             return dst
 
-        reorder_w2_words(0)
-        tab_w = [load_table("tab_w0", tab_words[0], after="w2_raw0")]
-        reorder_w2_words(1)
-        wg2_t = load_confidence("wg2_t", wg2, "w2_raw1", nc.scalar)
+        for a in range(PASSES):
+            reorder_w2_words(a)
+        tab_w = [load_table("tab_w0", tab_words[0], after="w2_raw")]
         v2_w = [gather("v2_w0", tab2_w[0][:], idx2, U32)]
         tab_w.append(load_table("tab_w1", tab_words[1], after="tab2_w0"))
         load_scales_stacked(tab_sc, tab_scales)
@@ -156,7 +149,7 @@ def tile_list_creep_life_weave_kernel(
             reorder_w2_scales(a)
         v_w = [gather("v_w%d" % g, tab_w[g][:], idx1, U32) for g in range(PASSES)]
         v_sc = gather("v_sc", tab_sc[:], idx1, U8)
-        w1_raw = {(0, 0): load_w1(0, 0, after="w2_raw0")}
+        w1_raw = {(0, 0): load_w1(0, 0, after="w2_raw")}
 
         def column(coefficients, i):
             a, t = divmod(i, PACK)
@@ -165,10 +158,31 @@ def tile_list_creep_life_weave_kernel(
         def slot(wide, t):
             return wide[:, t * S : (t + 1) * S]
 
-        cool, feature, weighted, hot_acc, pages = {}, {}, {}, {}, {}
+        def spread_wg2():
+            turned = bank(PACK - 1, "wg2_turned")
+            for s in range(S // P):
+                nc.tensor.transpose(turned[:, s * P : (s + 1) * P], wg2_rows[:, s * P : (s + 1) * P], identity[:])
+            spread = [bank(PACK + t, "wg2_spread%d" % t) for t in range(PACK)]
+            for s in range(S // P):
+                repeated = tile("wg2_repeated%d" % s, [P, PACK, QUADS, QUAD], F32)
+                for q in range(QUADS):
+                    nc.scalar.copy(
+                        repeated[:, :, q, :], turned[:, s * P : (s + 1) * P].rearrange("p (u t) -> p t u", t=PACK)
+                    )
+                for t in range(PACK):
+                    nc.tensor.transpose(
+                        spread[t][:, s * P : (s + 1) * P], repeated[:, t].rearrange("p q u -> p (q u)"), identity[:]
+                    )
+            return spread
+
+        cool, cool_weight, feature, weighted, hot_acc, pages = {}, {}, {}, {}, {}, {}
         w1_w, w1_sc, z_w, z_sc = {}, {}, {}, {}
 
-        def cool_values(i, square_after="square", recip_tag="recip"):
+        def weigh_cool(i):
+            cool_weight[i] = tile("cool_weight%d" % i, [P, S], F32)
+            nc.scalar.activation(cool_weight[i][:], wg2_spread[i % PACK][:], ACT.Copy, scale=column(amp_t, i))
+
+        def cool_values(i, square_after="square", root_tag="root"):
             a, t = divmod(i, PACK)
             acc = bank(i, "b%d" % i)
             for g in range(PASSES):
@@ -184,16 +198,14 @@ def tile_list_creep_life_weave_kernel(
                 )
             square = tile("square%d" % i, [P, S], F32, square_after)
             nc.scalar.activation(square[:], acc[:], ACT.Square)
-            root = tile("root%d" % i, [P, S], F32, "root")
+            root = tile("root%d" % i, [P, S], F32, root_tag)
             nc.scalar.activation(root[:], square[:], ACT.Abs_reciprocal_sqrt, bias=1.0)
-            recip = tile("recip%d" % i, [P, S], F32, recip_tag)
-            nc.scalar.activation(recip[:], root[:], ACT.Square)
             cool[i] = tile("cool%d" % i, [P, S], F32)
-            nc.scalar.activation(cool[i][:], recip[:], ACT.Copy, scale=column(amp_t, i))
+            nc.scalar.activation(cool[i][:], root[:], ACT.Square)
 
         def scatter_cool(i, page_after=None):
             pages[i] = tile("page%d" % i, [P, T2], F32, page_after)
-            nc.vector.tensor_tensor(pages[i][:].indirect(idx4[:]), cool[i][:], slot(wg2_t, i % PACK), MULT)
+            nc.vector.tensor_tensor(pages[i][:].indirect(idx4[:]), cool[i][:], cool_weight[i][:], MULT)
 
         def quantise_w1(g, a):
             grouped = tile("grouped%d%d" % (g, a), [P, PACK * KP], BF16)
@@ -266,17 +278,22 @@ def tile_list_creep_life_weave_kernel(
                     stop=(a == PASSES - 1 and m == 1),
                 )
 
+        wg2_spread = spread_wg2()
+        for i in range(PACK):
+            weigh_cool(i)
         cool_values(0)
         scatter_cool(0)
         w1_raw[1, 0] = load_w1(1, 0, after="cool0")
         cool_values(1)
         scatter_cool(1, page_after="tab2_w0")
-        wg1_t = load_confidence("wg1_t", wg1, "cool1", nc.sync)
-        cool_values(2, recip_tag="grouped00")
+        wg1_t = load_wg1(after="cool1")
+        cool_values(2, root_tag="grouped00")
         scatter_cool(2, page_after="tab_sc")
         w1_raw[0, 1] = load_w1(0, 1, after="cool2")
+        for i in range(PACK, PLANES):
+            weigh_cool(i)
         quantise_w1(0, 0)
-        cool_values(3, square_after="w2_raw0", recip_tag="grouped10")
+        cool_values(3, square_after="w2_raw", root_tag="grouped10")
         scatter_cool(3, page_after="grouped00")
         w1_raw[1, 1] = load_w1(1, 1, after="cool3")
         quantise_w1(1, 0)
@@ -284,7 +301,7 @@ def tile_list_creep_life_weave_kernel(
         scatter_cool(4, page_after="grouped10")
         w3_w = tile("w3_w", [P, PASSES, N], U32, "cool4")
         nc.sync.dma_start(w3_w[:].bitcast(I32), w3_words.rearrange("g p c i -> p g (c i)").bitcast(I32))
-        cool_values(5, square_after="recip", recip_tag="grouped01")
+        cool_values(5, square_after="root", root_tag="grouped01")
         scatter_cool(5)
 
         hot_matmuls(0)
@@ -302,9 +319,9 @@ def tile_list_creep_life_weave_kernel(
         scatter_hot(2)
         hot_feature(3)
         scatter_hot(3)
-        cool_values(6, square_after="recip")
+        cool_values(6, square_after="root", root_tag="square")
         scatter_cool(6)
-        cool_values(LAST, square_after="recip", recip_tag="square")
+        cool_values(LAST, square_after="root", root_tag="square")
 
         planes = tile("planes0", [P, PACK, T2], BF16, "grouped11")
         round_plane(planes, 0, 0, T2)

@@ -94,26 +94,26 @@ def tile_list_creep_life_weave_kernel(
 
         tab2_sc = tile("tab2_sc", [P, PASSES * TC], U8)
         w2_sc_raw = tile("w2_sc_raw", [P, PASSES * H], U8)
+        tab_sc = tile("tab_sc", [P, T], U8)
         nc.gpsimd.memset(tab2_sc[:].bitcast(I32), 0)
-        nc.vector.memset(w2_sc_raw[:].bitcast(I32), 0)
+        for plane in (w2_sc_raw, tab_sc):
+            nc.vector.memset(plane[:].bitcast(I32), 0)
         identity = tile("identity", [P, P], F32)
         make_identity(nc, identity[:])
 
+        warm = tile("warm", [P, 2], F32)
+        nc.vector.memset(warm[:, 0:1], 1.0)
+        nc.scalar.activation(warm[:, 1:2], warm[:, 0:1], ACT.Abs_reciprocal_sqrt)
+        wg2_rows = tile("wg2_rows", [P, S], F32)
+        nc.sync.dma_start(wg2_rows[:], wg2)
         w2_raw = tile("w2_raw", [P, PASSES, 2 * H], U8)
         nc.sync.dma_start(w2_raw[:].bitcast(I32), w2_words.bitcast(I32).rearrange("g p c -> p g c"))
         idx2 = load_list("idx2", offs2)
-        wg2_rows = tile("wg2_rows", [P, S], F32)
-        nc.sync.dma_start(wg2_rows[:], wg2)
-        idx1 = load_list("idx1", offs)
-        idx4 = load_list("idx4", offs4)
-        idx3 = load_list("idx3", offs3)
-        tab2_w = [load_table("tab2_w%d" % g, tab2_words[g]) for g in range(PASSES)]
         load_scales_side_by_side(tab2_sc, tab2_scales)
-        amp_t = load_coefficients("amp_t", amp)
+        tab2_w = [load_table("tab2_w%d" % g, tab2_words[g]) for g in range(PASSES)]
         load_scales_side_by_side(w2_sc_raw, w2_scales)
+        amp_t = load_coefficients("amp_t", amp)
         c1_t = load_coefficients("c1_t", c1)
-        tab_sc = tile("tab_sc", [P, T], U8)
-        nc.gpsimd.memset(tab_sc[:].bitcast(I32), 0)
         c0_t = load_coefficients("c0_t", c0)
 
         w2_w = [tile("w2_w%d" % a, [P, PASSES * 2 * KP], U8) for a in range(PASSES)]
@@ -139,17 +139,26 @@ def tile_list_creep_life_weave_kernel(
 
         for a in range(PASSES):
             reorder_w2_words(a)
+        idx1 = load_list("idx1", offs)
         tab_w = [load_table("tab_w0", tab_words[0], after="w2_raw")]
         v2_w = [gather("v2_w0", tab2_w[0][:], idx2, U32)]
         tab_w.append(load_table("tab_w1", tab_words[1], after="tab2_w0"))
         load_scales_stacked(tab_sc, tab_scales)
+        idx4 = load_list("idx4", offs4)
         v2_w.append(gather("v2_w1", tab2_w[1][:], idx2, U32))
+        w1_raw = {(0, 0): load_w1(0, 0, after="tab2_w1")}
         v2_sc = [gather("v2_sc%d" % g, tab2_sc[:, g * TC : (g + 1) * TC], idx2, U8) for g in range(PASSES)]
+        w1_raw[1, 0] = load_w1(1, 0, after="tab2_sc")
         for a in range(PASSES):
             reorder_w2_scales(a)
+        wg1_t = load_wg1(after="w2_sc_raw")
+        idx3 = load_list("idx3", offs3)
         v_w = [gather("v_w%d" % g, tab_w[g][:], idx1, U32) for g in range(PASSES)]
         v_sc = gather("v_sc", tab_sc[:], idx1, U8)
-        w1_raw = {(0, 0): load_w1(0, 0, after="w2_raw")}
+        w1_raw[0, 1] = load_w1(0, 1, after="w2_raw")
+        w1_raw[1, 1] = load_w1(1, 1, after="tab2_w0")
+        w3_w = tile("w3_w", [P, PASSES, N], U32, "tab_sc")
+        nc.sync.dma_start(w3_w[:].bitcast(I32), w3_words.rearrange("g p c i -> p g (c i)").bitcast(I32))
 
         def column(coefficients, i):
             a, t = divmod(i, PACK)
@@ -165,10 +174,8 @@ def tile_list_creep_life_weave_kernel(
             spread = [bank(PACK + t, "wg2_spread%d" % t) for t in range(PACK)]
             for s in range(S // P):
                 repeated = tile("wg2_repeated%d" % s, [P, PACK, QUADS, QUAD], F32)
-                for q in range(QUADS):
-                    nc.scalar.copy(
-                        repeated[:, :, q, :], turned[:, s * P : (s + 1) * P].rearrange("p (u t) -> p t u", t=PACK)
-                    )
+                rows = turned[:, s * P : (s + 1) * P].rearrange("p (u t) -> p t u", t=PACK)
+                nc.scalar.copy(repeated[:], rows.unsqueeze(2).to_broadcast([P, PACK, QUADS, QUAD]))
                 for t in range(PACK):
                     nc.tensor.transpose(
                         spread[t][:, s * P : (s + 1) * P], repeated[:, t].rearrange("p q u -> p (q u)"), identity[:]
@@ -182,9 +189,9 @@ def tile_list_creep_life_weave_kernel(
             cool_weight[i] = tile("cool_weight%d" % i, [P, S], F32)
             nc.scalar.activation(cool_weight[i][:], wg2_spread[i % PACK][:], ACT.Copy, scale=column(amp_t, i))
 
-        def cool_values(i, square_after="square", root_tag="root"):
+        def cool_values(i):
             a, t = divmod(i, PACK)
-            acc = bank(i, "b%d" % i)
+            acc = bank(t, "b%d" % i)
             for g in range(PASSES):
                 c = g * KP + t * P
                 nc.tensor.matmul_mx(
@@ -196,9 +203,9 @@ def tile_list_creep_life_weave_kernel(
                     start=(g == 0),
                     stop=(g == PASSES - 1),
                 )
-            square = tile("square%d" % i, [P, S], F32, square_after)
+            square = tile("square%d" % i, [P, S], F32, "square%d" % (i % 2))
             nc.scalar.activation(square[:], acc[:], ACT.Square)
-            root = tile("root%d" % i, [P, S], F32, root_tag)
+            root = tile("root%d" % i, [P, S], F32, "root%d" % (i % 2))
             nc.scalar.activation(root[:], square[:], ACT.Abs_reciprocal_sqrt, bias=1.0)
             cool[i] = tile("cool%d" % i, [P, S], F32)
             nc.scalar.activation(cool[i][:], root[:], ACT.Square)
@@ -220,7 +227,7 @@ def tile_list_creep_life_weave_kernel(
         def hot_matmuls(a):
             for t in range(PACK):
                 i = PACK * a + t
-                hot_acc[i] = bank(i, "a%d" % i)
+                hot_acc[i] = bank((i + PACK) % PLANES, "a%d" % i)
                 for g in range(PASSES):
                     nc.tensor.matmul_mx(
                         out=hot_acc[i][:],
@@ -279,87 +286,72 @@ def tile_list_creep_life_weave_kernel(
                 )
 
         wg2_spread = spread_wg2()
-        for i in range(PACK):
+        for i in range(PLANES):
             weigh_cool(i)
-        cool_values(0)
-        scatter_cool(0)
-        w1_raw[1, 0] = load_w1(1, 0, after="cool0")
-        cool_values(1)
-        scatter_cool(1, page_after="tab2_w0")
-        wg1_t = load_wg1(after="cool1")
-        cool_values(2, root_tag="grouped00")
-        scatter_cool(2, page_after="tab_sc")
-        w1_raw[0, 1] = load_w1(0, 1, after="cool2")
-        for i in range(PACK, PLANES):
-            weigh_cool(i)
+        for i in range(5):
+            cool_values(i)
+            scatter_cool(i)
         quantise_w1(0, 0)
-        cool_values(3, square_after="w2_raw", root_tag="grouped10")
-        scatter_cool(3, page_after="grouped00")
-        w1_raw[1, 1] = load_w1(1, 1, after="cool3")
         quantise_w1(1, 0)
-        cool_values(4, square_after="cool0")
-        scatter_cool(4, page_after="grouped10")
-        w3_w = tile("w3_w", [P, PASSES, N], U32, "cool4")
-        nc.sync.dma_start(w3_w[:].bitcast(I32), w3_words.rearrange("g p c i -> p g (c i)").bitcast(I32))
-        cool_values(5, square_after="root", root_tag="grouped01")
+        cool_values(5)
         scatter_cool(5)
-
         hot_matmuls(0)
+        quantise_w1(0, 1)
+        hot_weights(0, after="tab2_w1")
         hot_feature(0)
-        hot_weights(0, after="cool5")
         scatter_hot(0)
-        w3_sc = tile("w3_sc", [P, N], U8, "feature0")
+        hot_feature(1)
+        quantise_w1(1, 1)
+        scatter_hot(1)
+        for i in (2, 3):
+            hot_feature(i)
+            scatter_hot(i)
+        cool_values(6)
+        cool_values(LAST)
+        w3_sc = tile("w3_sc", [P, N], U8, "v2_sc0")
         nc.gpsimd.memset(w3_sc[:].bitcast(I32), 0)
         load_scales_stacked(w3_sc, w3_scales)
-        quantise_w1(0, 1)
-        hot_feature(1, after="cool2")
-        scatter_hot(1)
-        quantise_w1(1, 1)
-        hot_feature(2, after="cool3")
-        scatter_hot(2)
-        hot_feature(3)
-        scatter_hot(3)
-        cool_values(6, square_after="root", root_tag="square")
-        scatter_cool(6)
-        cool_values(LAST, square_after="root", root_tag="square")
 
-        planes = tile("planes0", [P, PACK, T2], BF16, "grouped11")
+        planes = tile("planes0", [P, PACK, T2], BF16, "tab2_sc")
         round_plane(planes, 0, 0, T2)
         round_plane(planes, 1, 0, T2)
         hot_matmuls(1)
         for i in range(PACK, PLANES):
-            hot_feature(i)
-        hot_weights(1, after="feature3")
-        for i in range(PACK, LAST):
-            scatter_hot(i)
+            hot_feature(i, after="cool%d" % (i - PACK))
+        hot_weights(1, after="w2_raw")
         round_plane(planes, 2, 0, T2)
         round_plane(planes, 3, 0, T2)
-        halves = [tile("z0%d" % h, [P, PACK * HALF], BF16) for h in range(2)]
-        for h in range(2):
-            nc.scalar.copy(*weave_views(halves[h][:], planes[:, :, h * HALF : (h + 1) * HALF]))
+        z0 = tile("z0", [P, PACK * T2], BF16, "tab2_w0")
+        nc.scalar.copy(*weave_views(z0[:], planes[:]))
+        scatter_hot(4)
+        scatter_hot(5)
+        scatter_cool(6, page_after="cool1")
+        scatter_hot(6)
         scores = [bank(b, "score%d" % b) for b in range(BANKS)]
-        quantise_z((0, 0), halves[0][:], after="feature6")
-        for b in range(BANKS // 2):
+        quantise_z((0, 0), z0[:])
+        for b in range(BANKS):
             score_pass(0, b, (0, 0), (b // 2) * CHUNK)
-        scatter_cool(LAST, page_after="z00")
-        quantise_z((0, 1), halves[1][:], after="cool%d" % LAST)
-        for b in range(BANKS // 2, BANKS):
-            score_pass(0, b, (0, 1), (b // 2) * CHUNK - HALF)
+        scatter_cool(LAST, page_after="tab2_w0")
         scatter_hot(LAST)
 
-        planes = tile("planes1", [P, PACK, T2], BF16, "cool0")
+        z1 = [tile("z1%d" % q, [P, CHUNK, PACK], BF16, "wg2_repeated%d" % q) for q in range(CHUNKS)]
         for i in range(PACK, LAST):
-            round_plane(planes, i, 0, T2)
+            for q in range(CHUNKS):
+                values = pages[i][:, q * CHUNK : (q + 1) * CHUNK]
+                if i == LAST - 1:
+                    nc.scalar.activation(
+                        z1[q][:, :, 2:4], values.unsqueeze(2).to_broadcast([P, CHUNK, 2]), ACT.Identity, bias=column(c0_t, i)
+                    )
+                else:
+                    nc.scalar.activation(z1[q][:, :, i % PACK], values, ACT.Identity, bias=column(c0_t, i))
         for q in range(CHUNKS):
-            round_plane(planes, LAST, q * CHUNK, CHUNK)
-        z = tile("z1", [P, PACK * T2], BF16, "cool5")
-        for q in range(CHUNKS):
-            cols = slice(PACK * q * CHUNK, PACK * (q + 1) * CHUNK)
-            nc.vector.tensor_copy(*weave_views(z[:, cols], planes[:, :, q * CHUNK : (q + 1) * CHUNK]))
-            quantise_z((1, q), z[:, cols])
+            nc.vector.tensor_scalar_add(
+                z1[q][:, :, PACK - 1], pages[LAST][:, q * CHUNK : (q + 1) * CHUNK], column(c0_t, LAST)
+            )
+            quantise_z((1, q), z1[q][:].rearrange("p c t -> p (c t)"))
             for b in (2 * q, 2 * q + 1):
                 score_pass(1, b, (1, q), 0)
-        staged = [tile("staged%d" % s, [P, CHUNKS * S], F32, ("cool2", "cool3")[s]) for s in range(2)]
+        staged = [tile("staged%d" % s, [P, CHUNKS * S], F32, ("tab2_w1", "w2_sc_raw")[s]) for s in range(2)]
         for b in range(BANKS):
             q, lower = divmod(b, 2)
             result = slot(staged[b // CHUNKS], b % CHUNKS)

@@ -94,23 +94,21 @@ def tile_list_creep_life_weave_kernel(
 
         tab2_sc = tile("tab2_sc", [P, PASSES * TC], U8)
         w2_sc_raw = tile("w2_sc_raw", [P, PASSES * H], U8)
-        tab_sc = tile("tab_sc", [P, T], U8)
         nc.gpsimd.memset(tab2_sc[:].bitcast(I32), 0)
-        for plane in (w2_sc_raw, tab_sc):
-            nc.vector.memset(plane[:].bitcast(I32), 0)
+        nc.vector.memset(w2_sc_raw[:].bitcast(I32), 0)
         identity = tile("identity", [P, P], F32)
         make_identity(nc, identity[:])
-
         warm = tile("warm", [P, 2], F32)
         nc.vector.memset(warm[:, 0:1], 1.0)
         nc.scalar.activation(warm[:, 1:2], warm[:, 0:1], ACT.Abs_reciprocal_sqrt)
-        wg2_rows = tile("wg2_rows", [P, S], F32)
-        nc.sync.dma_start(wg2_rows[:], wg2)
+
         w2_raw = tile("w2_raw", [P, PASSES, 2 * H], U8)
         nc.sync.dma_start(w2_raw[:].bitcast(I32), w2_words.bitcast(I32).rearrange("g p c -> p g c"))
         idx2 = load_list("idx2", offs2)
+        tab2_w = [load_table("tab2_w0", tab2_words[0])]
+        wg2_rows = tile("wg2_rows", [P, S], F32)
+        nc.sync.dma_start(wg2_rows[:], wg2)
         load_scales_side_by_side(tab2_sc, tab2_scales)
-        tab2_w = [load_table("tab2_w%d" % g, tab2_words[g]) for g in range(PASSES)]
         load_scales_side_by_side(w2_sc_raw, w2_scales)
         amp_t = load_coefficients("amp_t", amp)
         c1_t = load_coefficients("c1_t", c1)
@@ -137,29 +135,6 @@ def tile_list_creep_life_weave_kernel(
             nc.vector.tensor_copy(dst[:], window.indirect(idx[:]))
             return dst
 
-        for a in range(PASSES):
-            reorder_w2_words(a)
-        idx1 = load_list("idx1", offs)
-        tab_w = [load_table("tab_w0", tab_words[0], after="w2_raw")]
-        v2_w = [gather("v2_w0", tab2_w[0][:], idx2, U32)]
-        tab_w.append(load_table("tab_w1", tab_words[1], after="tab2_w0"))
-        load_scales_stacked(tab_sc, tab_scales)
-        idx4 = load_list("idx4", offs4)
-        v2_w.append(gather("v2_w1", tab2_w[1][:], idx2, U32))
-        w1_raw = {(0, 0): load_w1(0, 0, after="tab2_w1")}
-        v2_sc = [gather("v2_sc%d" % g, tab2_sc[:, g * TC : (g + 1) * TC], idx2, U8) for g in range(PASSES)]
-        w1_raw[1, 0] = load_w1(1, 0, after="tab2_sc")
-        for a in range(PASSES):
-            reorder_w2_scales(a)
-        wg1_t = load_wg1(after="w2_sc_raw")
-        idx3 = load_list("idx3", offs3)
-        v_w = [gather("v_w%d" % g, tab_w[g][:], idx1, U32) for g in range(PASSES)]
-        v_sc = gather("v_sc", tab_sc[:], idx1, U8)
-        w1_raw[0, 1] = load_w1(0, 1, after="w2_raw")
-        w1_raw[1, 1] = load_w1(1, 1, after="tab2_w0")
-        w3_w = tile("w3_w", [P, PASSES, N], U32, "tab_sc")
-        nc.sync.dma_start(w3_w[:].bitcast(I32), w3_words.rearrange("g p c i -> p g (c i)").bitcast(I32))
-
         def column(coefficients, i):
             a, t = divmod(i, PACK)
             return coefficients[:, a, t : t + 1]
@@ -182,8 +157,33 @@ def tile_list_creep_life_weave_kernel(
                     )
             return spread
 
+        for a in range(PASSES):
+            reorder_w2_words(a)
+        tab2_w.append(load_table("tab2_w1", tab2_words[1], after="w2_raw"))
+        v2_w = [gather("v2_w0", tab2_w[0][:], idx2, U32)]
+        idx1 = load_list("idx1", offs)
+        tab_w = [load_table("tab_w0", tab_words[0], after="tab2_w0")]
+        v2_sc = [gather("v2_sc%d" % g, tab2_sc[:, g * TC : (g + 1) * TC], idx2, U8) for g in range(PASSES)]
+        tab_w.append(load_table("tab_w1", tab_words[1], after="tab2_sc"))
+        v2_w.append(gather("v2_w1", tab2_w[1][:], idx2, U32))
+        wg2_spread = spread_wg2()
+        tab_sc = tile("tab_sc", [P, T], U8, "wg2_rows")
+        nc.gpsimd.memset(tab_sc[:].bitcast(I32), 0)
+        load_scales_stacked(tab_sc, tab_scales)
+        idx4 = load_list("idx4", offs4)
+        w1_raw = {(0, 0): load_w1(0, 0, after="w2_raw")}
+        for a in range(PASSES):
+            reorder_w2_scales(a)
+        w1_raw[1, 0] = load_w1(1, 0, after="w2_sc_raw")
+        v_w = [gather("v_w%d" % g, tab_w[g][:], idx1, U32) for g in range(PASSES)]
+        v_sc = gather("v_sc", tab_sc[:], idx1, U8)
+        w1_raw[0, 1] = load_w1(0, 1, after="tab2_w0")
+        w1_raw[1, 1] = load_w1(1, 1, after="tab2_sc")
+        wg1_t = load_wg1(after="wg2_rows")
+        idx3 = load_list("idx3", offs3)
+
         cool, cool_weight, feature, weighted, hot_acc, pages = {}, {}, {}, {}, {}, {}
-        w1_w, w1_sc, z_w, z_sc = {}, {}, {}, {}
+        grouped, w1_w, w1_sc, z_w, z_sc = {}, {}, {}, {}, {}
 
         def weigh_cool(i):
             cool_weight[i] = tile("cool_weight%d" % i, [P, S], F32)
@@ -191,7 +191,7 @@ def tile_list_creep_life_weave_kernel(
 
         def cool_values(i):
             a, t = divmod(i, PACK)
-            acc = bank(t, "b%d" % i)
+            acc = bank(t if i < 6 else i - 2, "b%d" % i)
             for g in range(PASSES):
                 c = g * KP + t * P
                 nc.tensor.matmul_mx(
@@ -203,9 +203,9 @@ def tile_list_creep_life_weave_kernel(
                     start=(g == 0),
                     stop=(g == PASSES - 1),
                 )
-            square = tile("square%d" % i, [P, S], F32, "square%d" % (i % 2))
+            square = tile("square%d" % i, [P, S], F32, "square%d" % (i % 2 if i > 1 else 0))
             nc.scalar.activation(square[:], acc[:], ACT.Square)
-            root = tile("root%d" % i, [P, S], F32, "root%d" % (i % 2))
+            root = tile("root%d" % i, [P, S], F32, "root%d" % (i % 2 if i > 1 else 0))
             nc.scalar.activation(root[:], square[:], ACT.Abs_reciprocal_sqrt, bias=1.0)
             cool[i] = tile("cool%d" % i, [P, S], F32)
             nc.scalar.activation(cool[i][:], root[:], ACT.Square)
@@ -214,15 +214,17 @@ def tile_list_creep_life_weave_kernel(
             pages[i] = tile("page%d" % i, [P, T2], F32, page_after)
             nc.vector.tensor_tensor(pages[i][:].indirect(idx4[:]), cool[i][:], cool_weight[i][:], MULT)
 
-        def quantise_w1(g, a):
-            grouped = tile("grouped%d%d" % (g, a), [P, PACK * KP], BF16)
+        def round_w1(g, a):
+            grouped[g, a] = tile("grouped%d%d" % (g, a), [P, PACK * KP], BF16)
             nc.scalar.copy(
-                grouped[:].rearrange("p (t m j) -> p m t j", t=PACK, j=PACK),
+                grouped[g, a][:].rearrange("p (t m j) -> p m t j", t=PACK, j=PACK),
                 w1_raw[g, a][:].rearrange("p j (m t) -> p m t j", t=PACK),
             )
-            w1_w[g, a] = tile("w1_w%d%d" % (g, a), [P, KP], U32)
+
+        def quantise_w1(g, a, after=None):
+            w1_w[g, a] = tile("w1_w%d%d" % (g, a), [P, KP], U32, after)
             w1_sc[g, a] = tile("w1_sc%d%d" % (g, a), [P, KP], U8)
-            nc.vector.quantize_mx(out=w1_w[g, a][:].bitcast(E4M3), scales=w1_sc[g, a][:], in_=grouped[:])
+            nc.vector.quantize_mx(out=w1_w[g, a][:].bitcast(E4M3), scales=w1_sc[g, a][:], in_=grouped[g, a][:])
 
         def hot_matmuls(a):
             for t in range(PACK):
@@ -239,21 +241,18 @@ def tile_list_creep_life_weave_kernel(
                         stop=(g == PASSES - 1),
                     )
 
-        def hot_weights(a, after):
-            weighted[a] = tile("weighted%d" % a, [P, PACK * S], F32, after)
-            for t in range(PACK):
-                i = PACK * a + t
-                nc.vector.scalar_tensor_tensor(
-                    slot(weighted[a], t), hot_acc[i][:], column(c1_t, i), slot(wg1_t, t), ADD, MULT
-                )
+        def hot_weight(i, after=None):
+            weighted[i] = tile("weighted%d" % i, [P, S], F32, after)
+            nc.vector.scalar_tensor_tensor(
+                weighted[i][:], hot_acc[i][:], column(c1_t, i), slot(wg1_t, i % PACK), ADD, MULT
+            )
 
         def hot_feature(i, after=None):
             feature[i] = tile("feature%d" % i, [P, S], F32, after)
             nc.scalar.copy(feature[i][:], hot_acc[i][:])
 
         def scatter_hot(i):
-            a, t = divmod(i, PACK)
-            nc.vector.tensor_tensor(pages[i][:].indirect(idx3[:]), feature[i][:], slot(weighted[a], t), MULT)
+            nc.vector.tensor_tensor(pages[i][:].indirect(idx3[:]), feature[i][:], weighted[i][:], MULT)
 
         def round_plane(planes, i, c, width):
             nc.scalar.activation(
@@ -285,53 +284,63 @@ def tile_list_creep_life_weave_kernel(
                     stop=(a == PASSES - 1 and m == 1),
                 )
 
-        wg2_spread = spread_wg2()
-        for i in range(PLANES):
-            weigh_cool(i)
         for i in range(5):
+            weigh_cool(i)
             cool_values(i)
             scatter_cool(i)
-        quantise_w1(0, 0)
-        quantise_w1(1, 0)
+        for i in range(5, PLANES):
+            weigh_cool(i)
+        for g in range(PASSES):
+            round_w1(g, 0)
+            quantise_w1(g, 0)
         cool_values(5)
         scatter_cool(5)
         hot_matmuls(0)
-        quantise_w1(0, 1)
-        hot_weights(0, after="tab2_w1")
-        hot_feature(0)
-        scatter_hot(0)
-        hot_feature(1)
-        quantise_w1(1, 1)
-        scatter_hot(1)
-        for i in (2, 3):
+        round_w1(0, 1)
+        round_w1(1, 1)
+        for i in range(PACK):
             hot_feature(i)
-            scatter_hot(i)
+        hot_weight(0)
+        hot_weight(1)
+        scatter_hot(0)
+        quantise_w1(0, 1, after="feature0")
+        hot_weight(2, after="grouped01")
+        scatter_hot(1)
+        quantise_w1(1, 1, after="feature1")
+        hot_weight(3, after="grouped11")
+        scatter_hot(2)
         cool_values(6)
         cool_values(LAST)
+        w3_w = tile("w3_w", [P, PASSES, N], U32, "v2_w0")
+        nc.sync.dma_start(w3_w[:].bitcast(I32), w3_words.rearrange("g p c i -> p g (c i)").bitcast(I32))
         w3_sc = tile("w3_sc", [P, N], U8, "v2_sc0")
         nc.gpsimd.memset(w3_sc[:].bitcast(I32), 0)
         load_scales_stacked(w3_sc, w3_scales)
 
-        planes = tile("planes0", [P, PACK, T2], BF16, "tab2_sc")
+        planes = tile("planes0", [P, PACK, T2], BF16, "w2_sc_raw")
         round_plane(planes, 0, 0, T2)
-        round_plane(planes, 1, 0, T2)
         hot_matmuls(1)
         for i in range(PACK, PLANES):
             hot_feature(i, after="cool%d" % (i - PACK))
-        hot_weights(1, after="w2_raw")
+        round_plane(planes, 1, 0, T2)
         round_plane(planes, 2, 0, T2)
+        hot_weight(4, after="grouped01")
+        scatter_hot(3)
         round_plane(planes, 3, 0, T2)
-        z0 = tile("z0", [P, PACK * T2], BF16, "tab2_w0")
+        z0 = tile("z0", [P, PACK * T2], BF16, "w2_raw")
         nc.scalar.copy(*weave_views(z0[:], planes[:]))
+        hot_weight(5, after="grouped11")
         scatter_hot(4)
+        hot_weight(6, after="grouped01")
+        scatter_cool(6, page_after="cool0")
         scatter_hot(5)
-        scatter_cool(6, page_after="cool1")
+        scatter_cool(LAST, page_after="cool1")
         scatter_hot(6)
-        scores = [bank(b, "score%d" % b) for b in range(BANKS)]
-        quantise_z((0, 0), z0[:])
+        quantise_z((0, 0), z0[:], after="cool%d" % LAST)
+        hot_weight(LAST, after="w2_raw")
+        scores = [bank((b + PACK) % BANKS, "score%d" % b) for b in range(BANKS)]
         for b in range(BANKS):
             score_pass(0, b, (0, 0), (b // 2) * CHUNK)
-        scatter_cool(LAST, page_after="tab2_w0")
         scatter_hot(LAST)
 
         z1 = [tile("z1%d" % q, [P, CHUNK, PACK], BF16, "wg2_repeated%d" % q) for q in range(CHUNKS)]
@@ -351,7 +360,7 @@ def tile_list_creep_life_weave_kernel(
             quantise_z((1, q), z1[q][:].rearrange("p c t -> p (c t)"))
             for b in (2 * q, 2 * q + 1):
                 score_pass(1, b, (1, q), 0)
-        staged = [tile("staged%d" % s, [P, CHUNKS * S], F32, ("tab2_w1", "w2_sc_raw")[s]) for s in range(2)]
+        staged = [tile("staged%d" % s, [P, CHUNKS * S], F32, ("tab2_w0", "tab2_sc")[s]) for s in range(2)]
         for b in range(BANKS):
             q, lower = divmod(b, 2)
             result = slot(staged[b // CHUNKS], b % CHUNKS)

@@ -119,15 +119,15 @@ def tile_list_creep_life_weave_kernel(
 
         def reorder_w2_words(a):
             nc.vector.tensor_copy(
-                w2_w[a][:].bitcast(U16).rearrange("p (g t m) -> p g m t", g=PASSES, t=PACK),
-                w2_raw[:].bitcast(U16)[:, :, a * KP : (a + 1) * KP].rearrange("p g (m t) -> p g m t", t=PACK),
+                w2_w[a][:].bitcast(U16).rearrange("p (g t m) -> p g t m", g=PASSES, t=PACK),
+                w2_raw[:].bitcast(U16)[:, :, a * KP : (a + 1) * KP].rearrange("p g (m t) -> p g t m", t=PACK),
             )
 
         def reorder_w2_scales(a):
             src = w2_sc_raw[:].rearrange("p (g c) -> p g c", g=PASSES)[:, :, a * KP : (a + 1) * KP]
             nc.vector.tensor_copy(
-                w2_sc[a][:].rearrange("p (g t m) -> p g m t", g=PASSES, t=PACK),
-                src.rearrange("p g (m t) -> p g m t", t=PACK),
+                w2_sc[a][:].rearrange("p (g t m) -> p g t m", g=PASSES, t=PACK),
+                src.rearrange("p g (m t) -> p g t m", t=PACK),
             )
 
         def gather(name, window, idx, dtype):
@@ -183,7 +183,7 @@ def tile_list_creep_life_weave_kernel(
         idx3 = load_list("idx3", offs3)
 
         cool, cool_weight, feature, weighted, hot_acc, pages = {}, {}, {}, {}, {}, {}
-        grouped, w1_w, w1_sc, z_w, z_sc = {}, {}, {}, {}, {}
+        hot, shifted, grouped, w1_w, w1_sc, z_w, z_sc = {}, {}, {}, {}, {}, {}, {}
 
         def weigh_cool(i):
             cool_weight[i] = tile("cool_weight%d" % i, [P, S], F32)
@@ -191,7 +191,7 @@ def tile_list_creep_life_weave_kernel(
 
         def cool_values(i):
             a, t = divmod(i, PACK)
-            acc = bank(t if i < 6 else i - 2, "b%d" % i)
+            acc = bank(t, "b%d" % i)
             for g in range(PASSES):
                 c = g * KP + t * P
                 nc.tensor.matmul_mx(
@@ -217,8 +217,8 @@ def tile_list_creep_life_weave_kernel(
         def round_w1(g, a):
             grouped[g, a] = tile("grouped%d%d" % (g, a), [P, PACK * KP], BF16)
             nc.scalar.copy(
-                grouped[g, a][:].rearrange("p (t m j) -> p m t j", t=PACK, j=PACK),
-                w1_raw[g, a][:].rearrange("p j (m t) -> p m t j", t=PACK),
+                grouped[g, a][:].rearrange("p (t m j) -> p m j t", t=PACK, j=PACK),
+                w1_raw[g, a][:].rearrange("p j (m t) -> p m j t", t=PACK),
             )
 
         def quantise_w1(g, a, after=None):
@@ -241,18 +241,28 @@ def tile_list_creep_life_weave_kernel(
                         stop=(g == PASSES - 1),
                     )
 
-        def hot_weight(i, after=None):
-            weighted[i] = tile("weighted%d" % i, [P, S], F32, after)
+        def hot_weight(i, dst):
+            weighted[i] = dst
             nc.vector.scalar_tensor_tensor(
-                weighted[i][:], hot_acc[i][:], column(c1_t, i), slot(wg1_t, i % PACK), ADD, MULT
+                weighted[i], hot_acc[i][:], column(c1_t, i), slot(wg1_t, i % PACK), ADD, MULT
             )
 
         def hot_feature(i, after=None):
             feature[i] = tile("feature%d" % i, [P, S], F32, after)
             nc.scalar.copy(feature[i][:], hot_acc[i][:])
 
+        def hot_shifted(i, after=None):
+            shifted[i] = tile("shifted%d" % i, [P, S], F32, after)
+            nc.scalar.activation(shifted[i][:], hot_acc[i][:], ACT.Identity, bias=column(c1_t, i))
+
+        def hot_products(i, after=None):
+            weighted[i] = tile("weighted%d" % i, [P, S], F32, after)
+            nc.gpsimd.tensor_tensor(weighted[i][:], shifted[i][:], slot(wg1_t, i % PACK), MULT)
+            hot[i] = tile("hot%d" % i, [P, S], F32)
+            nc.gpsimd.tensor_tensor(hot[i][:], weighted[i][:], feature[i][:], MULT)
+
         def scatter_hot(i):
-            nc.vector.tensor_tensor(pages[i][:].indirect(idx3[:]), feature[i][:], weighted[i][:], MULT)
+            nc.vector.tensor_copy(pages[i][:].indirect(idx3[:]), hot[i][:])
 
         def round_plane(planes, i, c, width):
             nc.scalar.activation(
@@ -284,32 +294,38 @@ def tile_list_creep_life_weave_kernel(
                     stop=(a == PASSES - 1 and m == 1),
                 )
 
-        for i in range(5):
+        for i in range(PACK):
             weigh_cool(i)
+        cool_values(0)
+        scatter_cool(0)
+        for i in range(PACK, PLANES):
+            weigh_cool(i)
+        for i in range(1, 6):
             cool_values(i)
             scatter_cool(i)
-        for i in range(5, PLANES):
-            weigh_cool(i)
         for g in range(PASSES):
             round_w1(g, 0)
             quantise_w1(g, 0)
-        cool_values(5)
-        scatter_cool(5)
-        hot_matmuls(0)
-        round_w1(0, 1)
-        round_w1(1, 1)
-        for i in range(PACK):
-            hot_feature(i)
-        hot_weight(0)
-        hot_weight(1)
-        scatter_hot(0)
-        quantise_w1(0, 1, after="feature0")
-        hot_weight(2, after="grouped01")
-        scatter_hot(1)
-        quantise_w1(1, 1, after="feature1")
-        hot_weight(3, after="grouped11")
-        scatter_hot(2)
         cool_values(6)
+        scatter_cool(6)
+        hot_matmuls(0)
+        first = tile("weighted0", [P, S], F32, "cool6")
+        hot_weight(0, first[:])
+        round_w1(0, 1)
+        quantise_w1(0, 1)
+        hot[0] = tile("hot0", [P, S], F32)
+        nc.vector.tensor_tensor(hot[0][:], weighted[0], hot_acc[0][:], MULT)
+        scatter_hot(0)
+        round_w1(1, 1)
+        quantise_w1(1, 1)
+        for i in range(1, PACK):
+            hot_feature(i)
+            hot_shifted(i)
+        hot_products(1, after="cool_weight6")
+        scatter_hot(1)
+        hot_products(2, after="grouped11")
+        scatter_hot(2)
+        hot_products(3)
         cool_values(LAST)
         w3_w = tile("w3_w", [P, PASSES, N], U32, "v2_w0")
         nc.sync.dma_start(w3_w[:].bitcast(I32), w3_words.rearrange("g p c i -> p g (c i)").bitcast(I32))
@@ -318,26 +334,21 @@ def tile_list_creep_life_weave_kernel(
         load_scales_stacked(w3_sc, w3_scales)
 
         planes = tile("planes0", [P, PACK, T2], BF16, "w2_sc_raw")
-        round_plane(planes, 0, 0, T2)
         hot_matmuls(1)
         for i in range(PACK, PLANES):
             hot_feature(i, after="cool%d" % (i - PACK))
-        round_plane(planes, 1, 0, T2)
-        round_plane(planes, 2, 0, T2)
-        hot_weight(4, after="grouped01")
+            hot_shifted(i, after="cool_weight%d" % (i - PACK))
+            hot_products(i)
+        for i in range(3):
+            round_plane(planes, i, 0, T2)
         scatter_hot(3)
         round_plane(planes, 3, 0, T2)
         z0 = tile("z0", [P, PACK * T2], BF16, "w2_raw")
         nc.scalar.copy(*weave_views(z0[:], planes[:]))
-        hot_weight(5, after="grouped11")
-        scatter_hot(4)
-        hot_weight(6, after="grouped01")
-        scatter_cool(6, page_after="cool0")
-        scatter_hot(5)
-        scatter_cool(LAST, page_after="cool1")
-        scatter_hot(6)
-        quantise_z((0, 0), z0[:], after="cool%d" % LAST)
-        hot_weight(LAST, after="w2_raw")
+        for i in (4, 5, 6):
+            scatter_hot(i)
+        quantise_z((0, 0), z0[:], after="hot5")
+        scatter_cool(LAST, page_after="w2_raw")
         scores = [bank((b + PACK) % BANKS, "score%d" % b) for b in range(BANKS)]
         for b in range(BANKS):
             score_pass(0, b, (0, 0), (b // 2) * CHUNK)

@@ -86,29 +86,36 @@ def tile_list_creep_life_weave_kernel(
                 nc.sync.dma_start(dst[QUAD * q : QUAD * (q + 1), :], rows)
             return dst
 
+        def load_w2(a, after=None):
+            dst = tile("w2_raw%d" % a, [P, PASSES, 2 * KP], U8, after)
+            src = w2_words[:, :, 2 * a * KP : 2 * (a + 1) * KP]
+            nc.sync.dma_start(dst[:].bitcast(I32), src.bitcast(I32).rearrange("g p c -> p g c"))
+            return dst
+
         def load_w1(g, a, after):
             dst = tile("w1_raw%d%d" % (g, a), [P, PACK, KP], F32, after)
             src = w1[g * KP : (g + 1) * KP, a * KP : (a + 1) * KP]
             nc.sync.dma_start(dst[:], src.rearrange("(p j) c -> p j c", j=PACK))
             return dst
 
-        tab2_sc = tile("tab2_sc", [P, PASSES * TC], U8)
+        tab2_sc = tile("tab2_sc", [P, TC], U8)
+        v2_sc_second = tile("v2_sc1", [P, S], U8)
         w2_sc_raw = tile("w2_sc_raw", [P, PASSES * H], U8)
         nc.gpsimd.memset(tab2_sc[:].bitcast(I32), 0)
         nc.vector.memset(w2_sc_raw[:].bitcast(I32), 0)
+        nc.vector.memset(v2_sc_second[:].bitcast(I32), 0)
         identity = tile("identity", [P, P], F32)
         make_identity(nc, identity[:])
         warm = tile("warm", [P, 2], F32)
         nc.vector.memset(warm[:, 0:1], 1.0)
         nc.scalar.activation(warm[:, 1:2], warm[:, 0:1], ACT.Abs_reciprocal_sqrt)
 
-        w2_raw = tile("w2_raw", [P, PASSES, 2 * H], U8)
-        nc.sync.dma_start(w2_raw[:].bitcast(I32), w2_words.bitcast(I32).rearrange("g p c -> p g c"))
+        w2_raw = [load_w2(0)]
         idx2 = load_list("idx2", offs2)
+        load_scales_stacked(tab2_sc, tab2_scales)
         tab2_w = [load_table("tab2_w0", tab2_words[0])]
         wg2_rows = tile("wg2_rows", [P, S], F32)
         nc.sync.dma_start(wg2_rows[:], wg2)
-        load_scales_side_by_side(tab2_sc, tab2_scales)
         load_scales_side_by_side(w2_sc_raw, w2_scales)
         amp_t = load_coefficients("amp_t", amp)
         c1_t = load_coefficients("c1_t", c1)
@@ -120,7 +127,7 @@ def tile_list_creep_life_weave_kernel(
         def reorder_w2_words(a):
             nc.vector.tensor_copy(
                 w2_w[a][:].bitcast(U16).rearrange("p (g t m) -> p g t m", g=PASSES, t=PACK),
-                w2_raw[:].bitcast(U16)[:, :, a * KP : (a + 1) * KP].rearrange("p g (m t) -> p g t m", t=PACK),
+                w2_raw[a][:].bitcast(U16).rearrange("p g (m t) -> p g t m", t=PACK),
             )
 
         def reorder_w2_scales(a):
@@ -147,40 +154,40 @@ def tile_list_creep_life_weave_kernel(
             for s in range(S // P):
                 nc.tensor.transpose(turned[:, s * P : (s + 1) * P], wg2_rows[:, s * P : (s + 1) * P], identity[:])
             spread = [bank(PACK + t, "wg2_spread%d" % t) for t in range(PACK)]
-            for s in range(S // P):
-                repeated = tile("wg2_repeated%d" % s, [P, PACK, QUADS, QUAD], F32)
-                rows = turned[:, s * P : (s + 1) * P].rearrange("p (u t) -> p t u", t=PACK)
-                nc.scalar.copy(repeated[:], rows.unsqueeze(2).to_broadcast([P, PACK, QUADS, QUAD]))
-                for t in range(PACK):
+            for t in range(PACK):
+                repeated = tile("wg2_repeated%d" % t, [P, S // P, QUADS, QUAD], F32)
+                rows = turned[:].rearrange("p (s u t) -> p t s u", t=PACK, u=QUAD)[:, t]
+                nc.scalar.copy(repeated[:], rows.unsqueeze(2).to_broadcast([P, S // P, QUADS, QUAD]))
+                for s in range(S // P):
                     nc.tensor.transpose(
-                        spread[t][:, s * P : (s + 1) * P], repeated[:, t].rearrange("p q u -> p (q u)"), identity[:]
+                        spread[t][:, s * P : (s + 1) * P], repeated[:, s].rearrange("p q u -> p (q u)"), identity[:]
                     )
             return spread
 
-        for a in range(PASSES):
-            reorder_w2_words(a)
-        tab2_w.append(load_table("tab2_w1", tab2_words[1], after="w2_raw"))
+        reorder_w2_words(0)
+        tab2_w.append(load_table("tab2_w1", tab2_words[1], after="w2_raw0"))
+        v2_sc = [gather("v2_sc0", tab2_sc[:], idx2, U8), v2_sc_second]
+        for q in range(QUADS):
+            nc.sync.dma_start(
+                v2_sc[1][QUAD * q : QUAD * q + SCALE_ROWS, :].bitcast(I32),
+                v2_sc[0][QUAD * q + SCALE_ROWS : QUAD * q + PASSES * SCALE_ROWS, :].bitcast(I32),
+            )
         v2_w = [gather("v2_w0", tab2_w[0][:], idx2, U32)]
+        w2_raw.append(load_w2(1, after="tab2_w0"))
         idx1 = load_list("idx1", offs)
-        tab_w = [load_table("tab_w0", tab_words[0], after="tab2_w0")]
-        v2_sc = [gather("v2_sc%d" % g, tab2_sc[:, g * TC : (g + 1) * TC], idx2, U8) for g in range(PASSES)]
-        tab_w.append(load_table("tab_w1", tab_words[1], after="tab2_sc"))
+        tab_w = [load_table("tab_w0", tab_words[0], after="tab2_sc")]
         v2_w.append(gather("v2_w1", tab2_w[1][:], idx2, U32))
         wg2_spread = spread_wg2()
         tab_sc = tile("tab_sc", [P, T], U8, "wg2_rows")
         nc.gpsimd.memset(tab_sc[:].bitcast(I32), 0)
         load_scales_stacked(tab_sc, tab_scales)
         idx4 = load_list("idx4", offs4)
-        w1_raw = {(0, 0): load_w1(0, 0, after="w2_raw")}
-        for a in range(PASSES):
-            reorder_w2_scales(a)
-        w1_raw[1, 0] = load_w1(1, 0, after="w2_sc_raw")
-        v_w = [gather("v_w%d" % g, tab_w[g][:], idx1, U32) for g in range(PASSES)]
+        reorder_w2_scales(0)
+        reorder_w2_words(1)
+        reorder_w2_scales(1)
+        w1_raw = {(0, 0): load_w1(0, 0, after="w2_raw0")}
+        v_w = [gather("v_w0", tab_w[0][:], idx1, U32)]
         v_sc = gather("v_sc", tab_sc[:], idx1, U8)
-        w1_raw[0, 1] = load_w1(0, 1, after="tab2_w0")
-        w1_raw[1, 1] = load_w1(1, 1, after="tab2_sc")
-        wg1_t = load_wg1(after="wg2_rows")
-        idx3 = load_list("idx3", offs3)
 
         cool, cool_weight, feature, weighted, hot_acc, pages = {}, {}, {}, {}, {}, {}
         hot, shifted, grouped, w1_w, w1_sc, z_w, z_sc = {}, {}, {}, {}, {}, {}, {}
@@ -189,7 +196,7 @@ def tile_list_creep_life_weave_kernel(
             cool_weight[i] = tile("cool_weight%d" % i, [P, S], F32)
             nc.scalar.activation(cool_weight[i][:], wg2_spread[i % PACK][:], ACT.Copy, scale=column(amp_t, i))
 
-        def cool_values(i):
+        def cool_values(i, parts=1):
             a, t = divmod(i, PACK)
             acc = bank(t, "b%d" % i)
             for g in range(PASSES):
@@ -204,11 +211,15 @@ def tile_list_creep_life_weave_kernel(
                     stop=(g == PASSES - 1),
                 )
             square = tile("square%d" % i, [P, S], F32, "square%d" % (i % 2 if i > 1 else 0))
-            nc.scalar.activation(square[:], acc[:], ACT.Square)
             root = tile("root%d" % i, [P, S], F32, "root%d" % (i % 2 if i > 1 else 0))
-            nc.scalar.activation(root[:], square[:], ACT.Abs_reciprocal_sqrt, bias=1.0)
             cool[i] = tile("cool%d" % i, [P, S], F32)
-            nc.scalar.activation(cool[i][:], root[:], ACT.Square)
+            cuts = [slice(h * S // parts, (h + 1) * S // parts) for h in range(parts)]
+            for cols in cuts:
+                nc.scalar.activation(square[:, cols], acc[:, cols], ACT.Square)
+            for cols in cuts:
+                nc.scalar.activation(root[:, cols], square[:, cols], ACT.Abs_reciprocal_sqrt, bias=1.0)
+            for cols in cuts:
+                nc.scalar.activation(cool[i][:, cols], root[:, cols], ACT.Square)
 
         def scatter_cool(i, page_after=None):
             pages[i] = tile("page%d" % i, [P, T2], F32, page_after)
@@ -294,15 +305,22 @@ def tile_list_creep_life_weave_kernel(
                     stop=(a == PASSES - 1 and m == 1),
                 )
 
-        for i in range(PACK):
-            weigh_cool(i)
-        cool_values(0)
+        weigh_cool(0)
+        cool_values(0, parts=2)
         scatter_cool(0)
-        for i in range(PACK, PLANES):
-            weigh_cool(i)
+        tab_w.append(load_table("tab_w1", tab_words[1], after="tab2_w0"))
+        v_w.append(gather("v_w1", tab_w[1][:], idx1, U32))
+        w1_raw[1, 0] = load_w1(1, 0, after="w2_sc_raw")
+        w1_raw[0, 1] = load_w1(0, 1, after="tab2_sc")
+        w1_raw[1, 1] = load_w1(1, 1, after="cool0")
+        wg1_t = load_wg1(after="wg2_rows")
+        idx3 = load_list("idx3", offs3)
         for i in range(1, 6):
+            weigh_cool(i)
             cool_values(i)
             scatter_cool(i)
+        for i in range(6, PLANES):
+            weigh_cool(i)
         for g in range(PASSES):
             round_w1(g, 0)
             quantise_w1(g, 0)
@@ -343,12 +361,12 @@ def tile_list_creep_life_weave_kernel(
             round_plane(planes, i, 0, T2)
         scatter_hot(3)
         round_plane(planes, 3, 0, T2)
-        z0 = tile("z0", [P, PACK * T2], BF16, "w2_raw")
+        z0 = tile("z0", [P, PACK * T2], BF16, "w2_raw0")
         nc.scalar.copy(*weave_views(z0[:], planes[:]))
         for i in (4, 5, 6):
             scatter_hot(i)
         quantise_z((0, 0), z0[:], after="hot5")
-        scatter_cool(LAST, page_after="w2_raw")
+        scatter_cool(LAST, page_after="w2_raw0")
         scores = [bank((b + PACK) % BANKS, "score%d" % b) for b in range(BANKS)]
         for b in range(BANKS):
             score_pass(0, b, (0, 0), (b // 2) * CHUNK)
@@ -375,9 +393,15 @@ def tile_list_creep_life_weave_kernel(
         for b in range(BANKS):
             q, lower = divmod(b, 2)
             result = slot(staged[b // CHUNKS], b % CHUNKS)
+            rows = out[2 * lower * P : 2 * (lower + 1) * P, q * CHUNK : (q + 1) * CHUNK]
+            if b == 0:
+                for m in range(2):
+                    part = slice(m * CHUNK, (m + 1) * CHUNK)
+                    nc.scalar.copy(result[:, part], scores[b][:, part])
+                    nc.sync.dma_start(rows[m * P : (m + 1) * P], result[:, part])
+                continue
             if q >= CHUNKS // 2 and lower == 1:
                 nc.vector.tensor_copy(result, scores[b][:])
             else:
                 nc.scalar.copy(result, scores[b][:])
-            rows = out[2 * lower * P : 2 * (lower + 1) * P, q * CHUNK : (q + 1) * CHUNK]
             nc.sync.dma_start(rows.rearrange("(m p) c -> p m c", p=P), result.rearrange("p (m c) -> p m c", m=2))

@@ -67,75 +67,85 @@ def tile_list_creep_life_weave_kernel(
                     src[:, SCALE_ROWS * q : SCALE_ROWS * (q + 1), :].bitcast(I32).rearrange("g r c -> r g c"),
                 )
 
-        def load_scales_stacked(dst, src):
+        def load_scales_stacked(dst, src, queue):
             for q in range(QUADS):
-                nc.sync.dma_start(
+                queue.dma_start(
                     dst[QUAD * q : QUAD * q + PASSES * SCALE_ROWS, :].bitcast(I32),
                     src[:, SCALE_ROWS * q : SCALE_ROWS * (q + 1), :].bitcast(I32),
                 )
 
-        def load_coefficients(name, src):
-            dst = tile(name, [P, PASSES, PACK], F32)
-            nc.gpsimd.dma_start(dst[:], src.rearrange("(a p t) -> p a t", a=PASSES, t=PACK))
+        def load_coefficients(name, src, a, queue):
+            dst = tile("%s%d" % (name, a), [P, PACK], F32)
+            if a == 0:
+                with nc.allow_non_contiguous_dma(reason="one value a partition and plane"):
+                    queue.dma_start(dst[:], src[0:KP].rearrange("(t p) -> p t", t=PACK))
+            else:
+                queue.dma_start(dst[:], src[KP:H].rearrange("(p t) -> p t", t=PACK))
             return dst
 
-        def load_wg1(after):
-            dst = tile("wg1_t", [P, PACK * S], F32, after)
-            rows = wg1.rearrange("(u t) j -> u (t j)", t=PACK)
+        def load_rows(name, src, after=None):
+            dst = tile(name, [P, S], F32, after)
+            nc.sync.dma_start(dst[:], src)
+            return dst
+
+        def load_spread(name, src, after=None):
+            dst = tile(name, [P, PACK * S], F32, after)
+            rows = src.rearrange("(u t) j -> u (t j)", t=PACK)
             for q in range(QUADS):
                 nc.sync.dma_start(dst[QUAD * q : QUAD * (q + 1), :], rows)
             return dst
 
-        def load_w2(a, after=None):
-            dst = tile("w2_raw%d" % a, [P, PASSES, 2 * KP], U8, after)
+        def load_w2(a):
+            dst = tile("w2_w%d" % a, [P, PASSES, 2 * KP], U8)
             src = w2_words[:, :, 2 * a * KP : 2 * (a + 1) * KP]
             nc.sync.dma_start(dst[:].bitcast(I32), src.bitcast(I32).rearrange("g p c -> p g c"))
             return dst
 
-        def load_w1(g, a, after):
-            dst = tile("w1_raw%d%d" % (g, a), [P, PACK, KP], F32, after)
+        def load_w1(g, a):
+            dst = tile("w1_raw%d%d" % (g, a), [P, PACK, KP], F32)
             src = w1[g * KP : (g + 1) * KP, a * KP : (a + 1) * KP]
             nc.sync.dma_start(dst[:], src.rearrange("(p j) c -> p j c", j=PACK))
             return dst
 
-        tab2_sc = tile("tab2_sc", [P, TC], U8)
-        v2_sc_second = tile("v2_sc1", [P, S], U8)
-        w2_sc_raw = tile("w2_sc_raw", [P, PASSES * H], U8)
-        nc.gpsimd.memset(tab2_sc[:].bitcast(I32), 0)
-        nc.vector.memset(w2_sc_raw[:].bitcast(I32), 0)
-        nc.vector.memset(v2_sc_second[:].bitcast(I32), 0)
-        identity = tile("identity", [P, P], F32)
-        make_identity(nc, identity[:])
+        tab2_sc = tile("tab2_sc", [P, PASSES * TC], U8)
+        w2_sc = tile("w2_sc", [P, PASSES * H], U8)
+        tab_sc = tile("tab_sc", [P, T], U8)
+        w3_sc = tile("w3_sc", [P, N], U8)
+        amp_t = [load_coefficients("amp_t", amp, 0, nc.gpsimd)]
+        nc.vector.memset(tab2_sc[:].bitcast(I32), 0)
+        nc.vector.memset(tab_sc[:].bitcast(I32), 0)
+        nc.vector.memset(w2_sc[:].bitcast(I32), 0)
+        nc.vector.memset(w3_sc[:].bitcast(I32), 0)
         warm = tile("warm", [P, 2], F32)
         nc.vector.memset(warm[:, 0:1], 1.0)
         nc.scalar.activation(warm[:, 1:2], warm[:, 0:1], ACT.Abs_reciprocal_sqrt)
 
-        w2_raw = [load_w2(0)]
         idx2 = load_list("idx2", offs2)
-        load_scales_stacked(tab2_sc, tab2_scales)
-        tab2_w = [load_table("tab2_w0", tab2_words[0])]
-        wg2_rows = tile("wg2_rows", [P, S], F32)
-        nc.sync.dma_start(wg2_rows[:], wg2)
-        load_scales_side_by_side(w2_sc_raw, w2_scales)
-        amp_t = load_coefficients("amp_t", amp)
-        c1_t = load_coefficients("c1_t", c1)
-        c0_t = load_coefficients("c0_t", c0)
-
-        w2_w = [tile("w2_w%d" % a, [P, PASSES * 2 * KP], U8) for a in range(PASSES)]
-        w2_sc = [tile("w2_sc%d" % a, [P, PASSES * KP], U8) for a in range(PASSES)]
-
-        def reorder_w2_words(a):
-            nc.vector.tensor_copy(
-                w2_w[a][:].bitcast(U16).rearrange("p (g t m) -> p g t m", g=PASSES, t=PACK),
-                w2_raw[a][:].bitcast(U16).rearrange("p g (m t) -> p g t m", t=PACK),
-            )
-
-        def reorder_w2_scales(a):
-            src = w2_sc_raw[:].rearrange("p (g c) -> p g c", g=PASSES)[:, :, a * KP : (a + 1) * KP]
-            nc.vector.tensor_copy(
-                w2_sc[a][:].rearrange("p (g t m) -> p g t m", g=PASSES, t=PACK),
-                src.rearrange("p g (m t) -> p g t m", t=PACK),
-            )
+        load_scales_side_by_side(tab2_sc, tab2_scales)
+        tab2_w = [load_table("tab2_w%d" % g, tab2_words[g]) for g in range(PASSES)]
+        wg2_rows = load_rows("wg2_rows", wg2)
+        w2_w = [load_w2(0)]
+        load_scales_side_by_side(w2_sc, w2_scales)
+        identity = tile("identity", [P, P], F32)
+        make_identity(nc, identity[:])
+        tab_w = [load_table("tab_w0", tab_words[0])]
+        idx1 = load_list("idx1", offs)
+        load_scales_stacked(tab_sc, tab_scales, nc.sync)
+        tab_w.append(load_table("tab_w1", tab_words[1]))
+        idx4 = load_list("idx4", offs4)
+        w2_w.append(load_w2(1))
+        w1_raw = {}
+        for g in range(PASSES):
+            w1_raw[g, 0] = load_w1(g, 0)
+        wg2_spread = load_spread("wg2_spread", wg2)
+        amp_t.append(load_coefficients("amp_t", amp, 1, nc.sync))
+        for g in range(PASSES):
+            w1_raw[g, 1] = load_w1(g, 1)
+        c1_t = [load_coefficients("c1_t", c1, a, nc.sync) for a in range(PASSES)]
+        wg1_rows = load_rows("wg1_rows", wg1)
+        idx3 = load_list("idx3", offs3)
+        c0_t = [load_coefficients("c0_t", c0, a, nc.sync) for a in range(PASSES)]
+        load_scales_stacked(w3_sc, w3_scales, nc.sync)
 
         def gather(name, window, idx, dtype):
             dst = tile(name, [P, S], dtype)
@@ -144,147 +154,170 @@ def tile_list_creep_life_weave_kernel(
 
         def column(coefficients, i):
             a, t = divmod(i, PACK)
-            return coefficients[:, a, t : t + 1]
+            return coefficients[a][:, t : t + 1]
 
         def slot(wide, t):
             return wide[:, t * S : (t + 1) * S]
 
-        def spread_wg2():
-            turned = bank(PACK - 1, "wg2_turned")
-            for s in range(S // P):
-                nc.tensor.transpose(turned[:, s * P : (s + 1) * P], wg2_rows[:, s * P : (s + 1) * P], identity[:])
-            spread = [bank(PACK + t, "wg2_spread%d" % t) for t in range(PACK)]
-            for t in range(PACK):
-                repeated = tile("wg2_repeated%d" % t, [P, S // P, QUADS, QUAD], F32)
-                rows = turned[:].rearrange("p (s u t) -> p t s u", t=PACK, u=QUAD)[:, t]
-                nc.scalar.copy(repeated[:], rows.unsqueeze(2).to_broadcast([P, S // P, QUADS, QUAD]))
-                for s in range(S // P):
-                    nc.tensor.transpose(
-                        spread[t][:, s * P : (s + 1) * P], repeated[:, s].rearrange("p q u -> p (q u)"), identity[:]
-                    )
-            return spread
-
-        reorder_w2_words(0)
-        tab2_w.append(load_table("tab2_w1", tab2_words[1], after="w2_raw0"))
-        v2_sc = [gather("v2_sc0", tab2_sc[:], idx2, U8), v2_sc_second]
-        for q in range(QUADS):
-            nc.sync.dma_start(
-                v2_sc[1][QUAD * q : QUAD * q + SCALE_ROWS, :].bitcast(I32),
-                v2_sc[0][QUAD * q + SCALE_ROWS : QUAD * q + PASSES * SCALE_ROWS, :].bitcast(I32),
-            )
-        v2_w = [gather("v2_w0", tab2_w[0][:], idx2, U32)]
-        w2_raw.append(load_w2(1, after="tab2_w0"))
-        idx1 = load_list("idx1", offs)
-        tab_w = [load_table("tab_w0", tab_words[0], after="tab2_sc")]
-        v2_w.append(gather("v2_w1", tab2_w[1][:], idx2, U32))
-        wg2_spread = spread_wg2()
-        tab_sc = tile("tab_sc", [P, T], U8, "wg2_rows")
-        nc.gpsimd.memset(tab_sc[:].bitcast(I32), 0)
-        load_scales_stacked(tab_sc, tab_scales)
-        idx4 = load_list("idx4", offs4)
-        reorder_w2_scales(0)
-        reorder_w2_words(1)
-        reorder_w2_scales(1)
-        w1_raw = {(0, 0): load_w1(0, 0, after="w2_raw0")}
+        v2_sc = [gather("v2_sc%d" % g, tab2_sc[:, g * TC : (g + 1) * TC], idx2, U8) for g in range(PASSES)]
+        v2_w = [gather("v2_w%d" % g, tab2_w[g][:], idx2, U32) for g in range(PASSES)]
         v_w = [gather("v_w0", tab_w[0][:], idx1, U32)]
         v_sc = gather("v_sc", tab_sc[:], idx1, U8)
+        v_w.append(gather("v_w1", tab_w[1][:], idx1, U32))
 
-        cool, cool_weight, feature, weighted, hot_acc, pages = {}, {}, {}, {}, {}, {}
-        hot, shifted, grouped, w1_w, w1_sc, z_w, z_sc = {}, {}, {}, {}, {}, {}, {}
+        cool, pages, hot, hot_acc, feature, shifted = {}, {}, {}, {}, {}, {}
+        grouped, w1_w, w1_sc, z_w, z_sc, squares, roots = {}, {}, {}, {}, {}, {}, {}
 
-        def weigh_cool(i):
-            cool_weight[i] = tile("cool_weight%d" % i, [P, S], F32)
-            nc.scalar.activation(cool_weight[i][:], wg2_spread[i % PACK][:], ACT.Copy, scale=column(amp_t, i))
+        def reciprocal(acc, k, dst_view, src_view, cols=slice(0, S)):
+            if cols.start == 0:
+                squares[k] = tile("square%d" % k, [P, S], F32, "root0" if k == 1 else ("wg2_rows", "amp_t0")[k % 2])
+                roots[k] = tile("root%d" % k, [P, S], F32, "root%d" % (k % 2))
+            nc.scalar.activation(squares[k][:, cols], acc, ACT.Square)
+            nc.scalar.activation(roots[k][:, cols], squares[k][:, cols], ACT.Abs_reciprocal_sqrt, bias=1.0)
+            nc.scalar.activation(dst_view, src_view(roots[k][:, cols]), ACT.Square)
 
-        def cool_values(i, parts=1):
-            a, t = divmod(i, PACK)
-            acc = bank(t, "b%d" % i)
-            for g in range(PASSES):
-                c = g * KP + t * P
-                nc.tensor.matmul_mx(
-                    out=acc[:],
-                    lhsT=w2_w[a][:, 2 * c : 2 * (c + P)].bitcast(E2M1),
-                    lhsT_scale=w2_sc[a][:, c : c + P],
-                    rhs=v2_w[g][:].bitcast(E4M3),
-                    rhs_scale=v2_sc[g][:],
-                    start=(g == 0),
-                    stop=(g == PASSES - 1),
-                )
-            square = tile("square%d" % i, [P, S], F32, "square%d" % (i % 2 if i > 1 else 0))
-            root = tile("root%d" % i, [P, S], F32, "root%d" % (i % 2 if i > 1 else 0))
+        def weigh_rows(i):
             cool[i] = tile("cool%d" % i, [P, S], F32)
-            cuts = [slice(h * S // parts, (h + 1) * S // parts) for h in range(parts)]
-            for cols in cuts:
-                nc.scalar.activation(square[:, cols], acc[:, cols], ACT.Square)
-            for cols in cuts:
-                nc.scalar.activation(root[:, cols], square[:, cols], ACT.Abs_reciprocal_sqrt, bias=1.0)
-            for cols in cuts:
-                nc.scalar.activation(cool[i][:, cols], root[:, cols], ACT.Square)
+            nc.scalar.activation(cool[i][:], wg2_rows[:], ACT.Copy, scale=column(amp_t, i))
 
-        def scatter_cool(i, page_after=None):
-            pages[i] = tile("page%d" % i, [P, T2], F32, page_after)
-            nc.vector.tensor_tensor(pages[i][:].indirect(idx4[:]), cool[i][:], cool_weight[i][:], MULT)
-
-        def round_w1(g, a):
-            grouped[g, a] = tile("grouped%d%d" % (g, a), [P, PACK * KP], BF16)
-            nc.scalar.copy(
-                grouped[g, a][:].rearrange("p (t m j) -> p m j t", t=PACK, j=PACK),
-                w1_raw[g, a][:].rearrange("p j (m t) -> p m j t", t=PACK),
-            )
-
-        def quantise_w1(g, a, after=None):
-            w1_w[g, a] = tile("w1_w%d%d" % (g, a), [P, KP], U32, after)
-            w1_sc[g, a] = tile("w1_sc%d%d" % (g, a), [P, KP], U8)
-            nc.vector.quantize_mx(out=w1_w[g, a][:].bitcast(E4M3), scales=w1_sc[g, a][:], in_=grouped[g, a][:])
-
-        def hot_matmuls(a):
-            for t in range(PACK):
-                i = PACK * a + t
-                hot_acc[i] = bank((i + PACK) % PLANES, "a%d" % i)
-                for g in range(PASSES):
+        def cool_direct(i, parts):
+            response = tile("response%d" % i, [P, S], F32)
+            width = S // parts
+            cuts = [slice(h * width, (h + 1) * width) for h in range(parts)]
+            accs = [bank(i + PACK * h, "b%d%d" % (i, h)) for h in range(parts)]
+            for g in range(PASSES):
+                for acc, cols in zip(accs, cuts):
                     nc.tensor.matmul_mx(
-                        out=hot_acc[i][:],
-                        lhsT=w1_w[g, a][:, t * P : (t + 1) * P].bitcast(E4M3),
-                        lhsT_scale=w1_sc[g, a][:, t * P : (t + 1) * P],
-                        rhs=v_w[g][:].bitcast(E4M3),
-                        rhs_scale=v_sc[SCALE_ROWS * g : P, :],
+                        out=acc[:, 0:width],
+                        lhsT=w2_w[0][:, g, 2 * i * P : 2 * (i + 1) * P].bitcast(E2M1),
+                        lhsT_scale=w2_sc[:, g * H + i * P : g * H + (i + 1) * P],
+                        rhs=v2_w[g][:, cols].bitcast(E4M3),
+                        rhs_scale=v2_sc[g][:, cols],
                         start=(g == 0),
                         stop=(g == PASSES - 1),
                     )
+            for acc, cols in zip(accs, cuts):
+                reciprocal(acc[:, 0:width], i, response[:, cols], lambda root: root, cols)
+                nc.gpsimd.tensor_tensor(cool[i][:, cols], cool[i][:, cols], response[:, cols], MULT)
 
-        def hot_weight(i, dst):
-            weighted[i] = dst
-            nc.vector.scalar_tensor_tensor(
-                weighted[i], hot_acc[i][:], column(c1_t, i), slot(wg1_t, i % PACK), ADD, MULT
+        def cool_turned(s, turned):
+            acc = bank(PACK + s, "b_turned%d" % s)
+            for g in range(PASSES):
+                nc.tensor.matmul_mx(
+                    out=acc[:],
+                    lhsT=v2_w[g][:, s * P : (s + 1) * P].bitcast(E4M3),
+                    lhsT_scale=v2_sc[g][:, s * P : (s + 1) * P],
+                    rhs=w2_w[1][:, g, :].bitcast(E2M1),
+                    rhs_scale=w2_sc[:, g * H + KP : g * H + H],
+                    start=(g == 0),
+                    stop=(g == PASSES - 1),
+                )
+            reciprocal(
+                acc[:], PACK + s,
+                turned[:, s * S : (s + 1) * S].rearrange("p (t m) -> p m t", t=PACK),
+                lambda root: root.rearrange("p (m t) -> p m t", t=PACK),
             )
 
-        def hot_feature(i, after=None):
-            feature[i] = tile("feature%d" % i, [P, S], F32, after)
+        def turn_back(i, turned):
+            t = i % PACK
+            back = bank(t, "back%d" % i)
+            for s in range(S // P):
+                c = s * S + t * P
+                nc.tensor.transpose(back[:, s * P : (s + 1) * P], turned[:, c : c + P], identity[:])
+            scaled = tile("scaled%d" % i, [P, S], F32)
+            nc.scalar.activation(scaled[:], back[:], ACT.Copy, scale=column(amp_t, i))
+            return scaled
+
+        def weigh_cool(i, scaled, after):
+            cool[i] = tile("cool%d" % i, [P, S], F32, after)
+            nc.gpsimd.tensor_tensor(cool[i][:], scaled[:], slot(wg2_spread, i % PACK), MULT)
+
+        def scatter_cool(i, after=None):
+            pages[i] = tile("page%d" % i, [P, T2], F32, after)
+            nc.vector.tensor_copy(pages[i][:].indirect(idx4[:]), cool[i][:])
+
+        def round_w1_natural():
+            grouped[0] = tile("grouped0", [P, PASSES, KP, PACK], BF16)
+            for g in range(PASSES):
+                for h in range(2):
+                    part = slice(h * KP // 2, (h + 1) * KP // 2)
+                    nc.gpsimd.tensor_scalar(
+                        grouped[0][:, g, part, :], w1_raw[g, 0][:, :, part].rearrange("p j c -> p c j"), 1.0, 0.0, MULT, ADD
+                    )
+
+        def round_w1_dealt():
+            grouped[1] = tile("grouped1", [P, PASSES, KP, PACK], BF16, "turned")
+            for g in range(PASSES):
+                nc.scalar.copy(
+                    grouped[1][:, g].rearrange("p (t m) j -> p m j t", t=PACK),
+                    w1_raw[g, 1][:].rearrange("p j (m t) -> p m j t", t=PACK),
+                )
+
+        def quantise_w1(a, after=None):
+            w1_w[a] = tile("w1_w%d" % a, [P, PASSES * KP], U32)
+            w1_sc[a] = tile("w1_sc%d" % a, [P, PASSES * KP], U8, after)
+            nc.vector.quantize_mx(
+                out=w1_w[a][:].bitcast(E4M3), scales=w1_sc[a][:], in_=grouped[a][:].rearrange("p g c j -> p (g c j)")
+            )
+
+        def hot_values(i):
+            a, t = divmod(i, PACK)
+            hot_acc[i] = bank(i, "a%d" % i)
+            for g in range(PASSES):
+                c = g * KP + t * P
+                nc.tensor.matmul_mx(
+                    out=hot_acc[i][:],
+                    lhsT=w1_w[a][:, c : c + P].bitcast(E4M3),
+                    lhsT_scale=w1_sc[a][:, c : c + P],
+                    rhs=v_w[g][:].bitcast(E4M3),
+                    rhs_scale=v_sc[SCALE_ROWS * g : P, :],
+                    start=(g == 0),
+                    stop=(g == PASSES - 1),
+                )
+            shifted[i] = tile("shifted%d" % i, [P, S], F32, "cool%d" % t if a else None)
+            nc.scalar.activation(shifted[i][:], hot_acc[i][:], ACT.Identity, bias=column(c1_t, i))
+            feature[i] = tile("feature%d" % i, [P, S], F32, "response%d" % t if a else None)
             nc.scalar.copy(feature[i][:], hot_acc[i][:])
 
-        def hot_shifted(i, after=None):
-            shifted[i] = tile("shifted%d" % i, [P, S], F32, after)
-            nc.scalar.activation(shifted[i][:], hot_acc[i][:], ACT.Identity, bias=column(c1_t, i))
-
-        def hot_products(i, after=None):
-            weighted[i] = tile("weighted%d" % i, [P, S], F32, after)
-            nc.gpsimd.tensor_tensor(weighted[i][:], shifted[i][:], slot(wg1_t, i % PACK), MULT)
-            hot[i] = tile("hot%d" % i, [P, S], F32)
-            nc.gpsimd.tensor_tensor(hot[i][:], weighted[i][:], feature[i][:], MULT)
+        def hot_products(i, weighted_after=None, hot_after=None):
+            weight = wg1_rows[:] if i < PACK else slot(wg1_spread, i % PACK)
+            weighted = tile("weighted%d" % i, [P, S], F32, weighted_after) if weighted_after else shifted[i]
+            nc.gpsimd.tensor_tensor(weighted[:], shifted[i][:], weight, MULT)
+            hot[i] = tile("hot%d" % i, [P, S], F32, hot_after) if hot_after else feature[i]
+            nc.gpsimd.tensor_tensor(hot[i][:], weighted[:], feature[i][:], MULT)
 
         def scatter_hot(i):
             nc.vector.tensor_copy(pages[i][:].indirect(idx3[:]), hot[i][:])
 
-        def round_plane(planes, i, c, width):
-            nc.scalar.activation(
-                planes[:, i % PACK, c : c + width], pages[i][:, c : c + width], ACT.Identity, bias=column(c0_t, i)
-            )
+        def turn_plane(i, z_turned):
+            for h in range(2):
+                acc = bank(2 * (i % 2) + h, "z_turned%d%d" % (i, h))
+                for s in range(PACK):
+                    nc.tensor.matmul(
+                        acc[:, s * P : (s + 1) * P], column(c0_t, i).to_broadcast([P, P]), identity[:],
+                        start=(s == 0), stop=False, is_transpose=True,
+                    )
+                for s in range(PACK):
+                    c = (h * PACK + s) * P
+                    nc.tensor.matmul(
+                        acc[:, s * P : (s + 1) * P], pages[i][:, c : c + P], identity[:],
+                        start=False, stop=(s == PACK - 1), is_transpose=True,
+                    )
+                nc.scalar.copy(z_turned[h][:, :, i * P : (i + 1) * P], acc[:].rearrange("p (s r) -> p s r", s=PACK))
 
-        def weave_views(z, planes):
-            return (
-                z.rearrange("p (c n t) -> p c t n", n=PACK, t=PACK),
-                planes.rearrange("p t (c n) -> p c t n", n=PACK),
-            )
+        def weave_turned(z, z_turned):
+            words = z[:].bitcast(F32)
+            for b in range(PACK):
+                acc = bank(PACK + b, "z_words%d" % b)
+                for s in range(2):
+                    pairs = z_turned[b // 2][:, 2 * (b % 2) + s, :].bitcast(F32)
+                    for u in range(2):
+                        c = (2 * s + u) * P
+                        nc.tensor.transpose(acc[:, c : c + P], pairs[:, u : 2 * P : 2], identity[:])
+                nc.scalar.copy(
+                    words[:, b * S : (b + 1) * S].rearrange("p (s n u) -> p s n u", s=2, u=2),
+                    acc[:].rearrange("p (s u n) -> p s n u", s=2, u=2),
+                )
 
         def quantise_z(key, z, after=None):
             width = z.shape[1] // PACK
@@ -305,75 +338,45 @@ def tile_list_creep_life_weave_kernel(
                     stop=(a == PASSES - 1 and m == 1),
                 )
 
-        weigh_cool(0)
-        cool_values(0, parts=2)
-        scatter_cool(0)
-        tab_w.append(load_table("tab_w1", tab_words[1], after="tab2_w0"))
-        v_w.append(gather("v_w1", tab_w[1][:], idx1, U32))
-        w1_raw[1, 0] = load_w1(1, 0, after="w2_sc_raw")
-        w1_raw[0, 1] = load_w1(0, 1, after="tab2_sc")
-        w1_raw[1, 1] = load_w1(1, 1, after="cool0")
-        wg1_t = load_wg1(after="wg2_rows")
-        idx3 = load_list("idx3", offs3)
-        for i in range(1, 6):
-            weigh_cool(i)
-            cool_values(i)
+        for i in range(PACK):
+            weigh_rows(i)
+        for i in range(PACK):
+            cool_direct(i, 2 if i == 0 else 1)
             scatter_cool(i)
-        for i in range(6, PLANES):
-            weigh_cool(i)
-        for g in range(PASSES):
-            round_w1(g, 0)
-            quantise_w1(g, 0)
-        cool_values(6)
-        scatter_cool(6)
-        hot_matmuls(0)
-        first = tile("weighted0", [P, S], F32, "cool6")
-        hot_weight(0, first[:])
-        round_w1(0, 1)
-        quantise_w1(0, 1)
-        hot[0] = tile("hot0", [P, S], F32)
-        nc.vector.tensor_tensor(hot[0][:], weighted[0], hot_acc[0][:], MULT)
-        scatter_hot(0)
-        round_w1(1, 1)
-        quantise_w1(1, 1)
-        for i in range(1, PACK):
-            hot_feature(i)
-            hot_shifted(i)
-        hot_products(1, after="cool_weight6")
-        scatter_hot(1)
-        hot_products(2, after="grouped11")
-        scatter_hot(2)
-        hot_products(3)
-        cool_values(LAST)
-        w3_w = tile("w3_w", [P, PASSES, N], U32, "v2_w0")
+        round_w1_natural()
+        wg1_spread = load_spread("wg1_spread", wg1, after="w1_raw00")
+
+        turned = tile("turned", [P, PACK * S], F32)
+        for s in range(S // P):
+            cool_turned(s, turned)
+        w3_w = tile("w3_w", [P, PASSES, N], U32, "tab2_w0")
         nc.sync.dma_start(w3_w[:].bitcast(I32), w3_words.rearrange("g p c i -> p g (c i)").bitcast(I32))
-        w3_sc = tile("w3_sc", [P, N], U8, "v2_sc0")
-        nc.gpsimd.memset(w3_sc[:].bitcast(I32), 0)
-        load_scales_stacked(w3_sc, w3_scales)
+        scaled = {i: turn_back(i, turned) for i in range(PACK, PLANES)}
+        weigh_cool(4, scaled[4], "w1_raw10")
+        scatter_cool(4)
+        weigh_cool(5, scaled[5], "scaled4")
+        quantise_w1(0, "scaled5")
+        scatter_cool(5)
+        weigh_cool(6, scaled[6], "grouped0")
+        round_w1_dealt()
+        quantise_w1(1)
+        scatter_cool(6, "w1_raw11")
 
-        planes = tile("planes0", [P, PACK, T2], BF16, "w2_sc_raw")
-        hot_matmuls(1)
-        for i in range(PACK, PLANES):
-            hot_feature(i, after="cool%d" % (i - PACK))
-            hot_shifted(i, after="cool_weight%d" % (i - PACK))
-            hot_products(i)
-        for i in range(3):
-            round_plane(planes, i, 0, T2)
-        scatter_hot(3)
-        round_plane(planes, 3, 0, T2)
-        z0 = tile("z0", [P, PACK * T2], BF16, "w2_raw0")
-        nc.scalar.copy(*weave_views(z0[:], planes[:]))
-        for i in (4, 5, 6):
+        for i in range(PLANES):
+            hot_values(i)
+        z_turned = [tile("z_turned%d" % h, [P, PACK, KP], BF16, ("tab2_w1", "wg2_rows")[h]) for h in range(2)]
+        hot_products(0, weighted_after="turned")
+        for i in range(PACK):
+            if i:
+                hot_products(i)
             scatter_hot(i)
-        quantise_z((0, 0), z0[:], after="hot5")
-        scatter_cool(LAST, page_after="w2_raw0")
-        scores = [bank((b + PACK) % BANKS, "score%d" % b) for b in range(BANKS)]
-        for b in range(BANKS):
-            score_pass(0, b, (0, 0), (b // 2) * CHUNK)
-        scatter_hot(LAST)
+            turn_plane(i, z_turned)
+        z0 = tile("z0", [P, PACK * T2], BF16, "w1_raw01")
+        weave_turned(z0, z_turned)
 
-        z1 = [tile("z1%d" % q, [P, CHUNK, PACK], BF16, "wg2_repeated%d" % q) for q in range(CHUNKS)]
-        for i in range(PACK, LAST):
+        z1 = [tile("z1%d" % q, [P, CHUNK, PACK], BF16, ("v2_w0", "v2_w1", "root1", "amp_t0")[q]) for q in range(CHUNKS)]
+
+        def round_plane(i):
             for q in range(CHUNKS):
                 values = pages[i][:, q * CHUNK : (q + 1) * CHUNK]
                 if i == LAST - 1:
@@ -382,6 +385,23 @@ def tile_list_creep_life_weave_kernel(
                     )
                 else:
                     nc.scalar.activation(z1[q][:, :, i % PACK], values, ACT.Identity, bias=column(c0_t, i))
+
+        for i in (4, 5):
+            hot_products(i)
+            scatter_hot(i)
+            round_plane(i)
+        hot_products(6, hot_after="root0")
+        quantise_z((0, 0), z0[:], after="response2")
+        scatter_hot(6)
+        round_plane(6)
+        weigh_cool(LAST, scaled[LAST], "cool2")
+        scatter_cool(LAST)
+        scores = [bank(b, "score%d" % b) for b in range(BANKS)]
+        for b in range(BANKS):
+            score_pass(0, b, (0, 0), (b // 2) * CHUNK)
+        hot_products(LAST)
+        scatter_hot(LAST)
+
         for q in range(CHUNKS):
             nc.vector.tensor_scalar_add(
                 z1[q][:, :, PACK - 1], pages[LAST][:, q * CHUNK : (q + 1) * CHUNK], column(c0_t, LAST)
@@ -389,7 +409,7 @@ def tile_list_creep_life_weave_kernel(
             quantise_z((1, q), z1[q][:].rearrange("p c t -> p (c t)"))
             for b in (2 * q, 2 * q + 1):
                 score_pass(1, b, (1, q), 0)
-        staged = [tile("staged%d" % s, [P, CHUNKS * S], F32, ("tab2_w0", "tab2_sc")[s]) for s in range(2)]
+        staged = [tile("staged%d" % s, [P, CHUNKS * S], F32, "tab_w%d" % s) for s in range(2)]
         for b in range(BANKS):
             q, lower = divmod(b, 2)
             result = slot(staged[b // CHUNKS], b % CHUNKS)

@@ -134,13 +134,9 @@ def tile_list_creep_life_weave_kernel(
         tab_w.append(load_table("tab_w1", tab_words[1]))
         idx4 = load_list("idx4", offs4)
         w2_w.append(load_w2(1))
-        w1_raw = {}
-        for g in range(PASSES):
-            w1_raw[g, 0] = load_w1(g, 0)
-        wg2_spread = load_spread("wg2_spread", wg2)
         amp_t.append(load_coefficients("amp_t", amp, 1, nc.sync))
-        for g in range(PASSES):
-            w1_raw[g, 1] = load_w1(g, 1)
+        wg2_spread = load_spread("wg2_spread", wg2)
+        w1_raw = {(g, a): load_w1(g, a) for a in range(PASSES) for g in range(PASSES)}
         c1_t = [load_coefficients("c1_t", c1, a, nc.sync) for a in range(PASSES)]
         wg1_rows = load_rows("wg1_rows", wg1)
         idx3 = load_list("idx3", offs3)
@@ -168,13 +164,11 @@ def tile_list_creep_life_weave_kernel(
         cool, pages, hot, hot_acc, feature, shifted = {}, {}, {}, {}, {}, {}
         grouped, w1_w, w1_sc, z_w, z_sc, squares, roots = {}, {}, {}, {}, {}, {}, {}
 
-        def reciprocal(acc, k, dst_view, src_view, cols=slice(0, S)):
+        def inverse_root(acc, k, dst_view, cols=slice(0, S), shape=lambda view: view):
             if cols.start == 0:
                 squares[k] = tile("square%d" % k, [P, S], F32, "root0" if k == 1 else ("wg2_rows", "amp_t0")[k % 2])
-                roots[k] = tile("root%d" % k, [P, S], F32, "root%d" % (k % 2))
             nc.scalar.activation(squares[k][:, cols], acc, ACT.Square)
-            nc.scalar.activation(roots[k][:, cols], squares[k][:, cols], ACT.Abs_reciprocal_sqrt, bias=1.0)
-            nc.scalar.activation(dst_view, src_view(roots[k][:, cols]), ACT.Square)
+            nc.scalar.activation(dst_view, shape(squares[k][:, cols]), ACT.Abs_reciprocal_sqrt, bias=1.0)
 
         def weigh_rows(i):
             cool[i] = tile("cool%d" % i, [P, S], F32)
@@ -182,6 +176,7 @@ def tile_list_creep_life_weave_kernel(
 
         def cool_direct(i, parts):
             response = tile("response%d" % i, [P, S], F32)
+            root = tile("root%d" % i, [P, S], F32) if i < 2 else response
             width = S // parts
             cuts = [slice(h * width, (h + 1) * width) for h in range(parts)]
             accs = [bank(i + PACK * h, "b%d%d" % (i, h)) for h in range(parts)]
@@ -197,7 +192,11 @@ def tile_list_creep_life_weave_kernel(
                         stop=(g == PASSES - 1),
                     )
             for acc, cols in zip(accs, cuts):
-                reciprocal(acc[:, 0:width], i, response[:, cols], lambda root: root, cols)
+                inverse_root(acc[:, 0:width], i, root[:, cols], cols)
+                if i < 2:
+                    nc.scalar.activation(response[:, cols], root[:, cols], ACT.Square)
+                else:
+                    nc.gpsimd.tensor_tensor(cool[i][:, cols], cool[i][:, cols], root[:, cols], MULT)
                 nc.gpsimd.tensor_tensor(cool[i][:, cols], cool[i][:, cols], response[:, cols], MULT)
 
         def cool_turned(s, turned):
@@ -212,10 +211,10 @@ def tile_list_creep_life_weave_kernel(
                     start=(g == 0),
                     stop=(g == PASSES - 1),
                 )
-            reciprocal(
+            inverse_root(
                 acc[:], PACK + s,
                 turned[:, s * S : (s + 1) * S].rearrange("p (t m) -> p m t", t=PACK),
-                lambda root: root.rearrange("p (m t) -> p m t", t=PACK),
+                shape=lambda view: view.rearrange("p (m t) -> p m t", t=PACK),
             )
 
         def turn_back(i, turned):
@@ -225,28 +224,29 @@ def tile_list_creep_life_weave_kernel(
                 c = s * S + t * P
                 nc.tensor.transpose(back[:, s * P : (s + 1) * P], turned[:, c : c + P], identity[:])
             scaled = tile("scaled%d" % i, [P, S], F32)
-            nc.scalar.activation(scaled[:], back[:], ACT.Copy, scale=column(amp_t, i))
+            nc.scalar.activation(scaled[:], back[:], ACT.Square)
             return scaled
 
         def weigh_cool(i, scaled, after):
-            cool[i] = tile("cool%d" % i, [P, S], F32, after)
-            nc.gpsimd.tensor_tensor(cool[i][:], scaled[:], slot(wg2_spread, i % PACK), MULT)
+            weight = tile("weight%d" % i, [P, S], F32)
+            nc.gpsimd.tensor_scalar(weight[:], slot(wg2_spread, i % PACK), column(amp_t, i), 0.0, MULT, ADD)
+            cool[i] = tile("cool%d" % i, [P, S], F32, after) if after else weight
+            nc.gpsimd.tensor_tensor(cool[i][:], scaled[:], weight[:], MULT)
 
         def scatter_cool(i, after=None):
             pages[i] = tile("page%d" % i, [P, T2], F32, after)
             nc.vector.tensor_copy(pages[i][:].indirect(idx4[:]), cool[i][:])
 
         def round_w1_natural():
-            grouped[0] = tile("grouped0", [P, PASSES, KP, PACK], BF16)
+            grouped[0] = tile("grouped0", [P, PASSES, KP, PACK], BF16, "turned")
             for g in range(PASSES):
-                for h in range(2):
-                    part = slice(h * KP // 2, (h + 1) * KP // 2)
-                    nc.gpsimd.tensor_scalar(
-                        grouped[0][:, g, part, :], w1_raw[g, 0][:, :, part].rearrange("p j c -> p c j"), 1.0, 0.0, MULT, ADD
-                    )
+                nc.scalar.copy(
+                    grouped[0][:, g].rearrange("p (c n) j -> p c j n", n=PACK),
+                    w1_raw[g, 0][:].rearrange("p j (c n) -> p c j n", n=PACK),
+                )
 
         def round_w1_dealt():
-            grouped[1] = tile("grouped1", [P, PASSES, KP, PACK], BF16, "turned")
+            grouped[1] = tile("grouped1", [P, PASSES, KP, PACK], BF16, "scaled5")
             for g in range(PASSES):
                 nc.scalar.copy(
                     grouped[1][:, g].rearrange("p (t m) j -> p m j t", t=PACK),
@@ -343,8 +343,6 @@ def tile_list_creep_life_weave_kernel(
         for i in range(PACK):
             cool_direct(i, 2 if i == 0 else 1)
             scatter_cool(i)
-        round_w1_natural()
-        wg1_spread = load_spread("wg1_spread", wg1, after="w1_raw00")
 
         turned = tile("turned", [P, PACK * S], F32)
         for s in range(S // P):
@@ -352,23 +350,25 @@ def tile_list_creep_life_weave_kernel(
         w3_w = tile("w3_w", [P, PASSES, N], U32, "tab2_w0")
         nc.sync.dma_start(w3_w[:].bitcast(I32), w3_words.rearrange("g p c i -> p g (c i)").bitcast(I32))
         scaled = {i: turn_back(i, turned) for i in range(PACK, PLANES)}
-        weigh_cool(4, scaled[4], "w1_raw10")
+        weigh_cool(4, scaled[4], None)
         scatter_cool(4)
-        weigh_cool(5, scaled[5], "scaled4")
-        quantise_w1(0, "scaled5")
-        scatter_cool(5)
-        weigh_cool(6, scaled[6], "grouped0")
+        weigh_cool(5, scaled[5], None)
+        round_w1_natural()
+        wg1_spread = load_spread("wg1_spread", wg1, after="w1_raw00")
+        quantise_w1(0)
+        scatter_cool(5, "w1_raw10")
+        weigh_cool(6, scaled[6], "turned")
+        scatter_cool(6)
+        weigh_cool(LAST, scaled[LAST], "weight6")
         round_w1_dealt()
         quantise_w1(1)
-        scatter_cool(6, "w1_raw11")
+        scatter_cool(LAST, "w1_raw11")
 
         for i in range(PLANES):
             hot_values(i)
         z_turned = [tile("z_turned%d" % h, [P, PACK, KP], BF16, ("tab2_w1", "wg2_rows")[h]) for h in range(2)]
-        hot_products(0, weighted_after="turned")
         for i in range(PACK):
-            if i:
-                hot_products(i)
+            hot_products(i, weighted_after="scaled5" if i == 1 else None)
             scatter_hot(i)
             turn_plane(i, z_turned)
         z0 = tile("z0", [P, PACK * T2], BF16, "w1_raw01")
@@ -391,11 +391,9 @@ def tile_list_creep_life_weave_kernel(
             scatter_hot(i)
             round_plane(i)
         hot_products(6, hot_after="root0")
-        quantise_z((0, 0), z0[:], after="response2")
         scatter_hot(6)
         round_plane(6)
-        weigh_cool(LAST, scaled[LAST], "cool2")
-        scatter_cool(LAST)
+        quantise_z((0, 0), z0[:], after="response2")
         scores = [bank(b, "score%d" % b) for b in range(BANKS)]
         for b in range(BANKS):
             score_pass(0, b, (0, 0), (b // 2) * CHUNK)
@@ -420,7 +418,7 @@ def tile_list_creep_life_weave_kernel(
                     nc.scalar.copy(result[:, part], scores[b][:, part])
                     nc.sync.dma_start(rows[m * P : (m + 1) * P], result[:, part])
                 continue
-            if q >= CHUNKS // 2 and lower == 1:
+            if b >= 5:
                 nc.vector.tensor_copy(result, scores[b][:])
             else:
                 nc.scalar.copy(result, scores[b][:])

@@ -122,8 +122,8 @@ def tile_list_creep_life_weave_kernel(
 
         idx2 = load_list("idx2", offs2)
         load_scales_side_by_side(tab2_sc, tab2_scales)
-        tab2_w = [load_table("tab2_w%d" % g, tab2_words[g]) for g in range(PASSES)]
         wg2_rows = load_rows("wg2_rows", wg2)
+        tab2_w = [load_table("tab2_w%d" % g, tab2_words[g]) for g in range(PASSES)]
         w2_w = [load_w2(0)]
         load_scales_side_by_side(w2_sc, w2_scales)
         identity = tile("identity", [P, P], F32)
@@ -211,10 +211,12 @@ def tile_list_creep_life_weave_kernel(
                     start=(g == 0),
                     stop=(g == PASSES - 1),
                 )
-            inverse_root(
-                acc[:], PACK + s,
+            root = tile("root%d" % (PACK + s), [P, S], F32, "root%d" % (s % 2))
+            inverse_root(acc[:], PACK + s, root[:])
+            nc.scalar.activation(
                 turned[:, s * S : (s + 1) * S].rearrange("p (t m) -> p m t", t=PACK),
-                shape=lambda view: view.rearrange("p (m t) -> p m t", t=PACK),
+                root[:].rearrange("p (m t) -> p m t", t=PACK),
+                ACT.Square,
             )
 
         def turn_back(i, turned):
@@ -223,15 +225,13 @@ def tile_list_creep_life_weave_kernel(
             for s in range(S // P):
                 c = s * S + t * P
                 nc.tensor.transpose(back[:, s * P : (s + 1) * P], turned[:, c : c + P], identity[:])
-            scaled = tile("scaled%d" % i, [P, S], F32)
-            nc.scalar.activation(scaled[:], back[:], ACT.Square)
-            return scaled
+            return back
 
-        def weigh_cool(i, scaled, after):
-            weight = tile("weight%d" % i, [P, S], F32)
-            nc.gpsimd.tensor_scalar(weight[:], slot(wg2_spread, i % PACK), column(amp_t, i), 0.0, MULT, ADD)
-            cool[i] = tile("cool%d" % i, [P, S], F32, after) if after else weight
-            nc.gpsimd.tensor_tensor(cool[i][:], scaled[:], weight[:], MULT)
+        def weigh_cool(i, after):
+            scaled = tile("scaled%d" % i, [P, S], F32)
+            nc.scalar.activation(scaled[:], backs[i][:], ACT.Copy, scale=column(amp_t, i))
+            cool[i] = tile("cool%d" % i, [P, S], F32, after)
+            nc.gpsimd.tensor_tensor(cool[i][:], scaled[:], slot(wg2_spread, i % PACK), MULT)
 
         def scatter_cool(i, after=None):
             pages[i] = tile("page%d" % i, [P, T2], F32, after)
@@ -245,13 +245,11 @@ def tile_list_creep_life_weave_kernel(
                     w1_raw[g, 0][:].rearrange("p j (c n) -> p c j n", n=PACK),
                 )
 
-        def round_w1_dealt():
-            grouped[1] = tile("grouped1", [P, PASSES, KP, PACK], BF16, "scaled5")
-            for g in range(PASSES):
-                nc.scalar.copy(
-                    grouped[1][:, g].rearrange("p (t m) j -> p m j t", t=PACK),
-                    w1_raw[g, 1][:].rearrange("p j (m t) -> p m j t", t=PACK),
-                )
+        def round_w1_dealt(g):
+            nc.scalar.copy(
+                grouped[1][:, g].rearrange("p (t m) j -> p m j t", t=PACK),
+                w1_raw[g, 1][:].rearrange("p j (m t) -> p m j t", t=PACK),
+            )
 
         def quantise_w1(a, after=None):
             w1_w[a] = tile("w1_w%d" % a, [P, PASSES * KP], U32)
@@ -303,7 +301,10 @@ def tile_list_creep_life_weave_kernel(
                         acc[:, s * P : (s + 1) * P], pages[i][:, c : c + P], identity[:],
                         start=False, stop=(s == PACK - 1), is_transpose=True,
                     )
-                nc.scalar.copy(z_turned[h][:, :, i * P : (i + 1) * P], acc[:].rearrange("p (s r) -> p s r", s=PACK))
+                nc.scalar.copy(
+                    z_turned[h][:].rearrange("p s (u m e) -> p s m u e", u=2, e=2)[:, :, i * QUAD : (i + 1) * QUAD],
+                    acc[:].rearrange("p (s m u e) -> p s m u e", s=PACK, u=2, e=2),
+                )
 
         def weave_turned(z, z_turned):
             words = z[:].bitcast(F32)
@@ -313,7 +314,7 @@ def tile_list_creep_life_weave_kernel(
                     pairs = z_turned[b // 2][:, 2 * (b % 2) + s, :].bitcast(F32)
                     for u in range(2):
                         c = (2 * s + u) * P
-                        nc.tensor.transpose(acc[:, c : c + P], pairs[:, u : 2 * P : 2], identity[:])
+                        nc.tensor.transpose(acc[:, c : c + P], pairs[:, u * P : (u + 1) * P], identity[:])
                 nc.scalar.copy(
                     words[:, b * S : (b + 1) * S].rearrange("p (s n u) -> p s n u", s=2, u=2),
                     acc[:].rearrange("p (s u n) -> p s n u", s=2, u=2),
@@ -338,6 +339,7 @@ def tile_list_creep_life_weave_kernel(
                     stop=(a == PASSES - 1 and m == 1),
                 )
 
+        backs = {}
         for i in range(PACK):
             weigh_rows(i)
         for i in range(PACK):
@@ -349,26 +351,28 @@ def tile_list_creep_life_weave_kernel(
             cool_turned(s, turned)
         w3_w = tile("w3_w", [P, PASSES, N], U32, "tab2_w0")
         nc.sync.dma_start(w3_w[:].bitcast(I32), w3_words.rearrange("g p c i -> p g (c i)").bitcast(I32))
-        scaled = {i: turn_back(i, turned) for i in range(PACK, PLANES)}
-        weigh_cool(4, scaled[4], None)
-        scatter_cool(4)
-        weigh_cool(5, scaled[5], None)
+        for i in range(PACK, PLANES):
+            backs[i] = turn_back(i, turned)
+        for i in (4, 5):
+            weigh_cool(i, None)
+            scatter_cool(i)
+        weigh_cool(6, None)
         round_w1_natural()
         wg1_spread = load_spread("wg1_spread", wg1, after="w1_raw00")
         quantise_w1(0)
-        scatter_cool(5, "w1_raw10")
-        weigh_cool(6, scaled[6], "turned")
-        scatter_cool(6)
-        weigh_cool(LAST, scaled[LAST], "weight6")
-        round_w1_dealt()
+        scatter_cool(6, "w1_raw10")
+        weigh_cool(LAST, "turned")
+        scatter_cool(LAST)
+        grouped[1] = tile("grouped1", [P, PASSES, KP, PACK], BF16, "scaled5")
+        round_w1_dealt(0)
+        hot_values(0)
+        round_w1_dealt(1)
         quantise_w1(1)
-        scatter_cool(LAST, "w1_raw11")
-
-        for i in range(PLANES):
+        for i in range(1, PLANES):
             hot_values(i)
         z_turned = [tile("z_turned%d" % h, [P, PACK, KP], BF16, ("tab2_w1", "wg2_rows")[h]) for h in range(2)]
         for i in range(PACK):
-            hot_products(i, weighted_after="scaled5" if i == 1 else None)
+            hot_products(i, "scaled5" if i == 1 else None, "w1_raw11" if i == 0 else None)
             scatter_hot(i)
             turn_plane(i, z_turned)
         z0 = tile("z0", [P, PACK * T2], BF16, "w1_raw01")

@@ -176,7 +176,7 @@ def tile_list_creep_life_weave_kernel(
 
         def cool_direct(i, parts):
             response = tile("response%d" % i, [P, S], F32)
-            root = tile("root%d" % i, [P, S], F32) if i < 2 else response
+            root = tile("root%d" % i, [P, S], F32, "root%d" % (i % 2))
             width = S // parts
             cuts = [slice(h * width, (h + 1) * width) for h in range(parts)]
             accs = [bank(i + PACK * h, "b%d%d" % (i, h)) for h in range(parts)]
@@ -193,11 +193,8 @@ def tile_list_creep_life_weave_kernel(
                     )
             for acc, cols in zip(accs, cuts):
                 inverse_root(acc[:, 0:width], i, root[:, cols], cols)
-                if i < 2:
-                    nc.scalar.activation(response[:, cols], root[:, cols], ACT.Square)
-                else:
-                    nc.gpsimd.tensor_tensor(cool[i][:, cols], cool[i][:, cols], root[:, cols], MULT)
-                nc.gpsimd.tensor_tensor(cool[i][:, cols], cool[i][:, cols], response[:, cols], MULT)
+                nc.scalar.activation(response[:, cols], root[:, cols], ACT.Square)
+            factors[i] = (response[:], cool[i][:])
 
         def cool_turned(s, turned):
             acc = bank(PACK + s, "b_turned%d" % s)
@@ -211,12 +208,10 @@ def tile_list_creep_life_weave_kernel(
                     start=(g == 0),
                     stop=(g == PASSES - 1),
                 )
-            root = tile("root%d" % (PACK + s), [P, S], F32, "root%d" % (s % 2))
-            inverse_root(acc[:], PACK + s, root[:])
-            nc.scalar.activation(
+            inverse_root(
+                acc[:], PACK + s,
                 turned[:, s * S : (s + 1) * S].rearrange("p (t m) -> p m t", t=PACK),
-                root[:].rearrange("p (m t) -> p m t", t=PACK),
-                ACT.Square,
+                shape=lambda view: view.rearrange("p (m t) -> p m t", t=PACK),
             )
 
         def turn_back(i, turned):
@@ -227,15 +222,16 @@ def tile_list_creep_life_weave_kernel(
                 nc.tensor.transpose(back[:, s * P : (s + 1) * P], turned[:, c : c + P], identity[:])
             return back
 
-        def weigh_cool(i, after):
-            scaled = tile("scaled%d" % i, [P, S], F32)
-            nc.scalar.activation(scaled[:], backs[i][:], ACT.Copy, scale=column(amp_t, i))
-            cool[i] = tile("cool%d" % i, [P, S], F32, after)
-            nc.gpsimd.tensor_tensor(cool[i][:], scaled[:], slot(wg2_spread, i % PACK), MULT)
+        def weigh_cool(i):
+            weight = tile("weight%d" % i, [P, S], F32)
+            nc.scalar.activation(weight[:], slot(wg2_spread, i % PACK), ACT.Copy, scale=column(amp_t, i))
+            response = tile("response%d" % i, [P, S], F32)
+            nc.scalar.activation(response[:], backs[i][:], ACT.Square)
+            factors[i] = (response[:], weight[:])
 
         def scatter_cool(i, after=None):
             pages[i] = tile("page%d" % i, [P, T2], F32, after)
-            nc.vector.tensor_copy(pages[i][:].indirect(idx4[:]), cool[i][:])
+            nc.vector.tensor_tensor(pages[i][:].indirect(idx4[:]), *factors[i], MULT)
 
         def round_w1_natural():
             grouped[0] = tile("grouped0", [P, PASSES, KP, PACK], BF16, "turned")
@@ -272,6 +268,8 @@ def tile_list_creep_life_weave_kernel(
                     start=(g == 0),
                     stop=(g == PASSES - 1),
                 )
+            if i == 0:
+                return
             shifted[i] = tile("shifted%d" % i, [P, S], F32, "cool%d" % t if a else None)
             nc.scalar.activation(shifted[i][:], hot_acc[i][:], ACT.Identity, bias=column(c1_t, i))
             feature[i] = tile("feature%d" % i, [P, S], F32, "response%d" % t if a else None)
@@ -301,10 +299,7 @@ def tile_list_creep_life_weave_kernel(
                         acc[:, s * P : (s + 1) * P], pages[i][:, c : c + P], identity[:],
                         start=False, stop=(s == PACK - 1), is_transpose=True,
                     )
-                nc.scalar.copy(
-                    z_turned[h][:].rearrange("p s (u m e) -> p s m u e", u=2, e=2)[:, :, i * QUAD : (i + 1) * QUAD],
-                    acc[:].rearrange("p (s m u e) -> p s m u e", s=PACK, u=2, e=2),
-                )
+                nc.scalar.copy(z_turned[h][:, :, i * P : (i + 1) * P], acc[:].rearrange("p (s r) -> p s r", s=PACK))
 
         def weave_turned(z, z_turned):
             words = z[:].bitcast(F32)
@@ -314,7 +309,7 @@ def tile_list_creep_life_weave_kernel(
                     pairs = z_turned[b // 2][:, 2 * (b % 2) + s, :].bitcast(F32)
                     for u in range(2):
                         c = (2 * s + u) * P
-                        nc.tensor.transpose(acc[:, c : c + P], pairs[:, u * P : (u + 1) * P], identity[:])
+                        nc.tensor.transpose(acc[:, c : c + P], pairs[:, u : 2 * P : 2], identity[:])
                 nc.scalar.copy(
                     words[:, b * S : (b + 1) * S].rearrange("p (s n u) -> p s n u", s=2, u=2),
                     acc[:].rearrange("p (s u n) -> p s n u", s=2, u=2),
@@ -339,7 +334,7 @@ def tile_list_creep_life_weave_kernel(
                     stop=(a == PASSES - 1 and m == 1),
                 )
 
-        backs = {}
+        backs, factors = {}, {}
         for i in range(PACK):
             weigh_rows(i)
         for i in range(PACK):
@@ -354,28 +349,35 @@ def tile_list_creep_life_weave_kernel(
         for i in range(PACK, PLANES):
             backs[i] = turn_back(i, turned)
         for i in (4, 5):
-            weigh_cool(i, None)
+            weigh_cool(i)
             scatter_cool(i)
-        weigh_cool(6, None)
         round_w1_natural()
-        wg1_spread = load_spread("wg1_spread", wg1, after="w1_raw00")
         quantise_w1(0)
+        weigh_cool(6)
         scatter_cool(6, "w1_raw10")
-        weigh_cool(LAST, "turned")
-        scatter_cool(LAST)
-        grouped[1] = tile("grouped1", [P, PASSES, KP, PACK], BF16, "scaled5")
-        round_w1_dealt(0)
+        grouped[1] = tile("grouped1", [P, PASSES, KP, PACK], BF16, "w1_raw00")
+        for g in range(PASSES):
+            round_w1_dealt(g)
+        wg1_spread = load_spread("wg1_spread", wg1, after="w1_raw01")
         hot_values(0)
-        round_w1_dealt(1)
+        weighted = tile("weighted0", [P, S], F32)
+        nc.vector.scalar_tensor_tensor(weighted[:], hot_acc[0][:], column(c1_t, 0), wg1_rows[:], ADD, MULT)
+        hot[0] = tile("hot0", [P, S], F32)
+        nc.vector.tensor_tensor(hot[0][:], weighted[:], hot_acc[0][:], MULT)
+        scatter_hot(0)
         quantise_w1(1)
-        for i in range(1, PLANES):
+        hot_values(1)
+        hot_values(2)
+        weigh_cool(LAST)
+        for i in range(3, PLANES):
             hot_values(i)
         z_turned = [tile("z_turned%d" % h, [P, PACK, KP], BF16, ("tab2_w1", "wg2_rows")[h]) for h in range(2)]
         for i in range(PACK):
-            hot_products(i, "scaled5" if i == 1 else None, "w1_raw11" if i == 0 else None)
-            scatter_hot(i)
+            if i:
+                hot_products(i, {1: "weight6", 2: "w1_raw00"}.get(i))
+                scatter_hot(i)
             turn_plane(i, z_turned)
-        z0 = tile("z0", [P, PACK * T2], BF16, "w1_raw01")
+        z0 = tile("z0", [P, PACK * T2], BF16, "turned")
         weave_turned(z0, z_turned)
 
         z1 = [tile("z1%d" % q, [P, CHUNK, PACK], BF16, ("v2_w0", "v2_w1", "root1", "amp_t0")[q]) for q in range(CHUNKS)]
@@ -390,24 +392,25 @@ def tile_list_creep_life_weave_kernel(
                 else:
                     nc.scalar.activation(z1[q][:, :, i % PACK], values, ACT.Identity, bias=column(c0_t, i))
 
-        for i in (4, 5):
-            hot_products(i)
+        for i in range(PACK, LAST):
+            hot_products(i, hot_after="root0" if i == LAST - 1 else None)
             scatter_hot(i)
             round_plane(i)
-        hot_products(6, hot_after="root0")
-        scatter_hot(6)
-        round_plane(6)
+        scatter_cool(LAST, "cool2")
+        hot_products(LAST)
         quantise_z((0, 0), z0[:], after="response2")
         scores = [bank(b, "score%d" % b) for b in range(BANKS)]
         for b in range(BANKS):
             score_pass(0, b, (0, 0), (b // 2) * CHUNK)
-        hot_products(LAST)
         scatter_hot(LAST)
 
         for q in range(CHUNKS):
-            nc.vector.tensor_scalar_add(
-                z1[q][:, :, PACK - 1], pages[LAST][:, q * CHUNK : (q + 1) * CHUNK], column(c0_t, LAST)
-            )
+            values = pages[LAST][:, q * CHUNK : (q + 1) * CHUNK]
+            if q % 2 == 0:
+                nc.vector.tensor_scalar_add(z1[q][:, :, PACK - 1], values, column(c0_t, LAST))
+            else:
+                nc.scalar.activation(z1[q][:, :, PACK - 1], values, ACT.Identity, bias=column(c0_t, LAST))
+        for q in range(CHUNKS):
             quantise_z((1, q), z1[q][:].rearrange("p c t -> p (c t)"))
             for b in (2 * q, 2 * q + 1):
                 score_pass(1, b, (1, q), 0)
@@ -422,7 +425,7 @@ def tile_list_creep_life_weave_kernel(
                     nc.scalar.copy(result[:, part], scores[b][:, part])
                     nc.sync.dma_start(rows[m * P : (m + 1) * P], result[:, part])
                 continue
-            if b >= 5:
+            if q >= 1 and lower == 1:
                 nc.vector.tensor_copy(result, scores[b][:])
             else:
                 nc.scalar.copy(result, scores[b][:])

@@ -74,14 +74,24 @@ def tile_list_creep_life_weave_kernel(
                     src[:, SCALE_ROWS * q : SCALE_ROWS * (q + 1), :].bitcast(I32),
                 )
 
-        def load_coefficients(name, src, a, queue):
-            dst = tile("%s%d" % (name, a), [P, PACK], F32)
-            if a == 0:
-                with nc.allow_non_contiguous_dma(reason="one value a partition and plane"):
-                    queue.dma_start(dst[:], src[0:KP].rearrange("(t p) -> p t", t=PACK))
-            else:
-                queue.dma_start(dst[:], src[KP:H].rearrange("(p t) -> p t", t=PACK))
-            return dst
+        def load_dealt(name, src):
+            dst = tile(name, [P, PACK], F32)
+            nc.gpsimd.dma_start(dst[:], src[KP:H].rearrange("(p t) -> p t", t=PACK))
+            return dst[:]
+
+        def load_natural(name, sources, queue):
+            rows = tile(name, [P, P], F32)
+            nc.gpsimd.memset(rows[:], 0.0)
+            for k, src in enumerate(sources):
+                queue.dma_start(rows[PACK * k : PACK * (k + 1), :], src[0:KP].rearrange("(t p) -> t p", t=PACK))
+            return rows
+
+        def turn_natural(name, rows, count, b):
+            acc = bank(b, name + "_turned")
+            nc.tensor.transpose(acc[:, 0:P], rows[:], identity[:])
+            dst = tile(name, [P, count * PACK], F32)
+            nc.scalar.copy(dst[:], acc[:, 0 : count * PACK])
+            return [dst[:, PACK * k : PACK * (k + 1)] for k in range(count)]
 
         def load_rows(name, src, after=None):
             dst = tile(name, [P, S], F32, after)
@@ -111,7 +121,12 @@ def tile_list_creep_life_weave_kernel(
         w2_sc = tile("w2_sc", [P, PASSES * H], U8)
         tab_sc = tile("tab_sc", [P, T], U8)
         w3_sc = tile("w3_sc", [P, N], U8)
-        amp_t = [load_coefficients("amp_t", amp, 0, nc.gpsimd)]
+        idx2 = load_list("idx2", offs2)
+        amp_rows = load_natural("amp_rows", [amp], nc.sync)
+        identity = tile("identity", [P, P], F32)
+        make_identity(nc, identity[:])
+        c_rows = load_natural("c_rows", [c1, c0], nc.gpsimd)
+        amp_dealt, c1_dealt, c0_dealt = load_dealt("amp_t1", amp), load_dealt("c1_t1", c1), load_dealt("c0_t1", c0)
         nc.vector.memset(tab2_sc[:].bitcast(I32), 0)
         nc.vector.memset(tab_sc[:].bitcast(I32), 0)
         nc.vector.memset(w2_sc[:].bitcast(I32), 0)
@@ -120,27 +135,21 @@ def tile_list_creep_life_weave_kernel(
         nc.vector.memset(warm[:, 0:1], 1.0)
         nc.scalar.activation(warm[:, 1:2], warm[:, 0:1], ACT.Abs_reciprocal_sqrt)
 
-        idx2 = load_list("idx2", offs2)
         load_scales_side_by_side(tab2_sc, tab2_scales)
         wg2_rows = load_rows("wg2_rows", wg2)
         tab2_w = [load_table("tab2_w%d" % g, tab2_words[g]) for g in range(PASSES)]
         w2_w = [load_w2(0)]
         load_scales_side_by_side(w2_sc, w2_scales)
-        identity = tile("identity", [P, P], F32)
-        make_identity(nc, identity[:])
         tab_w = [load_table("tab_w0", tab_words[0])]
         idx1 = load_list("idx1", offs)
+        idx4 = load_list("idx4", offs4)
         load_scales_stacked(tab_sc, tab_scales, nc.sync)
         tab_w.append(load_table("tab_w1", tab_words[1]))
-        idx4 = load_list("idx4", offs4)
         w2_w.append(load_w2(1))
-        amp_t.append(load_coefficients("amp_t", amp, 1, nc.sync))
         wg2_spread = load_spread("wg2_spread", wg2)
         w1_raw = {(g, a): load_w1(g, a) for a in range(PASSES) for g in range(PASSES)}
-        c1_t = [load_coefficients("c1_t", c1, a, nc.sync) for a in range(PASSES)]
         wg1_rows = load_rows("wg1_rows", wg1)
         idx3 = load_list("idx3", offs3)
-        c0_t = [load_coefficients("c0_t", c0, a, nc.sync) for a in range(PASSES)]
         load_scales_stacked(w3_sc, w3_scales, nc.sync)
 
         def gather(name, window, idx, dtype):
@@ -155,6 +164,7 @@ def tile_list_creep_life_weave_kernel(
         def slot(wide, t):
             return wide[:, t * S : (t + 1) * S]
 
+        amp_t = turn_natural("amp_t0", amp_rows, 1, LAST) + [amp_dealt]
         v2_sc = [gather("v2_sc%d" % g, tab2_sc[:, g * TC : (g + 1) * TC], idx2, U8) for g in range(PASSES)]
         v2_w = [gather("v2_w%d" % g, tab2_w[g][:], idx2, U32) for g in range(PASSES)]
         v_w = [gather("v_w0", tab_w[0][:], idx1, U32)]
@@ -352,6 +362,8 @@ def tile_list_creep_life_weave_kernel(
             weigh_cool(i)
             scatter_cool(i)
         round_w1_natural()
+        c1_natural, c0_natural = turn_natural("c_t0", c_rows, 2, LAST)
+        c1_t, c0_t = [c1_natural, c1_dealt], [c0_natural, c0_dealt]
         quantise_w1(0)
         weigh_cool(6)
         scatter_cool(6, "w1_raw10")
@@ -374,7 +386,7 @@ def tile_list_creep_life_weave_kernel(
         z_turned = [tile("z_turned%d" % h, [P, PACK, KP], BF16, ("tab2_w1", "wg2_rows")[h]) for h in range(2)]
         for i in range(PACK):
             if i:
-                hot_products(i, {1: "weight6", 2: "w1_raw00"}.get(i))
+                hot_products(i, {1: "weight6", 3: "shifted2"}.get(i), "w1_raw00" if i == 2 else None)
                 scatter_hot(i)
             turn_plane(i, z_turned)
         z0 = tile("z0", [P, PACK * T2], BF16, "turned")

@@ -101,7 +101,7 @@ def tile_list_creep_life_weave_kernel(
         def load_spread(name, src, after=None):
             dst = tile(name, [P, PACK * S], F32, after)
             rows = src.rearrange("(u t) j -> u (t j)", t=PACK)
-            for q in range(QUADS):
+            for q in (0, 2, 1, 3):
                 nc.sync.dma_start(dst[QUAD * q : QUAD * (q + 1), :], rows)
             return dst
 
@@ -121,30 +121,30 @@ def tile_list_creep_life_weave_kernel(
         w2_sc = tile("w2_sc", [P, PASSES * H], U8)
         tab_sc = tile("tab_sc", [P, T], U8)
         w3_sc = tile("w3_sc", [P, N], U8)
-        idx2 = load_list("idx2", offs2)
-        amp_rows = load_natural("amp_rows", [amp], nc.sync)
+        amp_rows = load_natural("amp_rows", [amp], nc.gpsimd)
         identity = tile("identity", [P, P], F32)
         make_identity(nc, identity[:])
         c_rows = load_natural("c_rows", [c1, c0], nc.gpsimd)
         amp_dealt, c1_dealt, c0_dealt = load_dealt("amp_t1", amp), load_dealt("c1_t1", c1), load_dealt("c0_t1", c0)
         nc.vector.memset(tab2_sc[:].bitcast(I32), 0)
-        nc.vector.memset(tab_sc[:].bitcast(I32), 0)
         nc.vector.memset(w2_sc[:].bitcast(I32), 0)
+        nc.vector.memset(tab_sc[:].bitcast(I32), 0)
         nc.vector.memset(w3_sc[:].bitcast(I32), 0)
         warm = tile("warm", [P, 2], F32)
         nc.vector.memset(warm[:, 0:1], 1.0)
         nc.scalar.activation(warm[:, 1:2], warm[:, 0:1], ACT.Abs_reciprocal_sqrt)
 
+        idx2 = load_list("idx2", offs2)
         load_scales_side_by_side(tab2_sc, tab2_scales)
-        wg2_rows = load_rows("wg2_rows", wg2)
         tab2_w = [load_table("tab2_w%d" % g, tab2_words[g]) for g in range(PASSES)]
+        wg2_rows = load_rows("wg2_rows", wg2)
         w2_w = [load_w2(0)]
         load_scales_side_by_side(w2_sc, w2_scales)
         tab_w = [load_table("tab_w0", tab_words[0])]
         idx1 = load_list("idx1", offs)
+        tab_w.append(load_table("tab_w1", tab_words[1]))
         idx4 = load_list("idx4", offs4)
         load_scales_stacked(tab_sc, tab_scales, nc.sync)
-        tab_w.append(load_table("tab_w1", tab_words[1]))
         w2_w.append(load_w2(1))
         wg2_spread = load_spread("wg2_spread", wg2)
         w1_raw = {(g, a): load_w1(g, a) for a in range(PASSES) for g in range(PASSES)}
@@ -152,8 +152,8 @@ def tile_list_creep_life_weave_kernel(
         idx3 = load_list("idx3", offs3)
         load_scales_stacked(w3_sc, w3_scales, nc.sync)
 
-        def gather(name, window, idx, dtype):
-            dst = tile(name, [P, S], dtype)
+        def gather(name, window, idx, dtype, after=None):
+            dst = tile(name, [P, S], dtype, after)
             nc.vector.tensor_copy(dst[:], window.indirect(idx[:]))
             return dst
 
@@ -167,9 +167,7 @@ def tile_list_creep_life_weave_kernel(
         amp_t = turn_natural("amp_t0", amp_rows, 1, LAST) + [amp_dealt]
         v2_sc = [gather("v2_sc%d" % g, tab2_sc[:, g * TC : (g + 1) * TC], idx2, U8) for g in range(PASSES)]
         v2_w = [gather("v2_w%d" % g, tab2_w[g][:], idx2, U32) for g in range(PASSES)]
-        v_w = [gather("v_w0", tab_w[0][:], idx1, U32)]
-        v_sc = gather("v_sc", tab_sc[:], idx1, U8)
-        v_w.append(gather("v_w1", tab_w[1][:], idx1, U32))
+        v_w = [gather("v_w%d" % g, tab_w[g][:], idx1, U32) for g in range(PASSES)]
 
         cool, pages, hot, hot_acc, feature, shifted = {}, {}, {}, {}, {}, {}
         grouped, w1_w, w1_sc, z_w, z_sc, squares, roots = {}, {}, {}, {}, {}, {}, {}
@@ -186,7 +184,7 @@ def tile_list_creep_life_weave_kernel(
 
         def cool_direct(i, parts):
             response = tile("response%d" % i, [P, S], F32)
-            root = tile("root%d" % i, [P, S], F32, "root%d" % (i % 2))
+            root = tile("root%d" % i, [P, S], F32, "root0" if i == 2 else None)
             width = S // parts
             cuts = [slice(h * width, (h + 1) * width) for h in range(parts)]
             accs = [bank(i + PACK * h, "b%d%d" % (i, h)) for h in range(parts)]
@@ -351,6 +349,7 @@ def tile_list_creep_life_weave_kernel(
             cool_direct(i, 2 if i == 0 else 1)
             scatter_cool(i)
 
+        v_sc = gather("v_sc", tab_sc[:], idx1, U8, after="root1")
         turned = tile("turned", [P, PACK * S], F32)
         for s in range(S // P):
             cool_turned(s, turned)
@@ -392,7 +391,7 @@ def tile_list_creep_life_weave_kernel(
         z0 = tile("z0", [P, PACK * T2], BF16, "turned")
         weave_turned(z0, z_turned)
 
-        z1 = [tile("z1%d" % q, [P, CHUNK, PACK], BF16, ("v2_w0", "v2_w1", "root1", "amp_t0")[q]) for q in range(CHUNKS)]
+        z1 = [tile("z1%d" % q, [P, CHUNK, PACK], BF16, ("v2_w0", "v2_w1", "root3", "amp_t0")[q]) for q in range(CHUNKS)]
 
         def round_plane(i):
             for q in range(CHUNKS):

@@ -121,12 +121,12 @@ def tile_list_creep_life_weave_kernel(
         w2_sc = tile("w2_sc", [P, PASSES * H], U8)
         tab_sc = tile("tab_sc", [P, T], U8)
         w3_sc = tile("w3_sc", [P, N], U8)
+        nc.gpsimd.memset(tab2_sc[:].bitcast(I32), 0)
         amp_rows = load_natural("amp_rows", [amp], nc.gpsimd)
         identity = tile("identity", [P, P], F32)
         make_identity(nc, identity[:])
         c_rows = load_natural("c_rows", [c1, c0], nc.gpsimd)
         amp_dealt, c1_dealt, c0_dealt = load_dealt("amp_t1", amp), load_dealt("c1_t1", c1), load_dealt("c0_t1", c0)
-        nc.vector.memset(tab2_sc[:].bitcast(I32), 0)
         nc.vector.memset(w2_sc[:].bitcast(I32), 0)
         nc.vector.memset(tab_sc[:].bitcast(I32), 0)
         nc.vector.memset(w3_sc[:].bitcast(I32), 0)
@@ -136,14 +136,15 @@ def tile_list_creep_life_weave_kernel(
 
         idx2 = load_list("idx2", offs2)
         load_scales_side_by_side(tab2_sc, tab2_scales)
-        tab2_w = [load_table("tab2_w%d" % g, tab2_words[g]) for g in range(PASSES)]
-        wg2_rows = load_rows("wg2_rows", wg2)
-        w2_w = [load_w2(0)]
         load_scales_side_by_side(w2_sc, w2_scales)
+        tab2_w = [load_table("tab2_w0", tab2_words[0])]
+        wg2_rows = load_rows("wg2_rows", wg2)
+        tab2_w.append(load_table("tab2_w1", tab2_words[1]))
+        w2_w = [load_w2(0)]
         tab_w = [load_table("tab_w0", tab_words[0])]
         idx1 = load_list("idx1", offs)
-        tab_w.append(load_table("tab_w1", tab_words[1]))
         idx4 = load_list("idx4", offs4)
+        tab_w.append(load_table("tab_w1", tab_words[1]))
         load_scales_stacked(tab_sc, tab_scales, nc.sync)
         w2_w.append(load_w2(1))
         wg2_spread = load_spread("wg2_spread", wg2)
@@ -152,9 +153,16 @@ def tile_list_creep_life_weave_kernel(
         idx3 = load_list("idx3", offs3)
         load_scales_stacked(w3_sc, w3_scales, nc.sync)
 
-        def gather(name, window, idx, dtype, after=None):
+        def pieces(parts):
+            return [slice(h * S // parts, (h + 1) * S // parts) for h in range(parts)]
+
+        def entries(idx, cols):
+            return idx[:, cols.start // 16 : cols.stop // 16]
+
+        def gather(name, window, idx, dtype, after=None, parts=1):
             dst = tile(name, [P, S], dtype, after)
-            nc.vector.tensor_copy(dst[:], window.indirect(idx[:]))
+            for cols in pieces(parts):
+                nc.vector.tensor_copy(dst[:, cols], window.indirect(entries(idx, cols)))
             return dst
 
         def column(coefficients, i):
@@ -166,8 +174,8 @@ def tile_list_creep_life_weave_kernel(
 
         amp_t = turn_natural("amp_t0", amp_rows, 1, LAST) + [amp_dealt]
         v2_sc = [gather("v2_sc%d" % g, tab2_sc[:, g * TC : (g + 1) * TC], idx2, U8) for g in range(PASSES)]
-        v2_w = [gather("v2_w%d" % g, tab2_w[g][:], idx2, U32) for g in range(PASSES)]
-        v_w = [gather("v_w%d" % g, tab_w[g][:], idx1, U32) for g in range(PASSES)]
+        v2_w = [gather("v2_w%d" % g, tab2_w[g][:], idx2, U32, parts=g + 1) for g in range(PASSES)]
+        v_w = [gather("v_w0", tab_w[0][:], idx1, U32)]
 
         cool, pages, hot, hot_acc, feature, shifted = {}, {}, {}, {}, {}, {}
         grouped, w1_w, w1_sc, z_w, z_sc, squares, roots = {}, {}, {}, {}, {}, {}, {}
@@ -202,7 +210,7 @@ def tile_list_creep_life_weave_kernel(
             for acc, cols in zip(accs, cuts):
                 inverse_root(acc[:, 0:width], i, root[:, cols], cols)
                 nc.scalar.activation(response[:, cols], root[:, cols], ACT.Square)
-            factors[i] = (response[:], cool[i][:])
+            factors[i] = (response, cool[i])
 
         def cool_turned(s, turned):
             acc = bank(PACK + s, "b_turned%d" % s)
@@ -235,11 +243,14 @@ def tile_list_creep_life_weave_kernel(
             nc.scalar.activation(weight[:], slot(wg2_spread, i % PACK), ACT.Copy, scale=column(amp_t, i))
             response = tile("response%d" % i, [P, S], F32)
             nc.scalar.activation(response[:], backs[i][:], ACT.Square)
-            factors[i] = (response[:], weight[:])
+            factors[i] = (response, weight)
 
-        def scatter_cool(i, after=None):
+        def scatter_cool(i, after=None, parts=1):
             pages[i] = tile("page%d" % i, [P, T2], F32, after)
-            nc.vector.tensor_tensor(pages[i][:].indirect(idx4[:]), *factors[i], MULT)
+            for cols in pieces(parts):
+                nc.vector.tensor_tensor(
+                    pages[i][:].indirect(entries(idx4, cols)), factors[i][0][:, cols], factors[i][1][:, cols], MULT
+                )
 
         def round_w1_natural():
             grouped[0] = tile("grouped0", [P, PASSES, KP, PACK], BF16, "turned")
@@ -346,10 +357,12 @@ def tile_list_creep_life_weave_kernel(
         for i in range(PACK):
             weigh_rows(i)
         for i in range(PACK):
-            cool_direct(i, 2 if i == 0 else 1)
-            scatter_cool(i)
+            parts = 2 if i == 0 else 1
+            cool_direct(i, parts)
+            scatter_cool(i, parts=parts)
 
-        v_sc = gather("v_sc", tab_sc[:], idx1, U8, after="root1")
+        v_w.append(gather("v_w1", tab_w[1][:], idx1, U32, after="root1"))
+        v_sc = gather("v_sc", tab_sc[:], idx1, U8, after="root3")
         turned = tile("turned", [P, PACK * S], F32)
         for s in range(S // P):
             cool_turned(s, turned)
@@ -391,7 +404,7 @@ def tile_list_creep_life_weave_kernel(
         z0 = tile("z0", [P, PACK * T2], BF16, "turned")
         weave_turned(z0, z_turned)
 
-        z1 = [tile("z1%d" % q, [P, CHUNK, PACK], BF16, ("v2_w0", "v2_w1", "root3", "amp_t0")[q]) for q in range(CHUNKS)]
+        z1 = [tile("z1%d" % q, [P, CHUNK, PACK], BF16, ("v2_w0", "v2_w1", "weight4", "amp_t0")[q]) for q in range(CHUNKS)]
 
         def round_plane(i):
             for q in range(CHUNKS):

@@ -27,10 +27,12 @@ QUADS = P // QUAD
 SCALE_ROWS = 4
 PLANES = PASSES * PACK
 LAST = PLANES - 1
-HALF = T2 // 2
-CHUNK = 256
-CHUNKS = T2 // CHUNK
-BANKS = 2 * CHUNKS
+LEAD = 256
+PAIR = 2 * P
+ROW = 4 * S
+BRIDGE = 5
+CHUNKS = ((0, 128), (128, 256), (256, 512), (512, 768), (768, 1024))
+DIRECT = 256
 
 
 def tile_list_creep_life_weave_kernel(
@@ -42,9 +44,21 @@ def tile_list_creep_life_weave_kernel(
         lists = ctx.enter_context(tc.tile_pool(name="lists", bufs=1))
         sbuf = ctx.enter_context(tc.tile_pool(name="sbuf", bufs=1))
         psum = ctx.enter_context(tc.psum_pool(name="psum", bufs=1))
+        spots = {"free": 0}
 
-        def tile(name, shape, dtype, after=None):
-            return sbuf.tile(shape, dtype, name=name, tag=after or name, align_bytes=64)
+        def reserve(name, size):
+            spots[name] = spots["free"]
+            spots["free"] = spots["free"] + (size + 63) // 64 * 64
+
+        def tile(name, shape, dtype, on=None, skip=0, room=0):
+            if on is None:
+                size = 4 if dtype in (F32, U32) else 2 if dtype == BF16 else 1
+                for extent in shape[1:]:
+                    size = size * extent
+                reserve(name, size + room)
+            else:
+                spots[name] = spots[on] + skip
+            return sbuf.tile(shape, dtype, name=name, align_bytes=64, offset=spots[name])
 
         def bank(b, name):
             return psum.tile([P, S], F32, name=name, tag="bank%d" % b)
@@ -54,9 +68,9 @@ def tile_list_creep_life_weave_kernel(
             nc.sync.dma_start(dst[:], src)
             return dst
 
-        def load_table(name, src, after=None):
-            dst = tile(name, [P, src.shape[1]], U32, after)
-            nc.sync.dma_start(dst[:].bitcast(I32), src.rearrange("p c i -> p (c i)").bitcast(I32))
+        def load_table(name, src, columns, queue, on=None, skip=0):
+            dst = tile(name, [P, columns], U32, on, skip)
+            queue.dma_start(dst[:].bitcast(I32), src.rearrange("p c i -> p (c i)").bitcast(I32))
             return dst
 
         def load_scales_side_by_side(dst, src):
@@ -67,9 +81,9 @@ def tile_list_creep_life_weave_kernel(
                     src[:, SCALE_ROWS * q : SCALE_ROWS * (q + 1), :].bitcast(I32).rearrange("g r c -> r g c"),
                 )
 
-        def load_scales_stacked(dst, src, queue):
+        def load_scales_stacked(dst, src):
             for q in range(QUADS):
-                queue.dma_start(
+                nc.sync.dma_start(
                     dst[QUAD * q : QUAD * q + PASSES * SCALE_ROWS, :].bitcast(I32),
                     src[:, SCALE_ROWS * q : SCALE_ROWS * (q + 1), :].bitcast(I32),
                 )
@@ -79,12 +93,8 @@ def tile_list_creep_life_weave_kernel(
             nc.gpsimd.dma_start(dst[:], src[KP:H].rearrange("(p t) -> p t", t=PACK))
             return dst[:]
 
-        def load_natural(name, sources, queue):
-            rows = tile(name, [P, P], F32)
-            nc.gpsimd.memset(rows[:], 0.0)
-            for k, src in enumerate(sources):
-                queue.dma_start(rows[PACK * k : PACK * (k + 1), :], src[0:KP].rearrange("(t p) -> t p", t=PACK))
-            return rows
+        def load_natural(rows, k, src, queue):
+            queue.dma_start(rows[PACK * k : PACK * (k + 1), :], src[0:KP].rearrange("(t p) -> t p", t=PACK))
 
         def turn_natural(name, rows, count, b):
             acc = bank(b, name + "_turned")
@@ -93,14 +103,14 @@ def tile_list_creep_life_weave_kernel(
             nc.scalar.copy(dst[:], acc[:, 0 : count * PACK])
             return [dst[:, PACK * k : PACK * (k + 1)] for k in range(count)]
 
-        def load_rows(name, src, after=None):
-            dst = tile(name, [P, S], F32, after)
+        def load_rows(name, src):
+            dst = tile(name, [P, S], F32)
             nc.sync.dma_start(dst[:], src)
             return dst
 
-        def load_spread(name, src, after=None):
-            dst = tile(name, [P, PACK * S], F32, after)
-            rows = src.rearrange("(u t) j -> u (t j)", t=PACK)
+        def load_spread(name, src, first, count):
+            dst = tile(name, [P, count * S], F32)
+            rows = src.rearrange("(u t) j -> u (t j)", t=PACK)[:, first * S : (first + count) * S]
             for q in (0, 2, 1, 3):
                 nc.sync.dma_start(dst[QUAD * q : QUAD * (q + 1), :], rows)
             return dst
@@ -111,59 +121,85 @@ def tile_list_creep_life_weave_kernel(
             nc.sync.dma_start(dst[:].bitcast(I32), src.bitcast(I32).rearrange("g p c -> p g c"))
             return dst
 
-        def load_w1(g, a):
-            dst = tile("w1_raw%d%d" % (g, a), [P, PACK, KP], F32)
-            src = w1[g * KP : (g + 1) * KP, a * KP : (a + 1) * KP]
-            nc.sync.dma_start(dst[:], src.rearrange("(p j) c -> p j c", j=PACK))
+        def load_w1(dst, g, first, count):
+            src = w1[g * KP : (g + 1) * KP, first : first + count]
+            nc.sync.dma_start(dst, src.rearrange("(p j) c -> p j c", j=PACK))
+
+        def load_w1_pair(h):
+            dst = tile("w1_pair%d" % h, [P, PASSES, PACK, PAIR], F32)
+            for g in range(PASSES):
+                load_w1(dst[:, g], g, h * PAIR, PAIR)
+            return dst
+
+        def load_w1_dealt(g):
+            dst = tile("w1_dealt%d" % g, [P, PACK, KP], F32)
+            load_w1(dst[:], g, KP, KP)
             return dst
 
         tab2_sc = tile("tab2_sc", [P, PASSES * TC], U8)
-        w2_sc = tile("w2_sc", [P, PASSES * H], U8)
+        w2_sc = [tile("w2_sc%d" % a, [P, PASSES * KP], U8) for a in range(PASSES)]
         tab_sc = tile("tab_sc", [P, T], U8)
         w3_sc = tile("w3_sc", [P, N], U8)
-        nc.gpsimd.memset(tab2_sc[:].bitcast(I32), 0)
-        amp_rows = load_natural("amp_rows", [amp], nc.gpsimd)
+        reserve("behind_amp", 4 * (S - LEAD) + (S - LEAD) + 4 * T)
+        amp_rows = tile("amp_rows", [P, P], F32, "behind_amp", 4 * (S - LEAD) - P)
+        c_rows = tile("c_rows", [P, P], F32)
         identity = tile("identity", [P, P], F32)
+        nc.gpsimd.memset(tab2_sc[:].bitcast(I32), 0)
+        nc.gpsimd.memset(amp_rows[:], 0.0)
         make_identity(nc, identity[:])
-        c_rows = load_natural("c_rows", [c1, c0], nc.gpsimd)
-        amp_dealt, c1_dealt, c0_dealt = load_dealt("amp_t1", amp), load_dealt("c1_t1", c1), load_dealt("c0_t1", c0)
-        nc.vector.memset(w2_sc[:].bitcast(I32), 0)
-        nc.vector.memset(tab_sc[:].bitcast(I32), 0)
-        nc.vector.memset(w3_sc[:].bitcast(I32), 0)
+        nc.gpsimd.memset(c_rows[:], 0.0)
+        amp_dealt = load_dealt("amp_dealt", amp)
+        load_natural(c_rows, 0, c1, nc.gpsimd)
+        load_natural(c_rows, 1, c0, nc.gpsimd)
+        c1_dealt, c0_dealt = load_dealt("c1_dealt", c1), load_dealt("c0_dealt", c0)
+        sign = tile("sign", [P, PACK], F32)
+        nc.gpsimd.tensor_scalar(sign[:], amp_dealt, 0.0, 2.0, mybir.AluOpType.is_ge, MULT)
+        nc.gpsimd.tensor_scalar(sign[:], sign[:], -1.0, 1.0, ADD, MULT)
+        size = tile("size", [P, PACK], F32)
+        nc.gpsimd.tensor_tensor(size[:], amp_dealt, sign[:], MULT)
+        half = tile("half", [P, PACK], F32)
+        nc.gpsimd.memset(half[:], 0.5)
+        root_size = tile("root_size", [P, PACK], F32)
+        nc.gpsimd.tensor_tensor(root_size[:], size[:], half[:], mybir.AluOpType.pow)
+        signed_c1 = tile("signed_c1", [P, PACK], F32)
+        nc.gpsimd.tensor_tensor(signed_c1[:], c1_dealt, sign[:], MULT)
+        for zeroed in (w2_sc[0], w2_sc[1], tab_sc, w3_sc):
+            nc.vector.memset(zeroed[:].bitcast(I32), 0)
         warm = tile("warm", [P, 2], F32)
         nc.vector.memset(warm[:, 0:1], 1.0)
         nc.scalar.activation(warm[:, 1:2], warm[:, 0:1], ACT.Abs_reciprocal_sqrt)
 
         idx2 = load_list("idx2", offs2)
         load_scales_side_by_side(tab2_sc, tab2_scales)
-        load_scales_side_by_side(w2_sc, w2_scales)
-        tab2_w = [load_table("tab2_w0", tab2_words[0])]
-        wg2_rows = load_rows("wg2_rows", wg2)
-        tab2_w.append(load_table("tab2_w1", tab2_words[1]))
+        tab2_w = [load_table("tab2_w%d" % g, tab2_words[g], TC, nc.sync) for g in range(PASSES)]
+        load_natural(amp_rows, 0, amp, nc.sync)
+        load_scales_side_by_side(w2_sc[0], w2_scales[:, :, 0:KP])
         w2_w = [load_w2(0)]
-        tab_w = [load_table("tab_w0", tab_words[0])]
+        wg2_rows = load_rows("wg2_rows", wg2)
         idx1 = load_list("idx1", offs)
         idx4 = load_list("idx4", offs4)
-        tab_w.append(load_table("tab_w1", tab_words[1]))
-        load_scales_stacked(tab_sc, tab_scales, nc.sync)
+        tab_w1 = load_table("tab_w1", tab_words[1], T, nc.sync)
         w2_w.append(load_w2(1))
-        wg2_spread = load_spread("wg2_spread", wg2)
-        w1_raw = {(g, a): load_w1(g, a) for a in range(PASSES) for g in range(PASSES)}
+        load_scales_side_by_side(w2_sc[1], w2_scales[:, :, KP:H])
+        wg2_spread = [load_spread("wg2_spread0", wg2, 0, 2)]
+        load_scales_stacked(tab_sc, tab_scales)
+        wg2_spread.append(load_spread("wg2_spread1", wg2, 2, 2))
+        w1_pair = [load_w1_pair(h) for h in range(2)]
         wg1_rows = load_rows("wg1_rows", wg1)
         idx3 = load_list("idx3", offs3)
-        load_scales_stacked(w3_sc, w3_scales, nc.sync)
+        w1_dealt = [load_w1_dealt(g) for g in range(PASSES)]
+        wg1_spread = load_spread("wg1_spread", wg1, 0, PACK)
+        load_scales_stacked(w3_sc, w3_scales)
+        w3_w = tile("w3_w", [P, PASSES, N], U32)
+        nc.sync.dma_start(w3_w[:].bitcast(I32), w3_words.rearrange("g p c i -> p g (c i)").bitcast(I32))
 
-        def pieces(parts):
-            return [slice(h * S // parts, (h + 1) * S // parts) for h in range(parts)]
+        lead, rest, whole = slice(0, LEAD), slice(LEAD, S), slice(0, S)
 
         def entries(idx, cols):
             return idx[:, cols.start // 16 : cols.stop // 16]
 
-        def gather(name, window, idx, dtype, after=None, parts=1):
-            dst = tile(name, [P, S], dtype, after)
-            for cols in pieces(parts):
-                nc.vector.tensor_copy(dst[:, cols], window.indirect(entries(idx, cols)))
-            return dst
+        def gather(dst, window, idx, cols):
+            nc.vector.tensor_copy(dst, window.indirect(entries(idx, cols)))
 
         def column(coefficients, i):
             a, t = divmod(i, PACK)
@@ -172,141 +208,214 @@ def tile_list_creep_life_weave_kernel(
         def slot(wide, t):
             return wide[:, t * S : (t + 1) * S]
 
-        amp_t = turn_natural("amp_t0", amp_rows, 1, LAST) + [amp_dealt]
-        v2_sc = [gather("v2_sc%d" % g, tab2_sc[:, g * TC : (g + 1) * TC], idx2, U8) for g in range(PASSES)]
-        v2_w = [gather("v2_w%d" % g, tab2_w[g][:], idx2, U32, parts=g + 1) for g in range(PASSES)]
-        v_w = [gather("v_w0", tab_w[0][:], idx1, U32)]
+        v2_w0_lead = tile("v2_w0_lead", [P, LEAD], U32)
+        v2_w1 = tile("v2_w1", [P, S], U32)
+        v2_sc0 = tile("v2_sc0", [P, S], U8)
+        v2_sc1_lead = tile("v2_sc1_lead", [P, LEAD], U8)
+        gather(v2_sc0[:], tab2_sc[:, 0:TC], idx2, whole)
+        gather(v2_sc1_lead[:], tab2_sc[:, TC : 2 * TC], idx2, lead)
+        gather(v2_w0_lead[:], tab2_w[0][:], idx2, lead)
+        gather(v2_w1[:, lead], tab2_w[1][:], idx2, lead)
+        gather(v2_w1[:, rest], tab2_w[1][:], idx2, rest)
+        amp_t = turn_natural("amp_natural", amp_rows, 1, 4)
+        tab_w = [load_table("tab_w0", tab_words[0], T, nc.scalar, "behind_amp", 5 * (S - LEAD)), tab_w1]
+        v2_w0_rest = tile("v2_w0_rest", [P, S - LEAD], U32, "behind_amp")
+        gather(v2_w0_rest[:], tab2_w[0][:], idx2, rest)
+        v2_sc1_rest = tile("v2_sc1_rest", [P, S - LEAD], U8, "behind_amp", 4 * (S - LEAD))
+        gather(v2_sc1_rest[:], tab2_sc[:, TC : 2 * TC], idx2, rest)
 
-        cool, pages, hot, hot_acc, feature, shifted = {}, {}, {}, {}, {}, {}
-        grouped, w1_w, w1_sc, z_w, z_sc, squares, roots = {}, {}, {}, {}, {}, {}, {}
+        def v2_words(g, first, last):
+            if g == 1:
+                return v2_w1[:, first:last]
+            if last <= LEAD:
+                return v2_w0_lead[:, first:last]
+            return v2_w0_rest[:, first - LEAD : last - LEAD]
 
-        def inverse_root(acc, k, dst_view, cols=slice(0, S), shape=lambda view: view):
-            if cols.start == 0:
-                squares[k] = tile("square%d" % k, [P, S], F32, "root0" if k == 1 else ("wg2_rows", "amp_t0")[k % 2])
-            nc.scalar.activation(squares[k][:, cols], acc, ACT.Square)
-            nc.scalar.activation(dst_view, shape(squares[k][:, cols]), ACT.Abs_reciprocal_sqrt, bias=1.0)
+        def v2_scales(g, first, last):
+            if g == 0:
+                return v2_sc0[:, first:last]
+            if last <= LEAD:
+                return v2_sc1_lead[:, first:last]
+            return v2_sc1_rest[:, first - LEAD : last - LEAD]
 
-        def weigh_rows(i):
-            cool[i] = tile("cool%d" % i, [P, S], F32)
-            nc.scalar.activation(cool[i][:], wg2_rows[:], ACT.Copy, scale=column(amp_t, i))
+        pages, responses, sums, hot, shifted, feature = {}, {}, {}, {}, {}, {}
+        w1_w, w1_sc = {}, {}
 
-        def cool_direct(i, parts):
+        def cool_product(i, b, cols):
+            acc = bank(b, "b%d_%d" % (i, cols.start))
+            cuts = [(g, cols.start, cols.stop) for g in range(PASSES)]
+            if cols == whole:
+                cuts = [(g, c, c + LEAD) for g in range(PASSES) for c in (0, LEAD)]
+            for n, (g, c, d) in enumerate(cuts):
+                nc.tensor.matmul_mx(
+                    out=acc[:, c - cols.start : d - cols.start],
+                    lhsT=w2_w[0][:, g, 2 * i * P : 2 * (i + 1) * P].bitcast(E2M1),
+                    lhsT_scale=w2_sc[0][:, g * KP + i * P : g * KP + (i + 1) * P],
+                    rhs=v2_words(g, c, d).bitcast(E4M3),
+                    rhs_scale=v2_scales(g, c, d),
+                    start=(n == 0),
+                    stop=(n == len(cuts) - 1),
+                )
+            return acc[:, 0 : cols.stop - cols.start]
+
+        def reciprocal(response, acc, square, root):
+            nc.scalar.activation(square, acc, ACT.Square)
+            nc.scalar.activation(root, square, ACT.Abs_reciprocal_sqrt, bias=1.0)
+            nc.scalar.activation(response, root, ACT.Square)
+
+        def scatter_fused(i, cols, values, weights):
+            nc.vector.tensor_tensor(pages[i][:].indirect(entries(idx4, cols)), values, weights, MULT)
+
+        reserve("second_piece", 3 * ROW // 2)
+        response0 = tile("response0", [P, S], F32)
+        pages[0] = tile("page0", [P, T2], F32)
+        acc = cool_product(0, 0, lead)
+        square = tile("square0_lead", [P, LEAD], F32)
+        root = tile("root0_lead", [P, LEAD], F32, "second_piece", 3 * ROW // 4)
+        weight = tile("weight0_lead", [P, LEAD], F32)
+        nc.scalar.activation(weight[:], wg2_rows[:, lead], ACT.Copy, scale=column(amp_t, 0))
+        reciprocal(response0[:, lead], acc, square[:], root[:])
+        scatter_fused(0, lead, response0[:, lead], weight[:])
+        v_w = [tile("v_w%d" % g, [P, S], U32) for g in range(PASSES)]
+        gather(v_w[0][:], tab_w[0][:], idx1, whole)
+        acc = cool_product(0, 1, rest)
+        square = tile("square0_rest", [P, S - LEAD], F32, "second_piece", ROW // 2)
+        weight = tile("weight0_rest", [P, S - LEAD], F32, "second_piece", ROW)
+        root = tile("root0_rest", [P, S - LEAD], F32)
+        nc.scalar.activation(weight[:], wg2_rows[:, rest], ACT.Copy, scale=column(amp_t, 0))
+        reciprocal(response0[:, rest], acc, square[:], root[:])
+        scatter_fused(0, rest, response0[:, rest], weight[:])
+        gather(v_w[1][:], tab_w[1][:], idx1, whole)
+
+        for i in range(1, PACK):
+            acc = cool_product(i, (i + 1) % PACK, whole)
+            square = tile("square%d" % i, [P, S], F32, "second_piece")
+            root = tile("root%d" % i, [P, S], F32)
             response = tile("response%d" % i, [P, S], F32)
-            root = tile("root%d" % i, [P, S], F32, "root0" if i == 2 else None)
-            width = S // parts
-            cuts = [slice(h * width, (h + 1) * width) for h in range(parts)]
-            accs = [bank(i + PACK * h, "b%d%d" % (i, h)) for h in range(parts)]
-            for g in range(PASSES):
-                for acc, cols in zip(accs, cuts):
-                    nc.tensor.matmul_mx(
-                        out=acc[:, 0:width],
-                        lhsT=w2_w[0][:, g, 2 * i * P : 2 * (i + 1) * P].bitcast(E2M1),
-                        lhsT_scale=w2_sc[:, g * H + i * P : g * H + (i + 1) * P],
-                        rhs=v2_w[g][:, cols].bitcast(E4M3),
-                        rhs_scale=v2_sc[g][:, cols],
-                        start=(g == 0),
-                        stop=(g == PASSES - 1),
-                    )
-            for acc, cols in zip(accs, cuts):
-                inverse_root(acc[:, 0:width], i, root[:, cols], cols)
-                nc.scalar.activation(response[:, cols], root[:, cols], ACT.Square)
-            factors[i] = (response, cool[i])
+            reciprocal(response[:], acc, square[:], root[:])
+            nc.scalar.activation(response[:], response[:], ACT.Copy, scale=column(amp_t, i))
+            pages[i] = tile("page%d" % i, [P, T2], F32)
+            scatter_fused(i, whole, response[:], wg2_rows[:])
 
-        def cool_turned(s, turned):
-            acc = bank(PACK + s, "b_turned%d" % s)
+        b_turned = []
+        for s in range(S // P):
+            acc = bank((5, 6, 7, 4)[s], "b_turned%d" % s)
+            b_turned.append(acc)
             for g in range(PASSES):
                 nc.tensor.matmul_mx(
                     out=acc[:],
-                    lhsT=v2_w[g][:, s * P : (s + 1) * P].bitcast(E4M3),
-                    lhsT_scale=v2_sc[g][:, s * P : (s + 1) * P],
+                    lhsT=v2_words(g, s * P, (s + 1) * P).bitcast(E4M3),
+                    lhsT_scale=v2_scales(g, s * P, (s + 1) * P),
                     rhs=w2_w[1][:, g, :].bitcast(E2M1),
-                    rhs_scale=w2_sc[:, g * H + KP : g * H + H],
+                    rhs_scale=w2_sc[1][:, g * KP : (g + 1) * KP],
                     start=(g == 0),
                     stop=(g == PASSES - 1),
                 )
-            inverse_root(
-                acc[:], PACK + s,
-                turned[:, s * S : (s + 1) * S].rearrange("p (t m) -> p m t", t=PACK),
-                shape=lambda view: view.rearrange("p (m t) -> p m t", t=PACK),
-            )
+        turned = [tile("turned%d" % h, [P, S // P, 2, P], F32) for h in range(2)]
+        squares = [tile("square_turned%d" % h, [P, S // P, P, 2], F32) for h in range(2)]
 
-        def turn_back(i, turned):
-            t = i % PACK
-            back = bank(t, "back%d" % i)
+        def respond_pair(h):
             for s in range(S // P):
-                c = s * S + t * P
-                nc.tensor.transpose(back[:, s * P : (s + 1) * P], turned[:, c : c + P], identity[:])
-            return back
-
-        def weigh_cool(i):
-            weight = tile("weight%d" % i, [P, S], F32)
-            nc.scalar.activation(weight[:], slot(wg2_spread, i % PACK), ACT.Copy, scale=column(amp_t, i))
-            response = tile("response%d" % i, [P, S], F32)
-            nc.scalar.activation(response[:], backs[i][:], ACT.Square)
-            factors[i] = (response, weight)
-
-        def scatter_cool(i, after=None, parts=1):
-            pages[i] = tile("page%d" % i, [P, T2], F32, after)
-            for cols in pieces(parts):
-                nc.vector.tensor_tensor(
-                    pages[i][:].indirect(entries(idx4, cols)), factors[i][0][:, cols], factors[i][1][:, cols], MULT
+                values = b_turned[s][:].rearrange("p (m t) -> p m t", t=PACK)[:, :, 2 * h : 2 * h + 2]
+                nc.scalar.activation(squares[h][:, s], values, ACT.Square)
+                nc.scalar.activation(
+                    turned[h][:, s].rearrange("p t m -> p m t"), squares[h][:, s], ACT.Abs_reciprocal_sqrt, bias=1.0
                 )
+            for t in (2 * h, 2 * h + 1):
+                back = bank((t + 1) % PACK, "back%d" % t)
+                for s in range(S // P):
+                    nc.tensor.transpose(back[:, s * P : (s + 1) * P], turned[h][:, s, t % 2, :], identity[:])
+                responses[PACK + t] = tile("response%d" % (PACK + t), [P, S], F32)
+                nc.scalar.activation(responses[PACK + t][:], back[:], ACT.Square, scale=root_size[:, t : t + 1])
 
-        def round_w1_natural():
-            grouped[0] = tile("grouped0", [P, PASSES, KP, PACK], BF16, "turned")
+        def spread_weights(i):
+            return slot(wg2_spread[i % PACK // 2], i % 2)
+
+        def scatter_cool(i, on=None):
+            pages[i] = tile("page%d" % i, [P, T2], F32, on)
+            scatter_fused(i, whole, responses[i][:], spread_weights(i))
+
+        respond_pair(0)
+        scatter_cool(4)
+        bridged = tile("bridged", [P, S], F32, "response4")
+        nc.gpsimd.tensor_tensor(bridged[:], responses[BRIDGE][:], spread_weights(BRIDGE), MULT)
+        v_sc = tile("v_sc", [P, S], U8)
+        gather(v_sc[:], tab_sc[:], idx1, whole)
+        respond_pair(1)
+        scatter_cool(6)
+        c1_natural, c0_natural = turn_natural("c_natural", c_rows, 2, 5)
+        c1_t, c0_t = [c1_natural, signed_c1], [c0_natural, c0_dealt]
+
+        def quantise(name, values, width, codes_on=None, codes_skip=0, scales_on=None, scales_skip=0):
+            codes = tile(name + "_w", [P, width], U32, codes_on, codes_skip)
+            scales = tile(name + "_sc", [P, width], U8, scales_on, scales_skip)
+            nc.vector.quantize_mx(out=codes[:].bitcast(E4M3), scales=scales[:], in_=values)
+            return codes, scales
+
+        def prepare_pair(h):
+            grouped = tile("grouped%d" % h, [P, PASSES, PAIR, PACK], BF16)
+            nc.scalar.copy(
+                grouped[:].rearrange("p g (c n) j -> p g c j n", n=PACK),
+                w1_pair[h][:].rearrange("p g j (c n) -> p g c j n", n=PACK),
+            )
+            codes, scales = quantise("w1_pair%d" % h, grouped[:].rearrange("p g c j -> p (g c j)"), PASSES * PAIR)
+            for i in (2 * h, 2 * h + 1):
+                w1_w[i] = [codes[:, g * PAIR + i % 2 * P : g * PAIR + (i % 2 + 1) * P] for g in range(PASSES)]
+                w1_sc[i] = [scales[:, g * PAIR + i % 2 * P : g * PAIR + (i % 2 + 1) * P] for g in range(PASSES)]
+
+        def prepare_dealt():
+            grouped = tile("grouped_dealt", [P, PASSES, KP, PACK], BF16, room=ROW)
             for g in range(PASSES):
                 nc.scalar.copy(
-                    grouped[0][:, g].rearrange("p (c n) j -> p c j n", n=PACK),
-                    w1_raw[g, 0][:].rearrange("p j (c n) -> p c j n", n=PACK),
+                    grouped[:, g].rearrange("p (t m) j -> p m j t", t=PACK),
+                    w1_dealt[g][:].rearrange("p j (m t) -> p m j t", t=PACK),
                 )
-
-        def round_w1_dealt(g):
-            nc.scalar.copy(
-                grouped[1][:, g].rearrange("p (t m) j -> p m j t", t=PACK),
-                w1_raw[g, 1][:].rearrange("p j (m t) -> p m j t", t=PACK),
+            codes, scales = quantise(
+                "w1_dealt", grouped[:].rearrange("p g c j -> p (g c j)"), PASSES * KP, scales_on="weighted1"
             )
+            for t in range(PACK):
+                w1_w[PACK + t] = [codes[:, g * KP + t * P : g * KP + (t + 1) * P] for g in range(PASSES)]
+                w1_sc[PACK + t] = [scales[:, g * KP + t * P : g * KP + (t + 1) * P] for g in range(PASSES)]
 
-        def quantise_w1(a, after=None):
-            w1_w[a] = tile("w1_w%d" % a, [P, PASSES * KP], U32)
-            w1_sc[a] = tile("w1_sc%d" % a, [P, PASSES * KP], U8, after)
-            nc.vector.quantize_mx(
-                out=w1_w[a][:].bitcast(E4M3), scales=w1_sc[a][:], in_=grouped[a][:].rearrange("p g c j -> p (g c j)")
-            )
-
-        def hot_values(i):
-            a, t = divmod(i, PACK)
-            hot_acc[i] = bank(i, "a%d" % i)
+        def hot_sums(i, b, shifted_on, shifted_skip=0):
+            acc = sums[i] = bank(b, "a%d" % i)
             for g in range(PASSES):
-                c = g * KP + t * P
                 nc.tensor.matmul_mx(
-                    out=hot_acc[i][:],
-                    lhsT=w1_w[a][:, c : c + P].bitcast(E4M3),
-                    lhsT_scale=w1_sc[a][:, c : c + P],
+                    out=acc[:],
+                    lhsT=w1_w[i][g].bitcast(E4M3),
+                    lhsT_scale=w1_sc[i][g],
                     rhs=v_w[g][:].bitcast(E4M3),
                     rhs_scale=v_sc[SCALE_ROWS * g : P, :],
                     start=(g == 0),
                     stop=(g == PASSES - 1),
                 )
-            if i == 0:
-                return
-            shifted[i] = tile("shifted%d" % i, [P, S], F32, "cool%d" % t if a else None)
-            nc.scalar.activation(shifted[i][:], hot_acc[i][:], ACT.Identity, bias=column(c1_t, i))
-            feature[i] = tile("feature%d" % i, [P, S], F32, "response%d" % t if a else None)
-            nc.scalar.copy(feature[i][:], hot_acc[i][:])
+            shifted[i] = tile("shifted%d" % i, [P, S], F32, shifted_on, shifted_skip)
+            scale = 1.0 if i < PACK else sign[:, i - PACK : i - PACK + 1]
+            nc.scalar.activation(shifted[i][:], acc[:], ACT.Identity, bias=column(c1_t, i), scale=scale)
 
-        def hot_products(i, weighted_after=None, hot_after=None):
+        def copy_feature(i, on, skip=0):
+            feature[i] = tile("feature%d" % i, [P, S], F32, on, skip)
+            nc.scalar.copy(feature[i][:], sums[i][:])
+
+        def hot_values(i, b, shifted_on, feature_on, feature_skip=0, shifted_skip=0):
+            hot_sums(i, b, shifted_on, shifted_skip)
+            copy_feature(i, feature_on, feature_skip)
+
+        def hot_products(i, on, skip=0):
             weight = wg1_rows[:] if i < PACK else slot(wg1_spread, i % PACK)
-            weighted = tile("weighted%d" % i, [P, S], F32, weighted_after) if weighted_after else shifted[i]
+            weighted = tile("weighted%d" % i, [P, S], F32, on, skip)
             nc.gpsimd.tensor_tensor(weighted[:], shifted[i][:], weight, MULT)
-            hot[i] = tile("hot%d" % i, [P, S], F32, hot_after) if hot_after else feature[i]
+            hot[i] = shifted[i]
             nc.gpsimd.tensor_tensor(hot[i][:], weighted[:], feature[i][:], MULT)
 
         def scatter_hot(i):
             nc.vector.tensor_copy(pages[i][:].indirect(idx3[:]), hot[i][:])
 
-        def turn_plane(i, z_turned):
+        z_turned = [tile("z_turned%d" % h, [P, PACK, KP], BF16, "w1_dealt0", 2 * ROW * h) for h in range(2)]
+
+        def turn_plane(i):
             for h in range(2):
-                acc = bank(2 * (i % 2) + h, "z_turned%d%d" % (i, h))
+                acc = bank((2, 6)[i % 2] + h, "z_turned%d%d" % (i, h))
                 for s in range(PACK):
                     nc.tensor.matmul(
                         acc[:, s * P : (s + 1) * P], column(c0_t, i).to_broadcast([P, P]), identity[:],
@@ -320,10 +429,10 @@ def tile_list_creep_life_weave_kernel(
                     )
                 nc.scalar.copy(z_turned[h][:, :, i * P : (i + 1) * P], acc[:].rearrange("p (s r) -> p s r", s=PACK))
 
-        def weave_turned(z, z_turned):
+        def weave_turned(z):
             words = z[:].bitcast(F32)
             for b in range(PACK):
-                acc = bank(PACK + b, "z_words%d" % b)
+                acc = bank((2, 3, 5, 0)[b], "z_words%d" % b)
                 for s in range(2):
                     pairs = z_turned[b // 2][:, 2 * (b % 2) + s, :].bitcast(F32)
                     for u in range(2):
@@ -334,123 +443,139 @@ def tile_list_creep_life_weave_kernel(
                     acc[:].rearrange("p (s u n) -> p s n u", s=2, u=2),
                 )
 
-        def quantise_z(key, z, after=None):
-            width = z.shape[1] // PACK
-            z_w[key] = tile("z_w%d%d" % key, [P, width], U32, after)
-            z_sc[key] = tile("z_sc%d%d" % key, [P, width], U8)
-            nc.vector.quantize_mx(out=z_w[key][:].bitcast(E4M3), scales=z_sc[key][:], in_=z)
+        prepare_pair(0)
+        scatter_cool(LAST, "w1_pair0")
+        prepare_pair(1)
+        pages[BRIDGE] = tile("page%d" % BRIDGE, [P, T2], F32, "w1_pair1")
+        nc.vector.tensor_copy(pages[BRIDGE][:].indirect(idx4[:]), bridged[:])
+        hot_values(0, 6, "response0", "response6")
+        hot_values(1, 7, "response1", "response2")
+        hot_products(0, "grouped1")
+        scatter_hot(0)
+        hot_products(1, "feature0")
+        scatter_hot(1)
+        prepare_dealt()
+        hot_values(2, 4, "w1_dealt1", "grouped_dealt", 4 * ROW)
+        hot_values(3, 1, "w1_dealt1", "w1_dealt1", 2 * ROW, shifted_skip=ROW)
+        hot_products(2, "feature1")
+        scatter_hot(2)
+        hot_products(3, "grouped_dealt", 4 * ROW - ROW // 2)
+        scatter_hot(3)
+        turn_plane(0)
+        turn_plane(1)
+        hot_values(4, 5, "response3", "root3")
+        hot_values(5, 0, "root2", "root1")
+        hot_values(6, 4, "square_turned0", "square_turned0", ROW)
+        turn_plane(2)
+        hot_sums(LAST, 1, "square_turned1")
+        turn_plane(3)
+        z0 = tile("z0", [P, PACK * T2], BF16, "turned0")
+        weave_turned(z0)
 
-        def score_pass(a, b, key, c):
-            for m in range(2):
-                n0 = (2 * (b % 2) + m) * P
+        z1 = tile("z1", [P, T2, PACK], BF16, "z_turned1", ROW)
+
+        def round_direct(i, first, last):
+            nc.scalar.activation(
+                z1[:, first:last, i % PACK], pages[i][:, first:last], ACT.Identity,
+                bias=column(c0_t, i), scale=sign[:, i - PACK : i - PACK + 1],
+            )
+
+        for i in (4, 5):
+            hot_products(i, "feature%d" % (i - 1))
+            scatter_hot(i)
+            round_direct(i, 0, T2)
+            if i == 4:
+                copy_feature(LAST, "z_turned1")
+        staging = tile("staging", [P, 2, T2 - DIRECT], BF16, "page4")
+        hot_products(6, "feature5")
+        scatter_hot(6)
+        round_direct(6, 0, DIRECT)
+        nc.scalar.activation(staging[:, 0, :], pages[6][:, DIRECT:T2], ACT.Identity, bias=column(c0_t, 6), scale=sign[:, 2:3])
+        hot_products(LAST, "feature6")
+
+        groups = []
+        for q, (first, last) in enumerate(CHUNKS):
+            tiles = S // (last - first)
+            for n0 in range(0, PACK, tiles):
+                groups.append((q, first, last, n0, tiles, bank(len(groups), "score%d" % len(groups))))
+
+        def score_pass(a, group, codes, scales):
+            q, first, last, n0, tiles, acc = group
+            width = last - first
+            for m in range(tiles):
+                rows = slice((n0 + m) * P, (n0 + m + 1) * P)
                 nc.tensor.matmul_mx(
-                    out=scores[b][:, m * CHUNK : (m + 1) * CHUNK],
-                    lhsT=w3_w[:, a, n0 : n0 + P].bitcast(E4M3),
-                    lhsT_scale=w3_sc[SCALE_ROWS * a : P, n0 : n0 + P],
-                    rhs=z_w[key][:, c : c + CHUNK].bitcast(E4M3),
-                    rhs_scale=z_sc[key][:, c : c + CHUNK],
+                    out=acc[:, m * width : (m + 1) * width],
+                    lhsT=w3_w[:, a, rows].bitcast(E4M3),
+                    lhsT_scale=w3_sc[SCALE_ROWS * a : P, rows],
+                    rhs=codes.bitcast(E4M3),
+                    rhs_scale=scales,
                     start=(a == 0 and m == 0),
-                    stop=(a == PASSES - 1 and m == 1),
+                    stop=(a == PASSES - 1 and m == tiles - 1),
                 )
 
-        backs, factors = {}, {}
-        for i in range(PACK):
-            weigh_rows(i)
-        for i in range(PACK):
-            parts = 2 if i == 0 else 1
-            cool_direct(i, parts)
-            scatter_cool(i, parts=parts)
+        def score_first_half(first, last, scales_on):
+            codes, scales = quantise(
+                "z0_%d" % first, z0[:, PACK * first : PACK * last], last - first, "w1_pair1", 2 * ROW + 4 * first, scales_on
+            )
+            for group in groups:
+                if first <= group[1] < last:
+                    cols = slice(group[1] - first, group[2] - first)
+                    score_pass(0, group, codes[:, cols], scales[:, cols])
 
-        v_w.append(gather("v_w1", tab_w[1][:], idx1, U32, after="root1"))
-        v_sc = gather("v_sc", tab_sc[:], idx1, U8, after="root3")
-        turned = tile("turned", [P, PACK * S], F32)
-        for s in range(S // P):
-            cool_turned(s, turned)
-        w3_w = tile("w3_w", [P, PASSES, N], U32, "tab2_w0")
-        nc.sync.dma_start(w3_w[:].bitcast(I32), w3_words.rearrange("g p c i -> p g (c i)").bitcast(I32))
-        for i in range(PACK, PLANES):
-            backs[i] = turn_back(i, turned)
-        for i in (4, 5):
-            weigh_cool(i)
-            scatter_cool(i)
-        round_w1_natural()
-        c1_natural, c0_natural = turn_natural("c_t0", c_rows, 2, LAST)
-        c1_t, c0_t = [c1_natural, c1_dealt], [c0_natural, c0_dealt]
-        quantise_w1(0)
-        weigh_cool(6)
-        scatter_cool(6, "w1_raw10")
-        grouped[1] = tile("grouped1", [P, PASSES, KP, PACK], BF16, "w1_raw00")
-        for g in range(PASSES):
-            round_w1_dealt(g)
-        wg1_spread = load_spread("wg1_spread", wg1, after="w1_raw01")
-        hot_values(0)
-        weighted = tile("weighted0", [P, S], F32)
-        nc.vector.scalar_tensor_tensor(weighted[:], hot_acc[0][:], column(c1_t, 0), wg1_rows[:], ADD, MULT)
-        hot[0] = tile("hot0", [P, S], F32)
-        nc.vector.tensor_tensor(hot[0][:], weighted[:], hot_acc[0][:], MULT)
-        scatter_hot(0)
-        quantise_w1(1)
-        hot_values(1)
-        hot_values(2)
-        weigh_cool(LAST)
-        for i in range(3, PLANES):
-            hot_values(i)
-        z_turned = [tile("z_turned%d" % h, [P, PACK, KP], BF16, ("tab2_w1", "wg2_rows")[h]) for h in range(2)]
-        for i in range(PACK):
-            if i:
-                hot_products(i, {1: "weight6", 3: "shifted2"}.get(i), "w1_raw00" if i == 2 else None)
-                scatter_hot(i)
-            turn_plane(i, z_turned)
-        z0 = tile("z0", [P, PACK * T2], BF16, "turned")
-        weave_turned(z0, z_turned)
+        score_first_half(0, 512, "weighted6")
+        nc.vector.tensor_copy(pages[LAST][:].indirect(entries(idx3, lead)), hot[LAST][:, lead])
+        score_first_half(512, 768, "weighted7")
+        nc.vector.tensor_copy(pages[LAST][:].indirect(entries(idx3, rest)), hot[LAST][:, rest])
+        score_first_half(768, 1024, "shifted7")
 
-        z1 = [tile("z1%d" % q, [P, CHUNK, PACK], BF16, ("v2_w0", "v2_w1", "weight4", "amp_t0")[q]) for q in range(CHUNKS)]
+        nc.vector.tensor_scalar(staging[:, 1, :], pages[LAST][:, DIRECT:T2], sign[:, 3:4], column(c0_t, LAST), MULT, ADD)
 
-        def round_plane(i):
-            for q in range(CHUNKS):
-                values = pages[i][:, q * CHUNK : (q + 1) * CHUNK]
-                if i == LAST - 1:
-                    nc.scalar.activation(
-                        z1[q][:, :, 2:4], values.unsqueeze(2).to_broadcast([P, CHUNK, 2]), ACT.Identity, bias=column(c0_t, i)
-                    )
-                else:
-                    nc.scalar.activation(z1[q][:, :, i % PACK], values, ACT.Identity, bias=column(c0_t, i))
-
-        for i in range(PACK, LAST):
-            hot_products(i, hot_after="root0" if i == LAST - 1 else None)
-            scatter_hot(i)
-            round_plane(i)
-        scatter_cool(LAST, "cool2")
-        hot_products(LAST)
-        quantise_z((0, 0), z0[:], after="response2")
-        scores = [bank(b, "score%d" % b) for b in range(BANKS)]
-        for b in range(BANKS):
-            score_pass(0, b, (0, 0), (b // 2) * CHUNK)
-        scatter_hot(LAST)
-
-        for q in range(CHUNKS):
-            values = pages[LAST][:, q * CHUNK : (q + 1) * CHUNK]
-            if q % 2 == 0:
-                nc.vector.tensor_scalar_add(z1[q][:, :, PACK - 1], values, column(c0_t, LAST))
+        def finish_chunk(q):
+            first, last = CHUNKS[q]
+            if last <= DIRECT:
+                round_direct(LAST, first, last)
             else:
-                nc.scalar.activation(z1[q][:, :, PACK - 1], values, ACT.Identity, bias=column(c0_t, LAST))
-        for q in range(CHUNKS):
-            quantise_z((1, q), z1[q][:].rearrange("p c t -> p (c t)"))
-            for b in (2 * q, 2 * q + 1):
-                score_pass(1, b, (1, q), 0)
-        staged = [tile("staged%d" % s, [P, CHUNKS * S], F32, "tab_w%d" % s) for s in range(2)]
-        for b in range(BANKS):
-            q, lower = divmod(b, 2)
-            result = slot(staged[b // CHUNKS], b % CHUNKS)
-            rows = out[2 * lower * P : 2 * (lower + 1) * P, q * CHUNK : (q + 1) * CHUNK]
+                nc.vector.tensor_copy(
+                    z1[:, first:last, 2:4], staging[:, :, first - DIRECT : last - DIRECT].rearrange("p t c -> p c t")
+                )
+
+        def score_chunk(q):
+            first, last = CHUNKS[q]
+            codes, scales = quantise(
+                "z1_%d" % q, z1[:, first:last, :].rearrange("p c t -> p (c t)"), last - first,
+                "grouped0", 4 * first, "tab2_sc", first,
+            )
+            for group in groups:
+                if group[0] == q:
+                    score_pass(1, group, codes[:], scales[:])
+
+        finish_chunk(0)
+        finish_chunk(1)
+        score_chunk(0)
+        finish_chunk(2)
+        score_chunk(1)
+        score_chunk(2)
+        finish_chunk(3)
+        finish_chunk(4)
+        score_chunk(3)
+        score_chunk(4)
+        for b, (q, first, last, n0, tiles, acc) in enumerate(groups):
+            result = tile("result%d" % b, [P, S], F32, "tab_w%d" % (b // PACK), b % PACK * ROW)
             if b == 0:
-                for m in range(2):
-                    part = slice(m * CHUNK, (m + 1) * CHUNK)
-                    nc.scalar.copy(result[:, part], scores[b][:, part])
-                    nc.sync.dma_start(rows[m * P : (m + 1) * P], result[:, part])
+                for m in (0, 2):
+                    part = slice(m * P, (m + 2) * P)
+                    nc.scalar.copy(result[:, part], acc[:, part])
+                    nc.sync.dma_start(
+                        out[part, first:last].rearrange("(m p) c -> p m c", p=P),
+                        result[:, part].rearrange("p (m c) -> p m c", m=2),
+                    )
                 continue
-            if q >= 1 and lower == 1:
-                nc.vector.tensor_copy(result, scores[b][:])
+            if b in (5, 6):
+                nc.vector.tensor_copy(result[:], acc[:])
             else:
-                nc.scalar.copy(result, scores[b][:])
-            nc.sync.dma_start(rows.rearrange("(m p) c -> p m c", p=P), result.rearrange("p (m c) -> p m c", m=2))
+                nc.scalar.copy(result[:], acc[:])
+            nc.sync.dma_start(
+                out[n0 * P : (n0 + tiles) * P, first:last].rearrange("(m p) c -> p m c", p=P),
+                result[:].rearrange("p (m c) -> p m c", m=tiles),
+            )

@@ -68,9 +68,9 @@ def tile_list_creep_life_weave_kernel(
             nc.sync.dma_start(dst[:], src)
             return dst
 
-        def load_table(name, src, columns, queue, on=None, skip=0):
-            dst = tile(name, [P, columns], U32, on, skip)
-            queue.dma_start(dst[:].bitcast(I32), src.rearrange("p c i -> p (c i)").bitcast(I32))
+        def load_table(name, src, columns):
+            dst = tile(name, [P, columns], U32)
+            nc.sync.dma_start(dst[:].bitcast(I32), src.rearrange("p c i -> p (c i)").bitcast(I32))
             return dst
 
         def load_scales_side_by_side(dst, src):
@@ -88,9 +88,9 @@ def tile_list_creep_life_weave_kernel(
                     src[:, SCALE_ROWS * q : SCALE_ROWS * (q + 1), :].bitcast(I32),
                 )
 
-        def load_dealt(name, src):
+        def load_dealt(name, src, queue=nc.gpsimd):
             dst = tile(name, [P, PACK], F32)
-            nc.gpsimd.dma_start(dst[:], src[KP:H].rearrange("(p t) -> p t", t=PACK))
+            queue.dma_start(dst[:], src[KP:H].rearrange("(p t) -> p t", t=PACK))
             return dst[:]
 
         def load_natural(rows, k, src, queue):
@@ -140,18 +140,14 @@ def tile_list_creep_life_weave_kernel(
         w2_sc = [tile("w2_sc%d" % a, [P, PASSES * KP], U8) for a in range(PASSES)]
         tab_sc = tile("tab_sc", [P, T], U8)
         w3_sc = tile("w3_sc", [P, N], U8)
-        reserve("behind_amp", 4 * (S - LEAD) + (S - LEAD) + 4 * T)
+        reserve("behind_amp", 4 * (S - LEAD) + 3 * P)
         amp_rows = tile("amp_rows", [P, P], F32, "behind_amp", 4 * (S - LEAD) - P)
         c_rows = tile("c_rows", [P, P], F32)
         identity = tile("identity", [P, P], F32)
         nc.gpsimd.memset(tab2_sc[:].bitcast(I32), 0)
         nc.gpsimd.memset(amp_rows[:], 0.0)
+        amp_dealt, c1_dealt = load_dealt("amp_dealt", amp), load_dealt("c1_dealt", c1)
         make_identity(nc, identity[:])
-        nc.gpsimd.memset(c_rows[:], 0.0)
-        amp_dealt = load_dealt("amp_dealt", amp)
-        load_natural(c_rows, 0, c1, nc.gpsimd)
-        load_natural(c_rows, 1, c0, nc.gpsimd)
-        c1_dealt, c0_dealt = load_dealt("c1_dealt", c1), load_dealt("c0_dealt", c0)
         sign = tile("sign", [P, PACK], F32)
         nc.gpsimd.tensor_scalar(sign[:], amp_dealt, 0.0, 2.0, mybir.AluOpType.is_ge, MULT)
         nc.gpsimd.tensor_scalar(sign[:], sign[:], -1.0, 1.0, ADD, MULT)
@@ -165,31 +161,35 @@ def tile_list_creep_life_weave_kernel(
         nc.gpsimd.tensor_tensor(signed_c1[:], c1_dealt, sign[:], MULT)
         for zeroed in (w2_sc[0], w2_sc[1], tab_sc, w3_sc):
             nc.vector.memset(zeroed[:].bitcast(I32), 0)
+        nc.vector.memset(c_rows[:], 0.0)
         warm = tile("warm", [P, 2], F32)
         nc.vector.memset(warm[:, 0:1], 1.0)
         nc.scalar.activation(warm[:, 1:2], warm[:, 0:1], ACT.Abs_reciprocal_sqrt)
 
         idx2 = load_list("idx2", offs2)
         load_scales_side_by_side(tab2_sc, tab2_scales)
-        tab2_w = [load_table("tab2_w%d" % g, tab2_words[g], TC, nc.sync) for g in range(PASSES)]
+        tab2_w = [load_table("tab2_w%d" % g, tab2_words[g], TC) for g in range(PASSES)]
         load_natural(amp_rows, 0, amp, nc.sync)
         load_scales_side_by_side(w2_sc[0], w2_scales[:, :, 0:KP])
         w2_w = [load_w2(0)]
         wg2_rows = load_rows("wg2_rows", wg2)
-        idx1 = load_list("idx1", offs)
         idx4 = load_list("idx4", offs4)
-        tab_w1 = load_table("tab_w1", tab_words[1], T, nc.sync)
+        idx1 = load_list("idx1", offs)
+        tab_w = [load_table("tab_w%d" % g, tab_words[g], T) for g in range(PASSES)]
         w2_w.append(load_w2(1))
         load_scales_side_by_side(w2_sc[1], w2_scales[:, :, KP:H])
         wg2_spread = [load_spread("wg2_spread0", wg2, 0, 2)]
         load_scales_stacked(tab_sc, tab_scales)
         wg2_spread.append(load_spread("wg2_spread1", wg2, 2, 2))
+        load_natural(c_rows, 0, c1, nc.sync)
+        load_natural(c_rows, 1, c0, nc.sync)
         w1_pair = [load_w1_pair(h) for h in range(2)]
         wg1_rows = load_rows("wg1_rows", wg1)
         idx3 = load_list("idx3", offs3)
         w1_dealt = [load_w1_dealt(g) for g in range(PASSES)]
         wg1_spread = load_spread("wg1_spread", wg1, 0, PACK)
         load_scales_stacked(w3_sc, w3_scales)
+        c0_dealt = load_dealt("c0_dealt", c0, nc.sync)
         w3_w = tile("w3_w", [P, PASSES, N], U32)
         nc.sync.dma_start(w3_w[:].bitcast(I32), w3_words.rearrange("g p c i -> p g (c i)").bitcast(I32))
 
@@ -218,7 +218,6 @@ def tile_list_creep_life_weave_kernel(
         gather(v2_w1[:, lead], tab2_w[1][:], idx2, lead)
         gather(v2_w1[:, rest], tab2_w[1][:], idx2, rest)
         amp_t = turn_natural("amp_natural", amp_rows, 1, 4)
-        tab_w = [load_table("tab_w0", tab_words[0], T, nc.scalar, "behind_amp", 5 * (S - LEAD)), tab_w1]
         v2_w0_rest = tile("v2_w0_rest", [P, S - LEAD], U32, "behind_amp")
         gather(v2_w0_rest[:], tab2_w[0][:], idx2, rest)
         v2_sc1_rest = tile("v2_sc1_rest", [P, S - LEAD], U8, "behind_amp", 4 * (S - LEAD))
@@ -276,8 +275,6 @@ def tile_list_creep_life_weave_kernel(
         nc.scalar.activation(weight[:], wg2_rows[:, lead], ACT.Copy, scale=column(amp_t, 0))
         reciprocal(response0[:, lead], acc, square[:], root[:])
         scatter_fused(0, lead, response0[:, lead], weight[:])
-        v_w = [tile("v_w%d" % g, [P, S], U32) for g in range(PASSES)]
-        gather(v_w[0][:], tab_w[0][:], idx1, whole)
         acc = cool_product(0, 1, rest)
         square = tile("square0_rest", [P, S - LEAD], F32, "second_piece", ROW // 2)
         weight = tile("weight0_rest", [P, S - LEAD], F32, "second_piece", ROW)
@@ -285,9 +282,11 @@ def tile_list_creep_life_weave_kernel(
         nc.scalar.activation(weight[:], wg2_rows[:, rest], ACT.Copy, scale=column(amp_t, 0))
         reciprocal(response0[:, rest], acc, square[:], root[:])
         scatter_fused(0, rest, response0[:, rest], weight[:])
-        gather(v_w[1][:], tab_w[1][:], idx1, whole)
+        v_w = [tile("v_w%d" % g, [P, S], U32) for g in range(PASSES)]
 
         for i in range(1, PACK):
+            if i <= PASSES:
+                gather(v_w[i - 1][:], tab_w[i - 1][:], idx1, whole)
             acc = cool_product(i, (i + 1) % PACK, whole)
             square = tile("square%d" % i, [P, S], F32, "second_piece")
             root = tile("root%d" % i, [P, S], F32)
@@ -483,9 +482,10 @@ def tile_list_creep_life_weave_kernel(
         for i in (4, 5):
             hot_products(i, "feature%d" % (i - 1))
             scatter_hot(i)
-            round_direct(i, 0, T2)
+            round_direct(i, 0, S)
             if i == 4:
                 copy_feature(LAST, "z_turned1")
+            round_direct(i, S, T2)
         staging = tile("staging", [P, 2, T2 - DIRECT], BF16, "page4")
         hot_products(6, "feature5")
         scatter_hot(6)
@@ -516,14 +516,14 @@ def tile_list_creep_life_weave_kernel(
 
         def score_first_half(first, last, scales_on):
             codes, scales = quantise(
-                "z0_%d" % first, z0[:, PACK * first : PACK * last], last - first, "w1_pair1", 2 * ROW + 4 * first, scales_on
+                "z0_%d" % first, z0[:, PACK * first : PACK * last], last - first, "w1_pair1", 2 * ROW + 4 * first, scales_on, first
             )
             for group in groups:
                 if first <= group[1] < last:
                     cols = slice(group[1] - first, group[2] - first)
                     score_pass(0, group, codes[:, cols], scales[:, cols])
 
-        score_first_half(0, 512, "weighted6")
+        score_first_half(0, 512, "weighted7")
         nc.vector.tensor_copy(pages[LAST][:].indirect(entries(idx3, lead)), hot[LAST][:, lead])
         score_first_half(512, 768, "weighted7")
         nc.vector.tensor_copy(pages[LAST][:].indirect(entries(idx3, rest)), hot[LAST][:, rest])

@@ -88,7 +88,7 @@ def tile_list_creep_life_weave_kernel(
                     src[:, SCALE_ROWS * q : SCALE_ROWS * (q + 1), :].bitcast(I32),
                 )
 
-        def load_dealt(name, src, queue=nc.gpsimd):
+        def load_dealt(name, src, queue):
             dst = tile(name, [P, PACK], F32)
             queue.dma_start(dst[:], src[KP:H].rearrange("(p t) -> p t", t=PACK))
             return dst[:]
@@ -146,7 +146,7 @@ def tile_list_creep_life_weave_kernel(
         identity = tile("identity", [P, P], F32)
         nc.gpsimd.memset(tab2_sc[:].bitcast(I32), 0)
         nc.gpsimd.memset(amp_rows[:], 0.0)
-        amp_dealt, c1_dealt = load_dealt("amp_dealt", amp), load_dealt("c1_dealt", c1)
+        amp_dealt = load_dealt("amp_dealt", amp, nc.gpsimd)
         make_identity(nc, identity[:])
         sign = tile("sign", [P, PACK], F32)
         nc.gpsimd.tensor_scalar(sign[:], amp_dealt, 0.0, 2.0, mybir.AluOpType.is_ge, MULT)
@@ -157,8 +157,6 @@ def tile_list_creep_life_weave_kernel(
         nc.gpsimd.memset(half[:], 0.5)
         root_size = tile("root_size", [P, PACK], F32)
         nc.gpsimd.tensor_tensor(root_size[:], size[:], half[:], mybir.AluOpType.pow)
-        signed_c1 = tile("signed_c1", [P, PACK], F32)
-        nc.gpsimd.tensor_tensor(signed_c1[:], c1_dealt, sign[:], MULT)
         for zeroed in (w2_sc[0], w2_sc[1], tab_sc, w3_sc):
             nc.vector.memset(zeroed[:].bitcast(I32), 0)
         nc.vector.memset(c_rows[:], 0.0)
@@ -187,6 +185,7 @@ def tile_list_creep_life_weave_kernel(
         wg1_rows = load_rows("wg1_rows", wg1)
         idx3 = load_list("idx3", offs3)
         w1_dealt = [load_w1_dealt(g) for g in range(PASSES)]
+        c1_dealt = load_dealt("c1_dealt", c1, nc.sync)
         wg1_spread = load_spread("wg1_spread", wg1, 0, PACK)
         load_scales_stacked(w3_sc, w3_scales)
         c0_dealt = load_dealt("c0_dealt", c0, nc.sync)
@@ -265,23 +264,22 @@ def tile_list_creep_life_weave_kernel(
         def scatter_fused(i, cols, values, weights):
             nc.vector.tensor_tensor(pages[i][:].indirect(entries(idx4, cols)), values, weights, MULT)
 
+        weights = [tile("weight%d" % i, [P, S], F32) for i in range(PACK)]
+        for i in range(PACK):
+            nc.vector.tensor_scalar_mul(weights[i][:], wg2_rows[:], column(amp_t, i))
         reserve("second_piece", 3 * ROW // 2)
         response0 = tile("response0", [P, S], F32)
         pages[0] = tile("page0", [P, T2], F32)
         acc = cool_product(0, 0, lead)
         square = tile("square0_lead", [P, LEAD], F32)
         root = tile("root0_lead", [P, LEAD], F32, "second_piece", 3 * ROW // 4)
-        weight = tile("weight0_lead", [P, LEAD], F32)
-        nc.scalar.activation(weight[:], wg2_rows[:, lead], ACT.Copy, scale=column(amp_t, 0))
         reciprocal(response0[:, lead], acc, square[:], root[:])
-        scatter_fused(0, lead, response0[:, lead], weight[:])
+        scatter_fused(0, lead, response0[:, lead], weights[0][:, lead])
         acc = cool_product(0, 1, rest)
         square = tile("square0_rest", [P, S - LEAD], F32, "second_piece", ROW // 2)
-        weight = tile("weight0_rest", [P, S - LEAD], F32, "second_piece", ROW)
         root = tile("root0_rest", [P, S - LEAD], F32)
-        nc.scalar.activation(weight[:], wg2_rows[:, rest], ACT.Copy, scale=column(amp_t, 0))
         reciprocal(response0[:, rest], acc, square[:], root[:])
-        scatter_fused(0, rest, response0[:, rest], weight[:])
+        scatter_fused(0, rest, response0[:, rest], weights[0][:, rest])
         v_w = [tile("v_w%d" % g, [P, S], U32) for g in range(PASSES)]
 
         for i in range(1, PACK):
@@ -292,9 +290,8 @@ def tile_list_creep_life_weave_kernel(
             root = tile("root%d" % i, [P, S], F32)
             response = tile("response%d" % i, [P, S], F32)
             reciprocal(response[:], acc, square[:], root[:])
-            nc.scalar.activation(response[:], response[:], ACT.Copy, scale=column(amp_t, i))
             pages[i] = tile("page%d" % i, [P, T2], F32)
-            scatter_fused(i, whole, response[:], wg2_rows[:])
+            scatter_fused(i, whole, response[:], weights[i][:])
 
         b_turned = []
         for s in range(S // P):
@@ -343,7 +340,7 @@ def tile_list_creep_life_weave_kernel(
         respond_pair(1)
         scatter_cool(6)
         c1_natural, c0_natural = turn_natural("c_natural", c_rows, 2, 5)
-        c1_t, c0_t = [c1_natural, signed_c1], [c0_natural, c0_dealt]
+        c1_t, c0_t = [c1_natural, c1_dealt], [c0_natural, c0_dealt]
 
         def quantise(name, values, width, codes_on=None, codes_skip=0, scales_on=None, scales_skip=0):
             codes = tile(name + "_w", [P, width], U32, codes_on, codes_skip)
@@ -389,12 +386,14 @@ def tile_list_creep_life_weave_kernel(
                     stop=(g == PASSES - 1),
                 )
             shifted[i] = tile("shifted%d" % i, [P, S], F32, shifted_on, shifted_skip)
-            scale = 1.0 if i < PACK else sign[:, i - PACK : i - PACK + 1]
-            nc.scalar.activation(shifted[i][:], acc[:], ACT.Identity, bias=column(c1_t, i), scale=scale)
+            nc.scalar.activation(shifted[i][:], acc[:], ACT.Identity, bias=column(c1_t, i))
 
         def copy_feature(i, on, skip=0):
             feature[i] = tile("feature%d" % i, [P, S], F32, on, skip)
-            nc.scalar.copy(feature[i][:], sums[i][:])
+            if i < PACK:
+                nc.scalar.copy(feature[i][:], sums[i][:])
+            else:
+                nc.scalar.activation(feature[i][:], sums[i][:], ACT.Copy, scale=sign[:, i - PACK : i - PACK + 1])
 
         def hot_values(i, b, shifted_on, feature_on, feature_skip=0, shifted_skip=0):
             hot_sums(i, b, shifted_on, shifted_skip)

@@ -28,11 +28,11 @@ SCALE_ROWS = 4
 PLANES = PASSES * PACK
 LAST = PLANES - 1
 LEAD = 256
-PAIR = 2 * P
 ROW = 4 * S
-BRIDGE = 5
+BRIDGES = (5, 7)
 CHUNKS = ((0, 128), (128, 256), (256, 512), (512, 768), (768, 1024))
 DIRECT = 256
+TINY = 2.0**-120
 
 
 def tile_list_creep_life_weave_kernel(
@@ -88,9 +88,9 @@ def tile_list_creep_life_weave_kernel(
                     src[:, SCALE_ROWS * q : SCALE_ROWS * (q + 1), :].bitcast(I32),
                 )
 
-        def load_dealt(name, src, queue):
+        def load_dealt(name, src):
             dst = tile(name, [P, PACK], F32)
-            queue.dma_start(dst[:], src[KP:H].rearrange("(p t) -> p t", t=PACK))
+            nc.sync.dma_start(dst[:], src[KP:H].rearrange("(p t) -> p t", t=PACK))
             return dst[:]
 
         def load_natural(rows, k, src, queue):
@@ -115,48 +115,28 @@ def tile_list_creep_life_weave_kernel(
                 nc.sync.dma_start(dst[QUAD * q : QUAD * (q + 1), :], rows)
             return dst
 
-        def load_w2(a):
-            dst = tile("w2_w%d" % a, [P, PASSES, 2 * KP], U8)
-            src = w2_words[:, :, 2 * a * KP : 2 * (a + 1) * KP]
+        def load_w2(name, first, last):
+            dst = tile(name, [P, PASSES, 2 * (last - first)], U8)
+            src = w2_words[:, :, 2 * first : 2 * last]
             nc.sync.dma_start(dst[:].bitcast(I32), src.bitcast(I32).rearrange("g p c -> p g c"))
             return dst
 
-        def load_w1(dst, g, first, count):
-            src = w1[g * KP : (g + 1) * KP, first : first + count]
-            nc.sync.dma_start(dst, src.rearrange("(p j) c -> p j c", j=PACK))
-
-        def load_w1_pair(h):
-            dst = tile("w1_pair%d" % h, [P, PASSES, PACK, PAIR], F32)
-            for g in range(PASSES):
-                load_w1(dst[:, g], g, h * PAIR, PAIR)
-            return dst
-
-        def load_w1_dealt(g):
-            dst = tile("w1_dealt%d" % g, [P, PACK, KP], F32)
-            load_w1(dst[:], g, KP, KP)
+        def load_w1(name, g, a):
+            dst = tile(name + "%d" % g, [P, PACK, KP], F32)
+            src = w1[g * KP : (g + 1) * KP, a * KP : (a + 1) * KP]
+            nc.sync.dma_start(dst[:], src.rearrange("(p j) c -> p j c", j=PACK))
             return dst
 
         tab2_sc = tile("tab2_sc", [P, PASSES * TC], U8)
         w2_sc = [tile("w2_sc%d" % a, [P, PASSES * KP], U8) for a in range(PASSES)]
         tab_sc = tile("tab_sc", [P, T], U8)
         w3_sc = tile("w3_sc", [P, N], U8)
-        reserve("behind_amp", 4 * (S - LEAD) + 3 * P)
-        amp_rows = tile("amp_rows", [P, P], F32, "behind_amp", 4 * (S - LEAD) - P)
+        amp_rows = tile("amp_rows", [P, P], F32)
         c_rows = tile("c_rows", [P, P], F32)
         identity = tile("identity", [P, P], F32)
-        nc.gpsimd.memset(tab2_sc[:].bitcast(I32), 0)
-        nc.gpsimd.memset(amp_rows[:], 0.0)
-        amp_dealt = load_dealt("amp_dealt", amp, nc.gpsimd)
         make_identity(nc, identity[:])
-        sign = tile("sign", [P, PACK], F32)
-        nc.gpsimd.tensor_scalar(sign[:], amp_dealt, 0.0, 2.0, mybir.AluOpType.is_ge, MULT)
-        nc.gpsimd.tensor_scalar(sign[:], sign[:], -1.0, 1.0, ADD, MULT)
-        size = tile("size", [P, PACK], F32)
-        nc.gpsimd.tensor_tensor(size[:], amp_dealt, sign[:], MULT)
-        half = tile("half", [P, PACK], F32)
-        nc.gpsimd.memset(half[:], 0.5)
-        root_size = tile("root_size", [P, PACK], F32)
-        nc.gpsimd.tensor_tensor(root_size[:], size[:], half[:], mybir.AluOpType.pow)
+        nc.vector.memset(tab2_sc[:].bitcast(I32), 0)
+        nc.vector.memset(amp_rows[:], 0.0)
         for zeroed in (w2_sc[0], w2_sc[1], tab_sc, w3_sc):
             nc.vector.memset(zeroed[:].bitcast(I32), 0)
         nc.vector.memset(c_rows[:], 0.0)
@@ -166,29 +146,31 @@ def tile_list_creep_life_weave_kernel(
 
         idx2 = load_list("idx2", offs2)
         load_scales_side_by_side(tab2_sc, tab2_scales)
-        tab2_w = [load_table("tab2_w%d" % g, tab2_words[g], TC) for g in range(PASSES)]
         load_natural(amp_rows, 0, amp, nc.sync)
-        load_scales_side_by_side(w2_sc[0], w2_scales[:, :, 0:KP])
-        w2_w = [load_w2(0)]
         wg2_rows = load_rows("wg2_rows", wg2)
+        tab2_w = [load_table("tab2_w%d" % g, tab2_words[g], TC) for g in range(PASSES)]
+        w2_first = load_w2("w2_first", 0, 2 * P)
+        load_scales_side_by_side(w2_sc[0], w2_scales[:, :, 0:KP])
         idx4 = load_list("idx4", offs4)
+        w2_next = load_w2("w2_next", 2 * P, KP)
         idx1 = load_list("idx1", offs)
         tab_w = [load_table("tab_w%d" % g, tab_words[g], T) for g in range(PASSES)]
-        w2_w.append(load_w2(1))
+        amp_dealt = load_dealt("amp_dealt", amp)
+        w2_second = load_w2("w2_second", KP, H)
         load_scales_side_by_side(w2_sc[1], w2_scales[:, :, KP:H])
         wg2_spread = [load_spread("wg2_spread0", wg2, 0, 2)]
         load_scales_stacked(tab_sc, tab_scales)
         wg2_spread.append(load_spread("wg2_spread1", wg2, 2, 2))
         load_natural(c_rows, 0, c1, nc.sync)
         load_natural(c_rows, 1, c0, nc.sync)
-        w1_pair = [load_w1_pair(h) for h in range(2)]
+        w1_natural = [load_w1("w1_natural", g, 0) for g in range(PASSES)]
         wg1_rows = load_rows("wg1_rows", wg1)
         idx3 = load_list("idx3", offs3)
-        w1_dealt = [load_w1_dealt(g) for g in range(PASSES)]
-        c1_dealt = load_dealt("c1_dealt", c1, nc.sync)
+        w1_dealt = [load_w1("w1_dealt", g, 1) for g in range(PASSES)]
+        c1_dealt = load_dealt("c1_dealt", c1)
         wg1_spread = load_spread("wg1_spread", wg1, 0, PACK)
         load_scales_stacked(w3_sc, w3_scales)
-        c0_dealt = load_dealt("c0_dealt", c0, nc.sync)
+        c0_dealt = load_dealt("c0_dealt", c0)
         w3_w = tile("w3_w", [P, PASSES, N], U32)
         nc.sync.dma_start(w3_w[:].bitcast(I32), w3_words.rearrange("g p c i -> p g (c i)").bitcast(I32))
 
@@ -217,9 +199,12 @@ def tile_list_creep_life_weave_kernel(
         gather(v2_w1[:, lead], tab2_w[1][:], idx2, lead)
         gather(v2_w1[:, rest], tab2_w[1][:], idx2, rest)
         amp_t = turn_natural("amp_natural", amp_rows, 1, 4)
-        v2_w0_rest = tile("v2_w0_rest", [P, S - LEAD], U32, "behind_amp")
+        weights = [tile("weight%d" % i, [P, S], F32) for i in range(PACK)]
+        for i in range(PACK):
+            nc.scalar.activation(weights[i][:], wg2_rows[:], ACT.Copy, scale=column(amp_t, i))
+        v2_w0_rest = tile("v2_w0_rest", [P, S - LEAD], U32, "wg2_rows")
         gather(v2_w0_rest[:], tab2_w[0][:], idx2, rest)
-        v2_sc1_rest = tile("v2_sc1_rest", [P, S - LEAD], U8, "behind_amp", 4 * (S - LEAD))
+        v2_sc1_rest = tile("v2_sc1_rest", [P, S - LEAD], U8, "wg2_rows", 4 * (S - LEAD))
         gather(v2_sc1_rest[:], tab2_sc[:, TC : 2 * TC], idx2, rest)
 
         def v2_words(g, first, last):
@@ -247,7 +232,7 @@ def tile_list_creep_life_weave_kernel(
             for n, (g, c, d) in enumerate(cuts):
                 nc.tensor.matmul_mx(
                     out=acc[:, c - cols.start : d - cols.start],
-                    lhsT=w2_w[0][:, g, 2 * i * P : 2 * (i + 1) * P].bitcast(E2M1),
+                    lhsT=(w2_first, w2_next)[i // 2][:, g, 2 * (i % 2) * P : 2 * (i % 2 + 1) * P].bitcast(E2M1),
                     lhsT_scale=w2_sc[0][:, g * KP + i * P : g * KP + (i + 1) * P],
                     rhs=v2_words(g, c, d).bitcast(E4M3),
                     rhs_scale=v2_scales(g, c, d),
@@ -264,34 +249,53 @@ def tile_list_creep_life_weave_kernel(
         def scatter_fused(i, cols, values, weights):
             nc.vector.tensor_tensor(pages[i][:].indirect(entries(idx4, cols)), values, weights, MULT)
 
-        weights = [tile("weight%d" % i, [P, S], F32) for i in range(PACK)]
-        for i in range(PACK):
-            nc.vector.tensor_scalar_mul(weights[i][:], wg2_rows[:], column(amp_t, i))
-        reserve("second_piece", 3 * ROW // 2)
-        response0 = tile("response0", [P, S], F32)
-        pages[0] = tile("page0", [P, T2], F32)
-        acc = cool_product(0, 0, lead)
-        square = tile("square0_lead", [P, LEAD], F32)
-        root = tile("root0_lead", [P, LEAD], F32, "second_piece", 3 * ROW // 4)
-        reciprocal(response0[:, lead], acc, square[:], root[:])
-        scatter_fused(0, lead, response0[:, lead], weights[0][:, lead])
-        acc = cool_product(0, 1, rest)
-        square = tile("square0_rest", [P, S - LEAD], F32, "second_piece", ROW // 2)
-        root = tile("root0_rest", [P, S - LEAD], F32)
-        reciprocal(response0[:, rest], acc, square[:], root[:])
-        scatter_fused(0, rest, response0[:, rest], weights[0][:, rest])
-        v_w = [tile("v_w%d" % g, [P, S], U32) for g in range(PASSES)]
+        def reciprocals(parts, region, next_region, root_region=None):
+            width = 4 * (parts[0][1].stop - parts[0][1].start)
+            accs = [cool_product(i, b, cols) for i, cols, b in parts]
+            names = ["%d_%d" % (i, cols.start) for i, cols, b in parts]
+            shape = [P, width // 4]
+            squares = [tile("square" + names[k], shape, F32, region, ROW // 2 + (k - 1) * width) for k in range(2)]
+            roots = [tile("root" + names[0], shape, F32, root_region), tile("root" + names[1], shape, F32, next_region, ROW // 2 - 2 * P)]
+            for k in range(2):
+                nc.scalar.activation(squares[k][:], accs[k], ACT.Square)
+            for k in range(2):
+                nc.scalar.activation(roots[k][:], squares[k][:], ACT.Abs_reciprocal_sqrt, bias=1.0)
+            for k, (i, cols, b) in enumerate(parts):
+                nc.scalar.activation(responses[i][:, cols], roots[k][:], ACT.Square)
 
-        for i in range(1, PACK):
-            if i <= PASSES:
-                gather(v_w[i - 1][:], tab_w[i - 1][:], idx1, whole)
-            acc = cool_product(i, (i + 1) % PACK, whole)
-            square = tile("square%d" % i, [P, S], F32, "second_piece")
-            root = tile("root%d" % i, [P, S], F32)
-            response = tile("response%d" % i, [P, S], F32)
-            reciprocal(response[:], acc, square[:], root[:])
+        for name in ("step0", "step1", "step2", "step3"):
+            reserve(name, ROW)
+        for i in range(2):
+            responses[i] = tile("response%d" % i, [P, S], F32)
             pages[i] = tile("page%d" % i, [P, T2], F32)
-            scatter_fused(i, whole, response[:], weights[i][:])
+            reciprocals([(i, slice(k * P, (k + 1) * P), 2 * i + k) for k in range(2)], "step%d" % i, "step%d" % (i + 1))
+            scatter_fused(i, lead, responses[i][:, lead], weights[i][:, lead])
+        reciprocals([(i, rest, i) for i in range(2)], "step2", "step3", "step0")
+        for i in range(2):
+            scatter_fused(i, rest, responses[i][:, rest], weights[i][:, rest])
+        v_w = []
+        for i in (2, 3):
+            v_w.append(tile("v_w%d" % (i - 2), [P, S], U32, ("step3", "root2")[i - 2]))
+            gather(v_w[i - 2][:], tab_w[i - 2][:], idx1, whole)
+            acc = cool_product(i, i, whole)
+            square = tile("square%d" % i, [P, S], F32, "step0")
+            root = tile("root%d" % i, [P, S], F32)
+            responses[i] = tile("response%d" % i, [P, S], F32)
+            reciprocal(responses[i][:], acc, square[:], root[:])
+            pages[i] = tile("page%d" % i, [P, T2], F32)
+            scatter_fused(i, whole, responses[i][:], weights[i][:])
+
+        sign_or_zero = tile("sign_or_zero", [P, PACK], F32, "weight1")
+        nc.scalar.activation(sign_or_zero[:], amp_dealt, ACT.Sign)
+        size = tile("size", [P, PACK], F32, "weight1", 64)
+        nc.scalar.activation(size[:], amp_dealt, ACT.Abs)
+        sign = tile("sign", [P, PACK], F32)
+        nc.scalar.activation(sign[:], sign_or_zero[:], ACT.Sign, scale=2.0, bias=1.0)
+        inverse = tile("inverse", [P, PACK], F32)
+        nc.scalar.activation(inverse[:], size[:], ACT.Abs_reciprocal_sqrt, bias=TINY)
+        root_size = tile("root_size", [P, PACK], F32)
+        for t in range(PACK):
+            nc.scalar.activation(root_size[:, t : t + 1], inverse[:, t : t + 1], ACT.Copy, scale=size[:, t : t + 1])
 
         b_turned = []
         for s in range(S // P):
@@ -302,7 +306,7 @@ def tile_list_creep_life_weave_kernel(
                     out=acc[:],
                     lhsT=v2_words(g, s * P, (s + 1) * P).bitcast(E4M3),
                     lhsT_scale=v2_scales(g, s * P, (s + 1) * P),
-                    rhs=w2_w[1][:, g, :].bitcast(E2M1),
+                    rhs=w2_second[:, g, :].bitcast(E2M1),
                     rhs_scale=w2_sc[1][:, g * KP : (g + 1) * KP],
                     start=(g == 0),
                     stop=(g == PASSES - 1),
@@ -310,7 +314,7 @@ def tile_list_creep_life_weave_kernel(
         turned = [tile("turned%d" % h, [P, S // P, 2, P], F32) for h in range(2)]
         squares = [tile("square_turned%d" % h, [P, S // P, P, 2], F32) for h in range(2)]
 
-        def respond_pair(h):
+        def turn_back_pair(h):
             for s in range(S // P):
                 values = b_turned[s][:].rearrange("p (m t) -> p m t", t=PACK)[:, :, 2 * h : 2 * h + 2]
                 nc.scalar.activation(squares[h][:, s], values, ACT.Square)
@@ -318,26 +322,37 @@ def tile_list_creep_life_weave_kernel(
                     turned[h][:, s].rearrange("p t m -> p m t"), squares[h][:, s], ACT.Abs_reciprocal_sqrt, bias=1.0
                 )
             for t in (2 * h, 2 * h + 1):
-                back = bank((t + 1) % PACK, "back%d" % t)
+                back = bank(t, "back%d" % t)
                 for s in range(S // P):
                     nc.tensor.transpose(back[:, s * P : (s + 1) * P], turned[h][:, s, t % 2, :], identity[:])
-                responses[PACK + t] = tile("response%d" % (PACK + t), [P, S], F32)
-                nc.scalar.activation(responses[PACK + t][:], back[:], ACT.Square, scale=root_size[:, t : t + 1])
+                backs[PACK + t] = back
+
+        def respond(i, on=None):
+            responses[i] = tile("response%d" % i, [P, S], F32, on)
+            nc.scalar.activation(responses[i][:], backs[i][:], ACT.Square, scale=root_size[:, i - PACK : i - PACK + 1])
 
         def spread_weights(i):
             return slot(wg2_spread[i % PACK // 2], i % 2)
 
-        def scatter_cool(i, on=None):
-            pages[i] = tile("page%d" % i, [P, T2], F32, on)
+        def scatter_cool(i):
+            pages[i] = tile("page%d" % i, [P, T2], F32)
             scatter_fused(i, whole, responses[i][:], spread_weights(i))
 
-        respond_pair(0)
+        backs = {}
+        turn_back_pair(0)
+        respond(4)
+        respond(5)
         scatter_cool(4)
-        bridged = tile("bridged", [P, S], F32, "response4")
-        nc.gpsimd.tensor_tensor(bridged[:], responses[BRIDGE][:], spread_weights(BRIDGE), MULT)
+        def weigh_bridge(i, on):
+            bridged[i] = tile("bridged%d" % i, [P, S], F32, on)
+            nc.gpsimd.tensor_tensor(bridged[i][:], responses[i][:], spread_weights(i), MULT)
+
+        bridged = {}
+        weigh_bridge(BRIDGES[0], "response4")
         v_sc = tile("v_sc", [P, S], U8)
         gather(v_sc[:], tab_sc[:], idx1, whole)
-        respond_pair(1)
+        turn_back_pair(1)
+        respond(6)
         scatter_cool(6)
         c1_natural, c0_natural = turn_natural("c_natural", c_rows, 2, 5)
         c1_t, c0_t = [c1_natural, c1_dealt], [c0_natural, c0_dealt]
@@ -348,30 +363,29 @@ def tile_list_creep_life_weave_kernel(
             nc.vector.quantize_mx(out=codes[:].bitcast(E4M3), scales=scales[:], in_=values)
             return codes, scales
 
-        def prepare_pair(h):
-            grouped = tile("grouped%d" % h, [P, PASSES, PAIR, PACK], BF16)
-            nc.scalar.copy(
-                grouped[:].rearrange("p g (c n) j -> p g c j n", n=PACK),
-                w1_pair[h][:].rearrange("p g j (c n) -> p g c j n", n=PACK),
-            )
-            codes, scales = quantise("w1_pair%d" % h, grouped[:].rearrange("p g c j -> p (g c j)"), PASSES * PAIR)
-            for i in (2 * h, 2 * h + 1):
-                w1_w[i] = [codes[:, g * PAIR + i % 2 * P : g * PAIR + (i % 2 + 1) * P] for g in range(PASSES)]
-                w1_sc[i] = [scales[:, g * PAIR + i % 2 * P : g * PAIR + (i % 2 + 1) * P] for g in range(PASSES)]
+        def quantise_w1(a, name, grouped, scales_on=None):
+            codes, scales = quantise(name, grouped[:].rearrange("p g c j -> p (g c j)"), PASSES * KP, scales_on=scales_on)
+            for t in range(PACK):
+                w1_w[PACK * a + t] = [codes[:, g * KP + t * P : g * KP + (t + 1) * P] for g in range(PASSES)]
+                w1_sc[PACK * a + t] = [scales[:, g * KP + t * P : g * KP + (t + 1) * P] for g in range(PASSES)]
+
+        def prepare_natural():
+            grouped = tile("grouped_natural", [P, PASSES, KP, PACK], BF16)
+            for g in range(PASSES):
+                nc.scalar.copy(
+                    grouped[:, g].rearrange("p (c n) j -> p c j n", n=PACK),
+                    w1_natural[g][:].rearrange("p j (c n) -> p c j n", n=PACK),
+                )
+            quantise_w1(0, "w1_first", grouped)
 
         def prepare_dealt():
-            grouped = tile("grouped_dealt", [P, PASSES, KP, PACK], BF16, room=ROW)
+            grouped = tile("grouped_dealt", [P, PASSES, KP, PACK], BF16)
             for g in range(PASSES):
                 nc.scalar.copy(
                     grouped[:, g].rearrange("p (t m) j -> p m j t", t=PACK),
                     w1_dealt[g][:].rearrange("p j (m t) -> p m j t", t=PACK),
                 )
-            codes, scales = quantise(
-                "w1_dealt", grouped[:].rearrange("p g c j -> p (g c j)"), PASSES * KP, scales_on="weighted1"
-            )
-            for t in range(PACK):
-                w1_w[PACK + t] = [codes[:, g * KP + t * P : g * KP + (t + 1) * P] for g in range(PASSES)]
-                w1_sc[PACK + t] = [scales[:, g * KP + t * P : g * KP + (t + 1) * P] for g in range(PASSES)]
+            quantise_w1(1, "w1_second", grouped, "weighted1")
 
         def hot_sums(i, b, shifted_on, shifted_skip=0):
             acc = sums[i] = bank(b, "a%d" % i)
@@ -399,11 +413,11 @@ def tile_list_creep_life_weave_kernel(
             hot_sums(i, b, shifted_on, shifted_skip)
             copy_feature(i, feature_on, feature_skip)
 
-        def hot_products(i, on, skip=0):
+        def hot_products(i, on, skip=0, hot_on=None):
             weight = wg1_rows[:] if i < PACK else slot(wg1_spread, i % PACK)
             weighted = tile("weighted%d" % i, [P, S], F32, on, skip)
             nc.gpsimd.tensor_tensor(weighted[:], shifted[i][:], weight, MULT)
-            hot[i] = shifted[i]
+            hot[i] = tile("hot%d" % i, [P, S], F32, hot_on) if hot_on else shifted[i]
             nc.gpsimd.tensor_tensor(hot[i][:], weighted[:], feature[i][:], MULT)
 
         def scatter_hot(i):
@@ -441,28 +455,29 @@ def tile_list_creep_life_weave_kernel(
                     acc[:].rearrange("p (s u n) -> p s n u", s=2, u=2),
                 )
 
-        prepare_pair(0)
-        scatter_cool(LAST, "w1_pair0")
-        prepare_pair(1)
-        pages[BRIDGE] = tile("page%d" % BRIDGE, [P, T2], F32, "w1_pair1")
-        nc.vector.tensor_copy(pages[BRIDGE][:].indirect(idx4[:]), bridged[:])
-        hot_values(0, 6, "response0", "response6")
+        prepare_natural()
+        respond(LAST, "w1_natural0")
+        weigh_bridge(BRIDGES[1], "grouped_natural")
+        for k, i in enumerate(BRIDGES):
+            pages[i] = tile("page%d" % i, [P, T2], F32, "w1_natural1", 2 * k * ROW)
+            nc.vector.tensor_copy(pages[i][:].indirect(idx4[:]), bridged[i][:])
+        hot_values(0, 6, "response0", "weight0")
         hot_values(1, 7, "response1", "response2")
-        hot_products(0, "grouped1")
+        hot_products(0, "grouped_natural", ROW)
         scatter_hot(0)
         hot_products(1, "feature0")
         scatter_hot(1)
         prepare_dealt()
-        hot_values(2, 4, "w1_dealt1", "grouped_dealt", 4 * ROW)
+        hot_values(2, 4, "w1_dealt1", "weight2")
         hot_values(3, 1, "w1_dealt1", "w1_dealt1", 2 * ROW, shifted_skip=ROW)
         hot_products(2, "feature1")
         scatter_hot(2)
-        hot_products(3, "grouped_dealt", 4 * ROW - ROW // 2)
+        hot_products(3, "feature2", hot_on="grouped_dealt")
         scatter_hot(3)
         turn_plane(0)
         turn_plane(1)
         hot_values(4, 5, "response3", "root3")
-        hot_values(5, 0, "root2", "root1")
+        hot_values(5, 0, "step2", "step1")
         hot_values(6, 4, "square_turned0", "square_turned0", ROW)
         turn_plane(2)
         hot_sums(LAST, 1, "square_turned1")
@@ -515,7 +530,7 @@ def tile_list_creep_life_weave_kernel(
 
         def score_first_half(first, last, scales_on):
             codes, scales = quantise(
-                "z0_%d" % first, z0[:, PACK * first : PACK * last], last - first, "w1_pair1", 2 * ROW + 4 * first, scales_on, first
+                "z0_%d" % first, z0[:, PACK * first : PACK * last], last - first, "w1_natural0", 2 * ROW + 4 * first, scales_on, first
             )
             for group in groups:
                 if first <= group[1] < last:
@@ -543,7 +558,7 @@ def tile_list_creep_life_weave_kernel(
             first, last = CHUNKS[q]
             codes, scales = quantise(
                 "z1_%d" % q, z1[:, first:last, :].rearrange("p c t -> p (c t)"), last - first,
-                "grouped0", 4 * first, "tab2_sc", first,
+                "grouped_natural", 2 * ROW + 4 * first, "tab2_sc", first,
             )
             for group in groups:
                 if group[0] == q:

@@ -88,9 +88,9 @@ def tile_list_creep_life_weave_kernel(
                     src[:, SCALE_ROWS * q : SCALE_ROWS * (q + 1), :].bitcast(I32),
                 )
 
-        def load_dealt(name, src):
+        def load_dealt(name, src, queue):
             dst = tile(name, [P, PACK], F32)
-            nc.sync.dma_start(dst[:], src[KP:H].rearrange("(p t) -> p t", t=PACK))
+            queue.dma_start(dst[:], src[KP:H].rearrange("(p t) -> p t", t=PACK))
             return dst[:]
 
         def load_natural(rows, k, src, queue):
@@ -135,6 +135,7 @@ def tile_list_creep_life_weave_kernel(
         c_rows = tile("c_rows", [P, P], F32)
         identity = tile("identity", [P, P], F32)
         make_identity(nc, identity[:])
+        c1_dealt = load_dealt("c1_dealt", c1, nc.gpsimd)
         nc.vector.memset(tab2_sc[:].bitcast(I32), 0)
         nc.vector.memset(amp_rows[:], 0.0)
         for zeroed in (w2_sc[0], w2_sc[1], tab_sc, w3_sc):
@@ -155,7 +156,7 @@ def tile_list_creep_life_weave_kernel(
         w2_next = load_w2("w2_next", 2 * P, KP)
         idx1 = load_list("idx1", offs)
         tab_w = [load_table("tab_w%d" % g, tab_words[g], T) for g in range(PASSES)]
-        amp_dealt = load_dealt("amp_dealt", amp)
+        amp_dealt = load_dealt("amp_dealt", amp, nc.sync)
         w2_second = load_w2("w2_second", KP, H)
         load_scales_side_by_side(w2_sc[1], w2_scales[:, :, KP:H])
         wg2_spread = [load_spread("wg2_spread0", wg2, 0, 2)]
@@ -167,10 +168,9 @@ def tile_list_creep_life_weave_kernel(
         wg1_rows = load_rows("wg1_rows", wg1)
         idx3 = load_list("idx3", offs3)
         w1_dealt = [load_w1("w1_dealt", g, 1) for g in range(PASSES)]
-        c1_dealt = load_dealt("c1_dealt", c1)
         wg1_spread = load_spread("wg1_spread", wg1, 0, PACK)
         load_scales_stacked(w3_sc, w3_scales)
-        c0_dealt = load_dealt("c0_dealt", c0)
+        c0_dealt = load_dealt("c0_dealt", c0, nc.sync)
         w3_w = tile("w3_w", [P, PASSES, N], U32)
         nc.sync.dma_start(w3_w[:].bitcast(I32), w3_words.rearrange("g p c i -> p g (c i)").bitcast(I32))
 

@@ -16,7 +16,6 @@ E4M3 = mybir.dt.float8_e4m3fn_x4
 E2M1 = mybir.dt.float4_e2m1fn_x4
 ACT = mybir.ActivationFunctionType
 MULT = mybir.AluOpType.mult
-ADD = mybir.AluOpType.add
 
 P = 128
 PACK = 4
@@ -74,7 +73,7 @@ def tile_list_creep_life_weave_kernel(
             return dst
 
         def load_scales_side_by_side(dst, src):
-            rows = dst[:].bitcast(I32).rearrange("p (g c) -> p g c", g=PASSES)
+            rows = dst.bitcast(I32).rearrange("p (g c) -> p g c", g=PASSES)
             for q in range(QUADS):
                 nc.sync.dma_start(
                     rows[QUAD * q : QUAD * q + SCALE_ROWS],
@@ -128,25 +127,26 @@ def tile_list_creep_life_weave_kernel(
             return dst
 
         tab2_sc = tile("tab2_sc", [P, PASSES * TC], U8)
-        w2_sc = [tile("w2_sc%d" % a, [P, PASSES * KP], U8) for a in range(PASSES)]
+        weight_sc = tile("weight_sc", [P, PASSES * H + N], U8)
+        w2_sc = [weight_sc[:, a * H : (a + 1) * H] for a in range(PASSES)]
+        w3_sc = weight_sc[:, PASSES * H :]
         tab_sc = tile("tab_sc", [P, T], U8)
-        w3_sc = tile("w3_sc", [P, N], U8)
         amp_rows = tile("amp_rows", [P, P], F32)
         c_rows = tile("c_rows", [P, P], F32)
         identity = tile("identity", [P, P], F32)
-        make_identity(nc, identity[:])
-        c1_dealt = load_dealt("c1_dealt", c1, nc.gpsimd)
-        nc.vector.memset(tab2_sc[:].bitcast(I32), 0)
-        nc.vector.memset(amp_rows[:], 0.0)
-        for zeroed in (w2_sc[0], w2_sc[1], tab_sc, w3_sc):
-            nc.vector.memset(zeroed[:].bitcast(I32), 0)
-        nc.vector.memset(c_rows[:], 0.0)
         warm = tile("warm", [P, 2], F32)
-        nc.vector.memset(warm[:, 0:1], 1.0)
+        nc.gpsimd.memset(tab2_sc[:].bitcast(I32), 0)
+        nc.gpsimd.memset(amp_rows[:], 0.0)
+        nc.gpsimd.memset(warm[:, 0:1], 1.0)
+        nc.gpsimd.memset(weight_sc[:].bitcast(I32), 0)
+        make_identity(nc, identity[:])
+        nc.gpsimd.memset(tab_sc[:].bitcast(I32), 0)
+        nc.gpsimd.memset(c_rows[:], 0.0)
+        c1_dealt, c0_dealt = load_dealt("c1_dealt", c1, nc.gpsimd), load_dealt("c0_dealt", c0, nc.gpsimd)
         nc.scalar.activation(warm[:, 1:2], warm[:, 0:1], ACT.Abs_reciprocal_sqrt)
 
         idx2 = load_list("idx2", offs2)
-        load_scales_side_by_side(tab2_sc, tab2_scales)
+        load_scales_side_by_side(tab2_sc[:], tab2_scales)
         load_natural(amp_rows, 0, amp, nc.sync)
         wg2_rows = load_rows("wg2_rows", wg2)
         tab2_w = [load_table("tab2_w%d" % g, tab2_words[g], TC) for g in range(PASSES)]
@@ -170,7 +170,6 @@ def tile_list_creep_life_weave_kernel(
         w1_dealt = [load_w1("w1_dealt", g, 1) for g in range(PASSES)]
         wg1_spread = load_spread("wg1_spread", wg1, 0, PACK)
         load_scales_stacked(w3_sc, w3_scales)
-        c0_dealt = load_dealt("c0_dealt", c0, nc.sync)
         w3_w = tile("w3_w", [P, PASSES, N], U32)
         nc.sync.dma_start(w3_w[:].bitcast(I32), w3_words.rearrange("g p c i -> p g (c i)").bitcast(I32))
 
@@ -387,7 +386,7 @@ def tile_list_creep_life_weave_kernel(
                 )
             quantise_w1(1, "w1_second", grouped, "weighted1")
 
-        def hot_sums(i, b, shifted_on, shifted_skip=0):
+        def hot_sums(i, b, shifted_on):
             acc = sums[i] = bank(b, "a%d" % i)
             for g in range(PASSES):
                 nc.tensor.matmul_mx(
@@ -399,7 +398,7 @@ def tile_list_creep_life_weave_kernel(
                     start=(g == 0),
                     stop=(g == PASSES - 1),
                 )
-            shifted[i] = tile("shifted%d" % i, [P, S], F32, shifted_on, shifted_skip)
+            shifted[i] = tile("shifted%d" % i, [P, S], F32, shifted_on)
             nc.scalar.activation(shifted[i][:], acc[:], ACT.Identity, bias=column(c1_t, i))
 
         def copy_feature(i, on, skip=0):
@@ -409,8 +408,8 @@ def tile_list_creep_life_weave_kernel(
             else:
                 nc.scalar.activation(feature[i][:], sums[i][:], ACT.Copy, scale=sign[:, i - PACK : i - PACK + 1])
 
-        def hot_values(i, b, shifted_on, feature_on, feature_skip=0, shifted_skip=0):
-            hot_sums(i, b, shifted_on, shifted_skip)
+        def hot_values(i, b, shifted_on, feature_on, feature_skip=0):
+            hot_sums(i, b, shifted_on)
             copy_feature(i, feature_on, feature_skip)
 
         def hot_products(i, on, skip=0, hot_on=None):
@@ -467,12 +466,12 @@ def tile_list_creep_life_weave_kernel(
         scatter_hot(0)
         hot_products(1, "feature0")
         scatter_hot(1)
+        hot_values(2, 4, "weight2", "weight3")
+        hot_values(3, 1, "response6", "response5")
         prepare_dealt()
-        hot_values(2, 4, "w1_dealt1", "weight2")
-        hot_values(3, 1, "w1_dealt1", "w1_dealt1", 2 * ROW, shifted_skip=ROW)
-        hot_products(2, "feature1")
+        hot_products(2, "feature1", hot_on="w1_dealt1")
         scatter_hot(2)
-        hot_products(3, "feature2", hot_on="grouped_dealt")
+        hot_products(3, "shifted2", hot_on="grouped_dealt")
         scatter_hot(3)
         turn_plane(0)
         turn_plane(1)
@@ -493,6 +492,12 @@ def tile_list_creep_life_weave_kernel(
                 bias=column(c0_t, i), scale=sign[:, i - PACK : i - PACK + 1],
             )
 
+        def round_staged(i, first, last):
+            nc.scalar.activation(
+                staging[:, i % 2, first - DIRECT : last - DIRECT], pages[i][:, first:last], ACT.Identity,
+                bias=column(c0_t, i), scale=sign[:, i - PACK : i - PACK + 1],
+            )
+
         for i in (4, 5):
             hot_products(i, "feature%d" % (i - 1))
             scatter_hot(i)
@@ -504,7 +509,7 @@ def tile_list_creep_life_weave_kernel(
         hot_products(6, "feature5")
         scatter_hot(6)
         round_direct(6, 0, DIRECT)
-        nc.scalar.activation(staging[:, 0, :], pages[6][:, DIRECT:T2], ACT.Identity, bias=column(c0_t, 6), scale=sign[:, 2:3])
+        round_staged(6, DIRECT, T2)
         hot_products(LAST, "feature6")
 
         groups = []
@@ -538,42 +543,40 @@ def tile_list_creep_life_weave_kernel(
                     score_pass(0, group, codes[:, cols], scales[:, cols])
 
         score_first_half(0, 512, "weighted7")
-        nc.vector.tensor_copy(pages[LAST][:].indirect(entries(idx3, lead)), hot[LAST][:, lead])
+        most, end = slice(0, S - P), slice(S - P, S)
+        nc.vector.tensor_copy(pages[LAST][:].indirect(entries(idx3, most)), hot[LAST][:, most])
         score_first_half(512, 768, "weighted7")
-        nc.vector.tensor_copy(pages[LAST][:].indirect(entries(idx3, rest)), hot[LAST][:, rest])
+        nc.vector.tensor_copy(pages[LAST][:].indirect(entries(idx3, end)), hot[LAST][:, end])
         score_first_half(768, 1024, "shifted7")
 
-        nc.vector.tensor_scalar(staging[:, 1, :], pages[LAST][:, DIRECT:T2], sign[:, 3:4], column(c0_t, LAST), MULT, ADD)
 
-        def finish_chunk(q):
-            first, last = CHUNKS[q]
-            if last <= DIRECT:
-                round_direct(LAST, first, last)
-            else:
-                nc.vector.tensor_copy(
-                    z1[:, first:last, 2:4], staging[:, :, first - DIRECT : last - DIRECT].rearrange("p t c -> p c t")
-                )
+        def write_pairs(first, last):
+            nc.vector.tensor_copy(
+                z1[:, first:last, 2:4], staging[:, :, first - DIRECT : last - DIRECT].rearrange("p t c -> p c t")
+            )
 
-        def score_chunk(q):
-            first, last = CHUNKS[q]
+        def score_second_half(first, last):
             codes, scales = quantise(
-                "z1_%d" % q, z1[:, first:last, :].rearrange("p c t -> p (c t)"), last - first,
+                "z1_%d" % first, z1[:, first:last, :].rearrange("p c t -> p (c t)"), last - first,
                 "grouped_natural", 2 * ROW + 4 * first, "tab2_sc", first,
             )
             for group in groups:
-                if group[0] == q:
-                    score_pass(1, group, codes[:], scales[:])
+                if first <= group[1] < last:
+                    cols = slice(group[1] - first, group[2] - first)
+                    score_pass(1, group, codes[:, cols], scales[:, cols])
 
-        finish_chunk(0)
-        finish_chunk(1)
-        score_chunk(0)
-        finish_chunk(2)
-        score_chunk(1)
-        score_chunk(2)
-        finish_chunk(3)
-        finish_chunk(4)
-        score_chunk(3)
-        score_chunk(4)
+        round_direct(LAST, 0, P)
+        round_staged(LAST, DIRECT, S)
+        round_direct(LAST, P, DIRECT)
+        round_staged(LAST, S, T2)
+        score_second_half(0, P)
+        write_pairs(DIRECT, S)
+        score_second_half(P, DIRECT)
+        score_second_half(DIRECT, S)
+        for first, last in CHUNKS[3:]:
+            write_pairs(first, last)
+        for first, last in CHUNKS[3:]:
+            score_second_half(first, last)
         for b, (q, first, last, n0, tiles, acc) in enumerate(groups):
             result = tile("result%d" % b, [P, S], F32, "tab_w%d" % (b // PACK), b % PACK * ROW)
             if b == 0:
@@ -585,7 +588,7 @@ def tile_list_creep_life_weave_kernel(
                         result[:, part].rearrange("p (m c) -> p m c", m=2),
                     )
                 continue
-            if b in (5, 6):
+            if b in (4, 5):
                 nc.vector.tensor_copy(result[:], acc[:])
             else:
                 nc.scalar.copy(result[:], acc[:])

@@ -137,11 +137,11 @@ def tile_list_creep_life_weave_kernel(
         warm = tile("warm", [P, 2], F32)
         nc.gpsimd.memset(tab2_sc[:].bitcast(I32), 0)
         nc.gpsimd.memset(amp_rows[:], 0.0)
-        nc.gpsimd.memset(warm[:, 0:1], 1.0)
-        nc.gpsimd.memset(weight_sc[:].bitcast(I32), 0)
         make_identity(nc, identity[:])
-        nc.gpsimd.memset(tab_sc[:].bitcast(I32), 0)
-        nc.gpsimd.memset(c_rows[:], 0.0)
+        nc.vector.memset(warm[:, 0:1], 1.0)
+        nc.vector.memset(weight_sc[:].bitcast(I32), 0)
+        nc.vector.memset(tab_sc[:].bitcast(I32), 0)
+        nc.vector.memset(c_rows[:], 0.0)
         c1_dealt, c0_dealt = load_dealt("c1_dealt", c1, nc.gpsimd), load_dealt("c0_dealt", c0, nc.gpsimd)
         nc.scalar.activation(warm[:, 1:2], warm[:, 0:1], ACT.Abs_reciprocal_sqrt)
 
@@ -272,10 +272,9 @@ def tile_list_creep_life_weave_kernel(
         reciprocals([(i, rest, i) for i in range(2)], "step2", "step3", "step0")
         for i in range(2):
             scatter_fused(i, rest, responses[i][:, rest], weights[i][:, rest])
-        v_w = []
+        v_w = [tile("v_w0", [P, S], U32, "step3")]
+        gather(v_w[0][:], tab_w[0][:], idx1, whole)
         for i in (2, 3):
-            v_w.append(tile("v_w%d" % (i - 2), [P, S], U32, ("step3", "root2")[i - 2]))
-            gather(v_w[i - 2][:], tab_w[i - 2][:], idx1, whole)
             acc = cool_product(i, i, whole)
             square = tile("square%d" % i, [P, S], F32, "step0")
             root = tile("root%d" % i, [P, S], F32)
@@ -351,6 +350,8 @@ def tile_list_creep_life_weave_kernel(
         v_sc = tile("v_sc", [P, S], U8)
         gather(v_sc[:], tab_sc[:], idx1, whole)
         turn_back_pair(1)
+        v_w.append(tile("v_w1", [P, S], U32, "square_turned1"))
+        gather(v_w[1][:], tab_w[1][:], idx1, whole)
         respond(6)
         scatter_cool(6)
         c1_natural, c0_natural = turn_natural("c_natural", c_rows, 2, 5)
@@ -471,7 +472,7 @@ def tile_list_creep_life_weave_kernel(
         prepare_dealt()
         hot_products(2, "feature1", hot_on="w1_dealt1")
         scatter_hot(2)
-        hot_products(3, "shifted2", hot_on="grouped_dealt")
+        hot_products(3, "grouped_dealt")
         scatter_hot(3)
         turn_plane(0)
         turn_plane(1)
@@ -479,10 +480,11 @@ def tile_list_creep_life_weave_kernel(
         hot_values(5, 0, "step2", "step1")
         hot_values(6, 4, "square_turned0", "square_turned0", ROW)
         turn_plane(2)
-        hot_sums(LAST, 1, "square_turned1")
+        hot_sums(LAST, 1, "root2")
         turn_plane(3)
         z0 = tile("z0", [P, PACK * T2], BF16, "turned0")
         weave_turned(z0)
+        copy_feature(LAST, "z_turned1")
 
         z1 = tile("z1", [P, T2, PACK], BF16, "z_turned1", ROW)
 
@@ -501,10 +503,7 @@ def tile_list_creep_life_weave_kernel(
         for i in (4, 5):
             hot_products(i, "feature%d" % (i - 1))
             scatter_hot(i)
-            round_direct(i, 0, S)
-            if i == 4:
-                copy_feature(LAST, "z_turned1")
-            round_direct(i, S, T2)
+            round_direct(i, 0, T2)
         staging = tile("staging", [P, 2, T2 - DIRECT], BF16, "page4")
         hot_products(6, "feature5")
         scatter_hot(6)

from contextlib import ExitStack

import concourse.mybir as mybir
from concourse.masks import make_identity

K, H, N, T, TC, S, T2 = 1024, 1024, 512, 2048, 1024, 512, 1024
FLOPS = 2 * (2 * K * H * S + H * N * T2)

F32 = mybir.dt.float32
BF16 = mybir.dt.bfloat16
I32 = mybir.dt.int32
U32 = mybir.dt.uint32
U16 = mybir.dt.uint16
U8 = mybir.dt.uint8
E4M3 = mybir.dt.float8_e4m3fn_x4
E2M1 = mybir.dt.float4_e2m1fn_x4
ACT = mybir.ActivationFunctionType
MULT = mybir.AluOpType.mult

P = 128
PACK = 4
KP = P * PACK
PASSES = 2
QUAD = 32
QUADS = P // QUAD
SCALE_ROWS = 4
PLANES = PASSES * PACK
LAST = PLANES - 1
LEAD = 256
ROW = 4 * S
BRIDGES = (5, 7)
CHUNKS = ((0, 128), (128, 256), (256, 512), (512, 768), (768, 1024))
DIRECT = 256
TINY = 2.0**-120


def tile_list_creep_life_weave_kernel(
    tc, tab_words, tab_scales, tab2_words, tab2_scales, offs, offs2, offs3, offs4,
    w1, w2_words, w2_scales, w3_words, w3_scales, c1, amp, c0, wg1, wg2, out,
):
    nc = tc.nc
    with ExitStack() as ctx:
        lists = ctx.enter_context(tc.tile_pool(name="lists", bufs=1))
        sbuf = ctx.enter_context(tc.tile_pool(name="sbuf", bufs=1))
        psum = ctx.enter_context(tc.psum_pool(name="psum", bufs=1))
        spots = {"free": 0}

        def reserve(name, size):
            spots[name] = spots["free"]
            spots["free"] = spots["free"] + (size + 63) // 64 * 64

        def tile(name, shape, dtype, on=None, skip=0, room=0):
            if on is None:
                size = 4 if dtype in (F32, U32) else 2 if dtype == BF16 else 1
                for extent in shape[1:]:
                    size = size * extent
                reserve(name, size + room)
            else:
                spots[name] = spots[on] + skip
            return sbuf.tile(shape, dtype, name=name, align_bytes=64, offset=spots[name])

        def bank(b, name):
            return psum.tile([P, S], F32, name=name, tag="bank%d" % b)

        def load_list(name, src):
            dst = lists.tile([P, S // 16], U16, name=name)
            nc.sync.dma_start(dst[:], src)
            return dst

        def load_table(name, src, columns):
            dst = tile(name, [P, columns], U32)
            nc.sync.dma_start(dst[:].bitcast(I32), src.rearrange("p c i -> p (c i)").bitcast(I32))
            return dst

        def load_scales_side_by_side(dst, src):
            rows = dst.bitcast(I32).rearrange("p (g c) -> p g c", g=PASSES)
            for q in range(QUADS):
                nc.sync.dma_start(
                    rows[QUAD * q : QUAD * q + SCALE_ROWS],
                    src[:, SCALE_ROWS * q : SCALE_ROWS * (q + 1), :].bitcast(I32).rearrange("g r c -> r g c"),
                )

        def load_scales_stacked(dst, src):
            for q in range(QUADS):
                nc.sync.dma_start(
                    dst[QUAD * q : QUAD * q + PASSES * SCALE_ROWS, :].bitcast(I32),
                    src[:, SCALE_ROWS * q : SCALE_ROWS * (q + 1), :].bitcast(I32),
                )

        def load_dealt(name, src, queue):
            dst = tile(name, [P, PACK], F32)
            queue.dma_start(dst[:], src[KP:H].rearrange("(p t) -> p t", t=PACK))
            return dst[:]

        def load_natural(rows, k, src, queue):
            queue.dma_start(rows[PACK * k : PACK * (k + 1), :], src[0:KP].rearrange("(t p) -> t p", t=PACK))

        def turn_natural(name, rows, count, b):
            acc = bank(b, name + "_turned")
            nc.tensor.transpose(acc[:, 0:P], rows[:], identity[:])
            dst = tile(name, [P, count * PACK], F32)
            nc.scalar.copy(dst[:], acc[:, 0 : count * PACK])
            return [dst[:, PACK * k : PACK * (k + 1)] for k in range(count)]

        def load_rows(name, src):
            dst = tile(name, [P, S], F32)
            nc.sync.dma_start(dst[:], src)
            return dst

        def load_spread(name, src, first, count):
            dst = tile(name, [P, count * S], F32)
            rows = src.rearrange("(u t) j -> u (t j)", t=PACK)[:, first * S : (first + count) * S]
            for q in (0, 2, 1, 3):
                nc.sync.dma_start(dst[QUAD * q : QUAD * (q + 1), :], rows)
            return dst

        def load_w2(name, first, last):
            dst = tile(name, [P, PASSES, 2 * (last - first)], U8)
            src = w2_words[:, :, 2 * first : 2 * last]
            nc.sync.dma_start(dst[:].bitcast(I32), src.bitcast(I32).rearrange("g p c -> p g c"))
            return dst

        def load_w1(name, g, a):
            dst = tile(name + "%d" % g, [P, PACK, KP], F32)
            src = w1[g * KP : (g + 1) * KP, a * KP : (a + 1) * KP]
            nc.sync.dma_start(dst[:], src.rearrange("(p j) c -> p j c", j=PACK))
            return dst

        tab2_sc = tile("tab2_sc", [P, PASSES * TC], U8)
        weight_sc = tile("weight_sc", [P, PASSES * H + N], U8)
        w2_sc = [weight_sc[:, a * H : (a + 1) * H] for a in range(PASSES)]
        w3_sc = weight_sc[:, PASSES * H :]
        tab_sc = tile("tab_sc", [P, T], U8)
        amp_rows = tile("amp_rows", [P, P], F32)
        c_rows = tile("c_rows", [P, P], F32)
        identity = tile("identity", [P, P], F32)
        warm = tile("warm", [P, 2], F32)
        nc.gpsimd.memset(tab2_sc[:].bitcast(I32), 0)
        nc.gpsimd.memset(amp_rows[:], 0.0)
        make_identity(nc, identity[:])
        nc.vector.memset(warm[:, 0:1], 1.0)
        nc.vector.memset(weight_sc[:].bitcast(I32), 0)
        nc.vector.memset(tab_sc[:].bitcast(I32), 0)
        nc.vector.memset(c_rows[:], 0.0)
        c1_dealt, c0_dealt = load_dealt("c1_dealt", c1, nc.gpsimd), load_dealt("c0_dealt", c0, nc.gpsimd)
        nc.scalar.activation(warm[:, 1:2], warm[:, 0:1], ACT.Abs_reciprocal_sqrt)

        idx2 = load_list("idx2", offs2)
        load_scales_side_by_side(tab2_sc[:], tab2_scales)
        load_natural(amp_rows, 0, amp, nc.sync)
        wg2_rows = load_rows("wg2_rows", wg2)
        tab2_w = [load_table("tab2_w%d" % g, tab2_words[g], TC) for g in range(PASSES)]
        w2_first = load_w2("w2_first", 0, 2 * P)
        load_scales_side_by_side(w2_sc[0], w2_scales[:, :, 0:KP])
        idx4 = load_list("idx4", offs4)
        w2_next = load_w2("w2_next", 2 * P, KP)
        idx1 = load_list("idx1", offs)
        tab_w = [load_table("tab_w%d" % g, tab_words[g], T) for g in range(PASSES)]
        amp_dealt = load_dealt("amp_dealt", amp, nc.sync)
        w2_second = load_w2("w2_second", KP, H)
        load_scales_side_by_side(w2_sc[1], w2_scales[:, :, KP:H])
        wg2_spread = [load_spread("wg2_spread0", wg2, 0, 2)]
        load_scales_stacked(tab_sc, tab_scales)
        wg2_spread.append(load_spread("wg2_spread1", wg2, 2, 2))
        load_natural(c_rows, 0, c1, nc.sync)
        load_natural(c_rows, 1, c0, nc.sync)
        w1_natural = [load_w1("w1_natural", g, 0) for g in range(PASSES)]
        wg1_rows = load_rows("wg1_rows", wg1)
        idx3 = load_list("idx3", offs3)
        w1_dealt = [load_w1("w1_dealt", g, 1) for g in range(PASSES)]
        wg1_spread = load_spread("wg1_spread", wg1, 0, PACK)
        load_scales_stacked(w3_sc, w3_scales)
        w3_w = tile("w3_w", [P, PASSES, N], U32)
        nc.sync.dma_start(w3_w[:].bitcast(I32), w3_words.rearrange("g p c i -> p g (c i)").bitcast(I32))

        lead, rest, whole = slice(0, LEAD), slice(LEAD, S), slice(0, S)

        def entries(idx, cols):
            return idx[:, cols.start // 16 : cols.stop // 16]

        def gather(dst, window, idx, cols):
            nc.vector.tensor_copy(dst, window.indirect(entries(idx, cols)))

        def column(coefficients, i):
            a, t = divmod(i, PACK)
            return coefficients[a][:, t : t + 1]

        def slot(wide, t):
            return wide[:, t * S : (t + 1) * S]

        v2_w0_lead = tile("v2_w0_lead", [P, LEAD], U32)
        v2_w1 = tile("v2_w1", [P, S], U32)
        v2_sc0 = tile("v2_sc0", [P, S], U8)
        v2_sc1_lead = tile("v2_sc1_lead", [P, LEAD], U8)
        gather(v2_sc0[:], tab2_sc[:, 0:TC], idx2, whole)
        gather(v2_sc1_lead[:], tab2_sc[:, TC : 2 * TC], idx2, lead)
        gather(v2_w0_lead[:], tab2_w[0][:], idx2, lead)
        gather(v2_w1[:, lead], tab2_w[1][:], idx2, lead)
        gather(v2_w1[:, rest], tab2_w[1][:], idx2, rest)
        amp_t = turn_natural("amp_natural", amp_rows, 1, 4)
        weights = [tile("weight%d" % i, [P, S], F32) for i in range(PACK)]
        for i in range(PACK):
            nc.scalar.activation(weights[i][:], wg2_rows[:], ACT.Copy, scale=column(amp_t, i))
        v2_w0_rest = tile("v2_w0_rest", [P, S - LEAD], U32, "wg2_rows")
        gather(v2_w0_rest[:], tab2_w[0][:], idx2, rest)
        v2_sc1_rest = tile("v2_sc1_rest", [P, S - LEAD], U8, "wg2_rows", 4 * (S - LEAD))
        gather(v2_sc1_rest[:], tab2_sc[:, TC : 2 * TC], idx2, rest)

        def v2_words(g, first, last):
            if g == 1:
                return v2_w1[:, first:last]
            if last <= LEAD:
                return v2_w0_lead[:, first:last]
            return v2_w0_rest[:, first - LEAD : last - LEAD]

        def v2_scales(g, first, last):
            if g == 0:
                return v2_sc0[:, first:last]
            if last <= LEAD:
                return v2_sc1_lead[:, first:last]
            return v2_sc1_rest[:, first - LEAD : last - LEAD]

        pages, responses, sums, hot, shifted, feature = {}, {}, {}, {}, {}, {}
        w1_w, w1_sc = {}, {}

        def cool_product(i, b, cols):
            acc = bank(b, "b%d_%d" % (i, cols.start))
            cuts = [(g, cols.start, cols.stop) for g in range(PASSES)]
            if cols == whole:
                cuts = [(g, c, c + LEAD) for g in range(PASSES) for c in (0, LEAD)]
            for n, (g, c, d) in enumerate(cuts):
                nc.tensor.matmul_mx(
                    out=acc[:, c - cols.start : d - cols.start],
                    lhsT=(w2_first, w2_next)[i // 2][:, g, 2 * (i % 2) * P : 2 * (i % 2 + 1) * P].bitcast(E2M1),
                    lhsT_scale=w2_sc[0][:, g * KP + i * P : g * KP + (i + 1) * P],
                    rhs=v2_words(g, c, d).bitcast(E4M3),
                    rhs_scale=v2_scales(g, c, d),
                    start=(n == 0),
                    stop=(n == len(cuts) - 1),
                )
            return acc[:, 0 : cols.stop - cols.start]

        def reciprocal(response, acc, square, root):
            nc.scalar.activation(square, acc, ACT.Square)
            nc.scalar.activation(root, square, ACT.Abs_reciprocal_sqrt, bias=1.0)
            nc.scalar.activation(response, root, ACT.Square)

        def scatter_fused(i, cols, values, weights):
            nc.vector.tensor_tensor(pages[i][:].indirect(entries(idx4, cols)), values, weights, MULT)

        def reciprocals(parts, region, next_region, root_region=None):
            width = 4 * (parts[0][1].stop - parts[0][1].start)
            accs = [cool_product(i, b, cols) for i, cols, b in parts]
            names = ["%d_%d" % (i, cols.start) for i, cols, b in parts]
            shape = [P, width // 4]
            squares = [tile("square" + names[k], shape, F32, region, ROW // 2 + (k - 1) * width) for k in range(2)]
            roots = [tile("root" + names[0], shape, F32, root_region), tile("root" + names[1], shape, F32, next_region, ROW // 2 - 2 * P)]
            for k in range(2):
                nc.scalar.activation(squares[k][:], accs[k], ACT.Square)
            for k in range(2):
                nc.scalar.activation(roots[k][:], squares[k][:], ACT.Abs_reciprocal_sqrt, bias=1.0)
            for k, (i, cols, b) in enumerate(parts):
                nc.scalar.activation(responses[i][:, cols], roots[k][:], ACT.Square)

        for name in ("step0", "step1", "step2", "step3"):
            reserve(name, ROW)
        for i in range(2):
            responses[i] = tile("response%d" % i, [P, S], F32)
            pages[i] = tile("page%d" % i, [P, T2], F32)
            reciprocals([(i, slice(k * P, (k + 1) * P), 2 * i + k) for k in range(2)], "step%d" % i, "step%d" % (i + 1))
            scatter_fused(i, lead, responses[i][:, lead], weights[i][:, lead])
        reciprocals([(i, rest, i) for i in range(2)], "step2", "step3", "step0")
        for i in range(2):
            scatter_fused(i, rest, responses[i][:, rest], weights[i][:, rest])
        v_w = [tile("v_w0", [P, S], U32, "step3")]
        gather(v_w[0][:], tab_w[0][:], idx1, whole)
        for i in (2, 3):
            acc = cool_product(i, i, whole)
            square = tile("square%d" % i, [P, S], F32, "step0")
            root = tile("root%d" % i, [P, S], F32)
            responses[i] = tile("response%d" % i, [P, S], F32)
            reciprocal(responses[i][:], acc, square[:], root[:])
            pages[i] = tile("page%d" % i, [P, T2], F32)
            scatter_fused(i, whole, responses[i][:], weights[i][:])

        sign_or_zero = tile("sign_or_zero", [P, PACK], F32, "weight1")
        nc.scalar.activation(sign_or_zero[:], amp_dealt, ACT.Sign)
        size = tile("size", [P, PACK], F32, "weight1", 64)
        nc.scalar.activation(size[:], amp_dealt, ACT.Abs)
        sign = tile("sign", [P, PACK], F32)
        nc.scalar.activation(sign[:], sign_or_zero[:], ACT.Sign, scale=2.0, bias=1.0)
        inverse = tile("inverse", [P, PACK], F32)
        nc.scalar.activation(inverse[:], size[:], ACT.Abs_reciprocal_sqrt, bias=TINY)
        root_size = tile("root_size", [P, PACK], F32)
        for t in range(PACK):
            nc.scalar.activation(root_size[:, t : t + 1], inverse[:, t : t + 1], ACT.Copy, scale=size[:, t : t + 1])

        b_turned = []
        for s in range(S // P):
            acc = bank((5, 6, 7, 4)[s], "b_turned%d" % s)
            b_turned.append(acc)
            for g in range(PASSES):
                nc.tensor.matmul_mx(
                    out=acc[:],
                    lhsT=v2_words(g, s * P, (s + 1) * P).bitcast(E4M3),
                    lhsT_scale=v2_scales(g, s * P, (s + 1) * P),
                    rhs=w2_second[:, g, :].bitcast(E2M1),
                    rhs_scale=w2_sc[1][:, g * KP : (g + 1) * KP],
                    start=(g == 0),
                    stop=(g == PASSES - 1),
                )
        turned = [tile("turned%d" % h, [P, S // P, 2, P], F32) for h in range(2)]
        squares = [tile("square_turned%d" % h, [P, S // P, P, 2], F32) for h in range(2)]

        def turn_back_pair(h):
            for s in range(S // P):
                values = b_turned[s][:].rearrange("p (m t) -> p m t", t=PACK)[:, :, 2 * h : 2 * h + 2]
                nc.scalar.activation(squares[h][:, s], values, ACT.Square)
                nc.scalar.activation(
                    turned[h][:, s].rearrange("p t m -> p m t"), squares[h][:, s], ACT.Abs_reciprocal_sqrt, bias=1.0
                )
            for t in (2 * h, 2 * h + 1):
                back = bank(t, "back%d" % t)
                for s in range(S // P):
                    nc.tensor.transpose(back[:, s * P : (s + 1) * P], turned[h][:, s, t % 2, :], identity[:])
                backs[PACK + t] = back

        def respond(i, on=None):
            responses[i] = tile("response%d" % i, [P, S], F32, on)
            nc.scalar.activation(responses[i][:], backs[i][:], ACT.Square, scale=root_size[:, i - PACK : i - PACK + 1])

        def spread_weights(i):
            return slot(wg2_spread[i % PACK // 2], i % 2)

        def scatter_cool(i):
            pages[i] = tile("page%d" % i, [P, T2], F32)
            scatter_fused(i, whole, responses[i][:], spread_weights(i))

        backs = {}
        turn_back_pair(0)
        respond(4)
        respond(5)
        scatter_cool(4)
        def weigh_bridge(i, on):
            bridged[i] = tile("bridged%d" % i, [P, S], F32, on)
            nc.gpsimd.tensor_tensor(bridged[i][:], responses[i][:], spread_weights(i), MULT)

        bridged = {}
        weigh_bridge(BRIDGES[0], "response4")
        v_sc = tile("v_sc", [P, S], U8)
        gather(v_sc[:], tab_sc[:], idx1, whole)
        turn_back_pair(1)
        v_w.append(tile("v_w1", [P, S], U32, "square_turned1"))
        gather(v_w[1][:], tab_w[1][:], idx1, whole)
        respond(6)
        scatter_cool(6)
        c1_natural, c0_natural = turn_natural("c_natural", c_rows, 2, 5)
        c1_t, c0_t = [c1_natural, c1_dealt], [c0_natural, c0_dealt]

        def quantise(name, values, width, codes_on=None, codes_skip=0, scales_on=None, scales_skip=0):
            codes = tile(name + "_w", [P, width], U32, codes_on, codes_skip)
            scales = tile(name + "_sc", [P, width], U8, scales_on, scales_skip)
            nc.vector.quantize_mx(out=codes[:].bitcast(E4M3), scales=scales[:], in_=values)
            return codes, scales

        def quantise_w1(a, name, grouped, scales_on=None):
            codes, scales = quantise(name, grouped[:].rearrange("p g c j -> p (g c j)"), PASSES * KP, scales_on=scales_on)
            for t in range(PACK):
                w1_w[PACK * a + t] = [codes[:, g * KP + t * P : g * KP + (t + 1) * P] for g in range(PASSES)]
                w1_sc[PACK * a + t] = [scales[:, g * KP + t * P : g * KP + (t + 1) * P] for g in range(PASSES)]

        def prepare_natural():
            grouped = tile("grouped_natural", [P, PASSES, KP, PACK], BF16)
            for g in range(PASSES):
                nc.scalar.copy(
                    grouped[:, g].rearrange("p (c n) j -> p c j n", n=PACK),
                    w1_natural[g][:].rearrange("p j (c n) -> p c j n", n=PACK),
                )
            quantise_w1(0, "w1_first", grouped)

        def prepare_dealt():
            grouped = tile("grouped_dealt", [P, PASSES, KP, PACK], BF16)
            for g in range(PASSES):
                nc.scalar.copy(
                    grouped[:, g].rearrange("p (t m) j -> p m j t", t=PACK),
                    w1_dealt[g][:].rearrange("p j (m t) -> p m j t", t=PACK),
                )
            quantise_w1(1, "w1_second", grouped, "weighted1")

        def hot_sums(i, b, shifted_on):
            acc = sums[i] = bank(b, "a%d" % i)
            for g in range(PASSES):
                nc.tensor.matmul_mx(
                    out=acc[:],
                    lhsT=w1_w[i][g].bitcast(E4M3),
                    lhsT_scale=w1_sc[i][g],
                    rhs=v_w[g][:].bitcast(E4M3),
                    rhs_scale=v_sc[SCALE_ROWS * g : P, :],
                    start=(g == 0),
                    stop=(g == PASSES - 1),
                )
            shifted[i] = tile("shifted%d" % i, [P, S], F32, shifted_on)
            nc.scalar.activation(shifted[i][:], acc[:], ACT.Identity, bias=column(c1_t, i))

        def copy_feature(i, on, skip=0):
            feature[i] = tile("feature%d" % i, [P, S], F32, on, skip)
            if i < PACK:
                nc.scalar.copy(feature[i][:], sums[i][:])
            else:
                nc.scalar.activation(feature[i][:], sums[i][:], ACT.Copy, scale=sign[:, i - PACK : i - PACK + 1])

        def hot_values(i, b, shifted_on, feature_on, feature_skip=0):
            hot_sums(i, b, shifted_on)
            copy_feature(i, feature_on, feature_skip)

        def hot_products(i, on, skip=0, hot_on=None):
            weight = wg1_rows[:] if i < PACK else slot(wg1_spread, i % PACK)
            weighted = tile("weighted%d" % i, [P, S], F32, on, skip)
            nc.gpsimd.tensor_tensor(weighted[:], shifted[i][:], weight, MULT)
            hot[i] = tile("hot%d" % i, [P, S], F32, hot_on) if hot_on else shifted[i]
            nc.gpsimd.tensor_tensor(hot[i][:], weighted[:], feature[i][:], MULT)

        def scatter_hot(i):
            nc.vector.tensor_copy(pages[i][:].indirect(idx3[:]), hot[i][:])

        z_turned = [tile("z_turned%d" % h, [P, PACK, KP], BF16, "w1_dealt0", 2 * ROW * h) for h in range(2)]

        def turn_plane(i):
            for h in range(2):
                acc = bank((2, 6)[i % 2] + h, "z_turned%d%d" % (i, h))
                for s in range(PACK):
                    nc.tensor.matmul(
                        acc[:, s * P : (s + 1) * P], column(c0_t, i).to_broadcast([P, P]), identity[:],
                        start=(s == 0), stop=False, is_transpose=True,
                    )
                for s in range(PACK):
                    c = (h * PACK + s) * P
                    nc.tensor.matmul(
                        acc[:, s * P : (s + 1) * P], pages[i][:, c : c + P], identity[:],
                        start=False, stop=(s == PACK - 1), is_transpose=True,
                    )
                nc.scalar.copy(z_turned[h][:, :, i * P : (i + 1) * P], acc[:].rearrange("p (s r) -> p s r", s=PACK))

        def weave_turned(z):
            words = z[:].bitcast(F32)
            for b in range(PACK):
                acc = bank((2, 3, 5, 0)[b], "z_words%d" % b)
                for s in range(2):
                    pairs = z_turned[b // 2][:, 2 * (b % 2) + s, :].bitcast(F32)
                    for u in range(2):
                        c = (2 * s + u) * P
                        nc.tensor.transpose(acc[:, c : c + P], pairs[:, u : 2 * P : 2], identity[:])
                nc.scalar.copy(
                    words[:, b * S : (b + 1) * S].rearrange("p (s n u) -> p s n u", s=2, u=2),
                    acc[:].rearrange("p (s u n) -> p s n u", s=2, u=2),
                )

        prepare_natural()
        respond(LAST, "w1_natural0")
        weigh_bridge(BRIDGES[1], "grouped_natural")
        for k, i in enumerate(BRIDGES):
            pages[i] = tile("page%d" % i, [P, T2], F32, "w1_natural1", 2 * k * ROW)
            nc.vector.tensor_copy(pages[i][:].indirect(idx4[:]), bridged[i][:])
        hot_values(0, 6, "response0", "weight0")
        hot_values(1, 7, "response1", "response2")
        hot_products(0, "grouped_natural", ROW)
        scatter_hot(0)
        hot_products(1, "feature0")
        scatter_hot(1)
        hot_values(2, 4, "weight2", "weight3")
        hot_values(3, 1, "response6", "response5")
        prepare_dealt()
        hot_products(2, "feature1", hot_on="w1_dealt1")
        scatter_hot(2)
        hot_products(3, "grouped_dealt")
        scatter_hot(3)
        turn_plane(0)
        turn_plane(1)
        hot_values(4, 5, "response3", "root3")
        hot_values(5, 0, "step2", "step1")
        hot_values(6, 4, "square_turned0", "square_turned0", ROW)
        turn_plane(2)
        hot_sums(LAST, 1, "root2")
        turn_plane(3)
        z0 = tile("z0", [P, PACK * T2], BF16, "turned0")
        weave_turned(z0)
        copy_feature(LAST, "z_turned1")

        z1 = tile("z1", [P, T2, PACK], BF16, "z_turned1", ROW)

        def round_direct(i, first, last):
            nc.scalar.activation(
                z1[:, first:last, i % PACK], pages[i][:, first:last], ACT.Identity,
                bias=column(c0_t, i), scale=sign[:, i - PACK : i - PACK + 1],
            )

        def round_staged(i, first, last):
            nc.scalar.activation(
                staging[:, i % 2, first - DIRECT : last - DIRECT], pages[i][:, first:last], ACT.Identity,
                bias=column(c0_t, i), scale=sign[:, i - PACK : i - PACK + 1],
            )

        for i in (4, 5):
            hot_products(i, "feature%d" % (i - 1))
            scatter_hot(i)
            round_direct(i, 0, T2)
        staging = tile("staging", [P, 2, T2 - DIRECT], BF16, "page4")
        hot_products(6, "feature5")
        scatter_hot(6)
        round_direct(6, 0, DIRECT)
        round_staged(6, DIRECT, T2)
        hot_products(LAST, "feature6")

        groups = []
        for q, (first, last) in enumerate(CHUNKS):
            tiles = S // (last - first)
            for n0 in range(0, PACK, tiles):
                groups.append((q, first, last, n0, tiles, bank(len(groups), "score%d" % len(groups))))

        def score_pass(a, group, codes, scales):
            q, first, last, n0, tiles, acc = group
            width = last - first
            for m in range(tiles):
                rows = slice((n0 + m) * P, (n0 + m + 1) * P)
                nc.tensor.matmul_mx(
                    out=acc[:, m * width : (m + 1) * width],
                    lhsT=w3_w[:, a, rows].bitcast(E4M3),
                    lhsT_scale=w3_sc[SCALE_ROWS * a : P, rows],
                    rhs=codes.bitcast(E4M3),
                    rhs_scale=scales,
                    start=(a == 0 and m == 0),
                    stop=(a == PASSES - 1 and m == tiles - 1),
                )

        def score_first_half(first, last, scales_on):
            codes, scales = quantise(
                "z0_%d" % first, z0[:, PACK * first : PACK * last], last - first, "w1_natural0", 2 * ROW + 4 * first, scales_on, first
            )
            for group in groups:
                if first <= group[1] < last:
                    cols = slice(group[1] - first, group[2] - first)
                    score_pass(0, group, codes[:, cols], scales[:, cols])

        score_first_half(0, 512, "weighted7")
        most, end = slice(0, S - P), slice(S - P, S)
        nc.vector.tensor_copy(pages[LAST][:].indirect(entries(idx3, most)), hot[LAST][:, most])
        score_first_half(512, 768, "weighted7")
        nc.vector.tensor_copy(pages[LAST][:].indirect(entries(idx3, end)), hot[LAST][:, end])
        score_first_half(768, 1024, "shifted7")


        def write_pairs(first, last):
            nc.vector.tensor_copy(
                z1[:, first:last, 2:4], staging[:, :, first - DIRECT : last - DIRECT].rearrange("p t c -> p c t")
            )

        def score_second_half(first, last):
            codes, scales = quantise(
                "z1_%d" % first, z1[:, first:last, :].rearrange("p c t -> p (c t)"), last - first,
                "grouped_natural", 2 * ROW + 4 * first, "tab2_sc", first,
            )
            for group in groups:
                if first <= group[1] < last:
                    cols = slice(group[1] - first, group[2] - first)
                    score_pass(1, group, codes[:, cols], scales[:, cols])

        round_direct(LAST, 0, P)
        round_staged(LAST, DIRECT, S)
        round_direct(LAST, P, DIRECT)
        round_staged(LAST, S, T2)
        score_second_half(0, P)
        write_pairs(DIRECT, S)
        score_second_half(P, DIRECT)
        score_second_half(DIRECT, S)
        for first, last in CHUNKS[3:]:
            write_pairs(first, last)
        for first, last in CHUNKS[3:]:
            score_second_half(first, last)
        for b, (q, first, last, n0, tiles, acc) in enumerate(groups):
            result = tile("result%d" % b, [P, S], F32, "tab_w%d" % (b // PACK), b % PACK * ROW)
            if b == 0:
                for m in (0, 2):
                    part = slice(m * P, (m + 2) * P)
                    nc.scalar.copy(result[:, part], acc[:, part])
                    nc.sync.dma_start(
                        out[part, first:last].rearrange("(m p) c -> p m c", p=P),
                        result[:, part].rearrange("p (m c) -> p m c", m=2),
                    )
                continue
            if b in (4, 5):
                nc.vector.tensor_copy(result[:], acc[:])
            else:
                nc.scalar.copy(result[:], acc[:])
            nc.sync.dma_start(
                out[n0 * P : (n0 + tiles) * P, first:last].rearrange("(m p) c -> p m c", p=P),
                result[:].rearrange("p (m c) -> p m c", m=tiles),
            )
